import numpy as np
import ml_dtypes


def mxq(x, axis, fmt="e4m3"):
    dtype, down = {"e4m3": (ml_dtypes.float8_e4m3fn, 7), "e5m2": (ml_dtypes.float8_e5m2, 14)}[fmt]
    v = np.moveaxis(np.asarray(x, np.float32).astype(ml_dtypes.bfloat16).astype(np.float64), axis, -1)
    blocks = v.reshape(v.shape[:-1] + (-1, 32))
    amax = np.abs(blocks).max(-1, keepdims=True)
    byte = np.maximum(np.where(amax > 0, np.frexp(amax)[1] - 1 + 127, 0) - down, 1)
    scale = np.exp2(byte - 127.0)
    codes = (blocks / scale).astype(np.float32).astype(dtype).astype(np.float64)
    return np.moveaxis((codes * scale).reshape(v.shape), -1, axis)


WIDE = False


def mx_kscale(k):
    if not WIDE:
        return np.ones(k)
    levels = np.array([10, -10, 5, -5, 0])
    if k % 512:
        return np.exp2(np.random.permutation(np.resize(levels, k // 32))).repeat(32)
    a = np.empty((k // 512, 16))
    for p in range(k // 512):
        a[p, :8] = np.random.permutation(np.resize(levels, 8))
        for g in range(8):
            far = levels[np.abs(levels - a[p, g]) >= 10]
            a[p, g + 8] = far[np.random.randint(len(far))]
    return np.exp2(a.ravel()).repeat(32)


def f64(x):
    return np.asarray(x).astype(np.float64)


def striped(idx):
    return np.tile(idx.reshape(-1, 16).T, (8, 1)).astype(np.uint16)


def unstriped(offs):
    return offs[:16].T.reshape(-1).astype(np.int64)


E2M1 = np.array([0.0, 0.5, 1.0, 1.5, 2.0, 3.0, 4.0, 6.0, -0.0, -0.5, -1.0, -1.5, -2.0, -3.0, -4.0, -6.0])


def pack_weight(w, fmt):
    k, n = w.shape
    w = f64(np.asarray(w, np.float32).astype(ml_dtypes.bfloat16)).reshape(k // 32, 32, n)
    amax = np.abs(w).max(1)
    if fmt == "e4m3":
        byte = np.frexp(amax)[1] - 1 + 127 - 7
    else:
        mant, ex = np.frexp(amax / 6.0)
        byte = np.where(mant > 0.5, ex, ex - 1) + 127
    byte = np.clip(np.where(amax > 0, byte, 1), 1, 254)
    scaled = (w * np.exp2(127.0 - byte)[:, None, :]).reshape(k, n).astype(np.float32)
    by_word = np.ascontiguousarray(scaled.reshape(k // 512, 128, 4, n).transpose(0, 1, 3, 2))
    if fmt == "e4m3":
        words = by_word.astype(ml_dtypes.float8_e4m3fn).view(np.uint8)
    else:
        c = by_word.astype(ml_dtypes.float4_e2m1fn).view(np.uint8) & 0xF
        words = (c[..., 0::2] | (c[..., 1::2] << 4)).reshape(k // 512, 128, 2 * n)
    return np.ascontiguousarray(words), np.ascontiguousarray(byte.astype(np.uint8).reshape(k // 512, 16, n))


def unpack_weight(words, scales, fmt):
    g, _, n = scales.shape
    words = np.ascontiguousarray(words).reshape(g, 128, n, -1)
    if fmt == "e4m3":
        vals = words.view(ml_dtypes.float8_e4m3fn).astype(np.float64)
    else:
        nib = np.empty((g, 128, n, 4), np.uint8)
        nib[..., 0::2] = words & 0xF
        nib[..., 1::2] = words >> 4
        vals = E2M1[nib]
    vals = vals * np.repeat(np.exp2(scales.astype(np.float64) - 127.0), 8, axis=1)[..., None]
    return vals.transpose(0, 1, 3, 2).reshape(g * 512, n)


def relu(v):
    return np.maximum(v, 0.0)


K, T, E, C, H, N = 1024, 2048, 8, 128, 512, 384


def by_expert(wq, xq):
    return np.concatenate([wq[e].T @ xq[:, e * C:(e + 1) * C] for e in range(E)], axis=1)


def setup_inputs():
    n = np.random.standard_normal
    s = mx_kscale(K)[:, None]
    u = mx_kscale(H)
    x = pack_weight(n((K, T)) * s, "e4m3")
    return {
        "x_words": x[0],
        "x_scales": x[1],
        "w1": (n((E, K, H)) / np.sqrt(K) / s[None] * u[None, None, :]).astype(np.float32),
        "w2": (n((E, H, N)) / np.sqrt(H) / u[None, :, None]).astype(np.float32),
        "gate": np.tile(np.random.uniform(0.2, 1.0, E * C), (N, 1)).astype(np.float32),
        "offs": striped(np.random.permutation(T)[:E * C]),
        "dst": striped(np.random.permutation(T)[:E * C]),
    }


def reference(x_words, x_scales, w1, w2, gate, offs, dst):
    idx = unstriped(offs)
    xq = unpack_weight(x_words, x_scales, "e4m3")[:, idx]
    h = relu(by_expert(mxq(f64(w1), 1, "e4m3"), xq))
    y = by_expert(mxq(f64(w2), 1, "e4m3"), mxq(h, 0, "e4m3"))
    out = np.zeros((N, T))
    out[:, unstriped(dst)] = f64(gate) * y
    return out

@@ -1,0 +1,199 @@
+from contextlib import ExitStack
+
+import concourse.mybir as mybir
+
+K, T, E, C, H, N = 1024, 2048, 8, 128, 512, 384
+S = E * C
+FLOPS = 2 * S * (K * H + H * N)
+
+F32 = mybir.dt.float32
+BF16 = mybir.dt.bfloat16
+I32 = mybir.dt.int32
+U32 = mybir.dt.uint32
+U16 = mybir.dt.uint16
+U8 = mybir.dt.uint8
+FP8X4 = mybir.dt.float8_e4m3fn_x4
+COPY = mybir.ActivationFunctionType.Copy
+RELU = mybir.ActivationFunctionType.Relu
+MULT = mybir.AluOpType.mult
+
+P = 128
+PACK = 4
+PASSES = K // (P * PACK)
+NT = N // P
+PAIR = 2 * C
+VECTOR_M = (0, 0)
+VECTOR_M_LAST = 64
+W2_ON_SCALAR = (6, 7)
+GATE_FIRST = False
+
+
+def tile_moe_two_mlp_relu_kernel(
+    tc, x_words, x_scales, w1, w2, gate, offs, dst, out
+):
+    nc = tc.nc
+    with ExitStack() as ctx:
+        keep = ctx.enter_context(tc.tile_pool(name="keep", bufs=1))
+        raw1 = ctx.enter_context(tc.tile_pool(name="raw1", bufs=8))
+        raw2 = ctx.enter_context(tc.tile_pool(name="raw2", bufs=4))
+        work = ctx.enter_context(tc.tile_pool(name="work", bufs=3))
+        code = ctx.enter_context(tc.tile_pool(name="code", bufs=6))
+        psum1 = ctx.enter_context(tc.psum_pool(name="psum1", bufs=3))
+        psum2 = ctx.enter_context(tc.psum_pool(name="psum2", bufs=4))
+
+        src_list = keep.tile([P, S // 16], U16, name="src_list")
+        dst_list = keep.tile([P, S // 16], U16, name="dst_list")
+        tok_words = [keep.tile([P, T], I32, name=f"tok_words{o}") for o in range(PASSES)]
+        tok_scales = keep.tile([P, T], U8, name="tok_scales")
+        slot_words = [keep.tile([P, S], U32, name=f"slot_words{o}", align_bytes=64) for o in range(PASSES)]
+        slot_scales = keep.tile([P, S], U8, name="slot_scales", align_bytes=64)
+        gate_sb = keep.tile([P, NT, S], F32, name="gate_sb")
+        out_sb = [keep.tile([P, T], F32, name=f"out_sb{c}") for c in range(NT)]
+        gate_rows = gate.rearrange("(c p) s -> p c s", p=P)
+
+        def load_words(o):
+            nc.sync.dma_start(tok_words[o][:], x_words[o].rearrange("p t r -> p (t r)").bitcast(I32))
+
+        def load_scales(o, q):
+            nc.sync.dma_start(
+                tok_scales[32 * q + 4 * o : 32 * q + 4 * o + 4, :].bitcast(I32),
+                x_scales[o, 4 * q : 4 * q + 4, :].bitcast(I32),
+            )
+
+        def load_w1(e, o):
+            raw = raw1.tile([P, PACK, H], F32, name="w1_raw")
+            nc.sync.dma_start(raw[:], w1[e, o * 512 : (o + 1) * 512, :].rearrange("(p j) i -> p j i", j=PACK))
+            return raw
+
+        def quantize_w1(raw, vector_m):
+            grouped = work.tile([P, PACK, P, PACK], BF16, name="w1_bf16", align_bytes=64)
+            src = raw[:].rearrange("p j (m t) -> p m j t", t=PACK)
+            dstv = grouped[:].rearrange("p t m j -> p m j t")
+            split = P - vector_m
+            if split > 0:
+                nc.scalar.activation(dstv[:, 0:split], src[:, 0:split], COPY)
+            if vector_m > 0:
+                nc.vector.tensor_copy(dstv[:, split:P], src[:, split:P])
+            codes = code.tile([P, H], U32, name="w1_codes", align_bytes=64)
+            scales = code.tile([P, H], U8, name="w1_scales", align_bytes=64)
+            nc.vector.quantize_mx(
+                out=codes[:].bitcast(FP8X4), scales=scales[:], in_=grouped[:].rearrange("p t m j -> p (t m j)")
+            )
+            return codes, scales
+
+        def first_layer(e, raws):
+            quantized = []
+            for o in range(PASSES):
+                last = e == E - 1 and o == PASSES - 1
+                quantized.append(quantize_w1(raws[o], VECTOR_M_LAST if last else VECTOR_M[o]))
+            slots = slice(e * C, (e + 1) * C)
+            acc = psum1.tile([P, PACK, C], F32, name="acc1")
+            for t in range(PACK):
+                cols = slice(t * P, (t + 1) * P)
+                for o in range(PASSES):
+                    codes, scales = quantized[o]
+                    nc.tensor.matmul_mx(
+                        out=acc[:, t, :],
+                        lhsT=codes[:, cols].bitcast(FP8X4),
+                        lhsT_scale=scales[:, cols],
+                        rhs=slot_words[o][:, slots].bitcast(FP8X4),
+                        rhs_scale=slot_scales[4 * o : P, slots],
+                        start=(o == 0),
+                        stop=(o == PASSES - 1),
+                    )
+            h_bf16 = work.tile([P, C, PACK], BF16, name="h_bf16", align_bytes=64)
+            nc.scalar.activation(h_bf16[:], acc[:].rearrange("p t s -> p s t"), RELU)
+            h_codes = code.tile([P, C], U32, name="h_codes", align_bytes=64)
+            h_scales = code.tile([P, C], U8, name="h_scales", align_bytes=64)
+            nc.vector.quantize_mx(
+                out=h_codes[:].bitcast(FP8X4), scales=h_scales[:], in_=h_bf16[:].rearrange("p s t -> p (s t)")
+            )
+            return h_codes, h_scales
+
+        def load_w2(e, c0, c1):
+            raw = raw2.tile([P, PACK, (c1 - c0) * P], F32, name="w2_raw")
+            nc.sync.dma_start(raw[:], w2[e, :, c0 * P : c1 * P].rearrange("(p j) n -> p j n", j=PACK))
+            return raw
+
+        def second_layer(e, h, raw, c0, c1, y_pair):
+            h_codes, h_scales = h
+            width = (c1 - c0) * P
+            grouped = work.tile([P, width, PACK], BF16, name="w2_bf16", align_bytes=64)
+            dstv = grouped[:].rearrange("p (g i) j -> p g j i", i=4)
+            src = raw[:].rearrange("p j (g i) -> p g j i", i=4)
+            if e in W2_ON_SCALAR:
+                nc.scalar.activation(dstv, src, COPY)
+            else:
+                nc.vector.tensor_copy(dstv, src)
+            codes = code.tile([P, width], U32, name="w2_codes", align_bytes=64)
+            scales = code.tile([P, width], U8, name="w2_scales", align_bytes=64)
+            for n0 in range(0, width, 256):
+                n1 = min(n0 + 256, width)
+                nc.vector.quantize_mx(
+                    out=codes[:, n0:n1].bitcast(FP8X4),
+                    scales=scales[:, n0:n1],
+                    in_=grouped[:, n0:n1, :].rearrange("p n j -> p (n j)"),
+                )
+            acc = psum2.tile([P, c1 - c0, C], F32, name="acc2")
+            for c in range(c1 - c0):
+                cols = slice(c * P, (c + 1) * P)
+                nc.tensor.matmul_mx(
+                    out=acc[:, c, :],
+                    lhsT=codes[:, cols].bitcast(FP8X4),
+                    lhsT_scale=scales[:, cols],
+                    rhs=h_codes[:].bitcast(FP8X4),
+                    rhs_scale=h_scales[:],
+                    start=True,
+                    stop=True,
+                )
+            half = slice((e % 2) * C, (e % 2 + 1) * C)
+            if GATE_FIRST:
+                nc.vector.tensor_tensor(y_pair[:, c0:c1, half], acc[:], gate_sb[:, c0:c1, e * C : (e + 1) * C], MULT)
+            else:
+                nc.scalar.copy(y_pair[:, c0:c1, half], acc[:])
+
+        def scatter(pair, c, y_pair):
+            window = out_sb[c][:].indirect(dst_list[:, pair * (PAIR // 16) : (pair + 1) * (PAIR // 16)])
+            if GATE_FIRST:
+                nc.vector.tensor_copy(window, y_pair[:, c, :])
+            else:
+                nc.vector.tensor_tensor(window, y_pair[:, c, :], gate_sb[:, c, pair * PAIR : (pair + 1) * PAIR], MULT)
+
+        nc.vector.memset(tok_scales[:].bitcast(I32), 0)
+        load_words(0)
+        nc.sync.dma_start(src_list[:], offs)
+        raws = [load_w1(0, 0)]
+        for q in range(4):
+            load_scales(0, q)
+        load_words(1)
+        for q in range(4):
+            load_scales(1, q)
+        raws.append(load_w1(0, 1))
+        nc.sync.dma_start(dst_list[:], dst)
+        for c in range(NT):
+            nc.vector.memset(out_sb[c][:], 0.0)
+        for o in range(PASSES):
+            nc.vector.tensor_copy(slot_words[o][:], tok_words[o][:].bitcast(U32).indirect(src_list[:]))
+        nc.vector.tensor_copy(slot_scales[:], tok_scales[:].indirect(src_list[:]))
+
+        h_prev = first_layer(0, raws)
+        early = S - PAIR
+        y_pair = None
+        for e in range(E):
+            h = h_prev
+            if e + 1 < E:
+                h_prev = first_layer(e + 1, [load_w1(e + 1, o) for o in range(PASSES)])
+            if e == 0:
+                nc.sync.dma_start(gate_sb[:, :, 0:early], gate_rows[:, :, 0:early])
+            if e == E - 2:
+                nc.sync.dma_start(gate_sb[:, :, early:S], gate_rows[:, :, early:S])
+            if e % 2 == 0:
+                y_pair = work.tile([P, NT, PAIR], F32, name="y_pair")
+            pieces = [(c, c + 1) for c in range(NT)] if e == E - 1 else [(0, NT)]
+            for c0, c1 in pieces:
+                second_layer(e, h, load_w2(e, c0, c1), c0, c1, y_pair)
+                if e % 2 == 1:
+                    for c in range(c0, c1):
+                        scatter(e // 2, c, y_pair)
+                        if e == E - 1:
+                            nc.sync.dma_start(out[c * P : (c + 1) * P, :], out_sb[c][:])

@@ -22,10 +22,20 @@ PACK = 4
 PASSES = K // (P * PACK)
 NT = N // P
 PAIR = 2 * C
-VECTOR_M = (0, 0)
-VECTOR_M_LAST = 64
-W2_ON_SCALAR = (6, 7)
-GATE_FIRST = False
+R1 = 9
+WB = 4
+SPLITQ = True
+L15 = True
+S2 = 16
+GATE_FIRST = True
+VM = [0, 0] + [32] * 10 + [48, 64, 48, 64]
+HEAD = [("x", 0), ("offs",), ("w", 0), ("s", 0), ("x", 1), ("s", 1), ("w", 1), ("dst",)]
+RA = [2, 4, 6, 8, 10, 12, 15]
+YA = [(p, c, 4 * p + 5 + c) for p in range(2) for c in range(3)]
+PIECES = [(0, 0, 3, 2, "V"), (1, 0, 3, 4, "V"), (2, 0, 3, 6, "V"), (3, 0, 3, 8, "V"), (4, 0, 2, 12, "S"), (5, 0, 2, 10, "V"), (6, 1, 2, 14, "V")]
+GL = [(0, 0, 3, 4), (1, 0, 3, 8), (2, 0, 1, 5)]
+TAILLOADS = [("w", 7, 0, 1), ("g", 2, 1, 2), ("w", 6, 0, 1), ("g", 3, 0, 1), ("w", 4, 2, 3), ("w", 7, 1, 2), ("g", 3, 1, 2), ("w", 5, 2, 3), ("w", 6, 2, 3), ("g", 3, 2, 3), ("w", 7, 2, 3), ("g", 2, 2, 3)]
+TAIL = [("D", 7, 0, 1, "S"), ("D", 6, 0, 1, "S"), ("R",), ("D", 4, 2, 3, "V"), ("D", 7, 1, 2, "S"), ("Y", 2, 1), ("Y", 2, 0), ("D", 5, 2, 3, "S"), ("D", 6, 2, 3, "S"), ("Y", 3, 0), ("D", 7, 2, 3, "S"), ("Y", 3, 1), ("Y", 2, 2), ("Y", 3, 2)]
 
 
 def tile_moe_two_mlp_relu_kernel(
@@ -34,22 +44,36 @@ def tile_moe_two_mlp_relu_kernel(
     nc = tc.nc
     with ExitStack() as ctx:
         keep = ctx.enter_context(tc.tile_pool(name="keep", bufs=1))
-        raw1 = ctx.enter_context(tc.tile_pool(name="raw1", bufs=8))
-        raw2 = ctx.enter_context(tc.tile_pool(name="raw2", bufs=4))
-        work = ctx.enter_context(tc.tile_pool(name="work", bufs=3))
-        code = ctx.enter_context(tc.tile_pool(name="code", bufs=6))
-        psum1 = ctx.enter_context(tc.psum_pool(name="psum1", bufs=3))
-        psum2 = ctx.enter_context(tc.psum_pool(name="psum2", bufs=4))
+        psum = ctx.enter_context(tc.psum_pool(name="psum", bufs=1))
+
+        def ring(pool, name, count, shape, dtype):
+            return [pool.tile(shape, dtype, name=f"{name}{i}", align_bytes=64) for i in range(count)]
 
         src_list = keep.tile([P, S // 16], U16, name="src_list")
         dst_list = keep.tile([P, S // 16], U16, name="dst_list")
-        tok_words = [keep.tile([P, T], I32, name=f"tok_words{o}") for o in range(PASSES)]
+        tok_words = ring(keep, "tok_words", PASSES, [P, T], I32)
         tok_scales = keep.tile([P, T], U8, name="tok_scales")
-        slot_words = [keep.tile([P, S], U32, name=f"slot_words{o}", align_bytes=64) for o in range(PASSES)]
+        slot_words = ring(keep, "slot_words", PASSES, [P, S], U32)
         slot_scales = keep.tile([P, S], U8, name="slot_scales", align_bytes=64)
         gate_sb = keep.tile([P, NT, S], F32, name="gate_sb")
-        out_sb = [keep.tile([P, T], F32, name=f"out_sb{c}") for c in range(NT)]
+        out_sb = ring(keep, "out_sb", NT, [P, T], F32)
+        w1_raw = ring(keep, "w1_raw", R1, [P, PACK, H], F32)
+        w1_bf16 = ring(keep, "w1_bf16", WB, [P, PACK, P, PACK], BF16)
+        w1_codes = ring(keep, "w1_codes", 6, [P, H], U32)
+        w1_scales = ring(keep, "w1_scales", 6, [P, H], U8)
+        w2_raw = ring(keep, "w2_raw", 4, [P, PACK * N], F32)
+        w2_bf16 = ring(keep, "w2_bf16", 4, [P, N, PACK], BF16)
+        w2_codes = ring(keep, "w2_codes", 4, [P, N], U32)
+        w2_scales = ring(keep, "w2_scales", 4, [P, N], U8)
+        h_codes = ring(keep, "h_codes", E, [P, C], U32)
+        h_scales = ring(keep, "h_scales", E, [P, C], U8)
+        h_last = keep.tile([P, C * PACK], BF16, name="h_last", align_bytes=64)
+        y_last = ring(keep, "y_last", 6, [P, PAIR], F32)
+        acc1 = [psum.tile([P, PACK, C], F32, name=f"acc1_{i}") for i in range(3)]
+        acc2 = [psum.tile([P, PAIR], F32, name=f"acc2_{i}") for i in range(5)]
         gate_rows = gate.rearrange("(c p) s -> p c s", p=P)
+        bank_of = {}
+        y_used = []
 
         def load_words(o):
             nc.sync.dma_start(tok_words[o][:], x_words[o].rearrange("p t r -> p (t r)").bitcast(I32))
@@ -60,140 +84,187 @@ def tile_moe_two_mlp_relu_kernel(
                 x_scales[o, 4 * q : 4 * q + 4, :].bitcast(I32),
             )
 
-        def load_w1(e, o):
-            raw = raw1.tile([P, PACK, H], F32, name="w1_raw")
-            nc.sync.dma_start(raw[:], w1[e, o * 512 : (o + 1) * 512, :].rearrange("(p j) i -> p j i", j=PACK))
-            return raw
+        def load_w1(u):
+            e, o = divmod(u, PASSES)
+            rows = w1[e, o * 512 : (o + 1) * 512, :].rearrange("(p j) i -> p j i", j=PACK)
+            parts = 2 if u == 15 and L15 else 1
+            for a in range(parts):
+                cols = slice(a * H // parts, (a + 1) * H // parts)
+                nc.sync.dma_start(w1_raw[u % R1][:, :, cols], rows[:, :, cols])
 
-        def quantize_w1(raw, vector_m):
-            grouped = work.tile([P, PACK, P, PACK], BF16, name="w1_bf16", align_bytes=64)
-            src = raw[:].rearrange("p j (m t) -> p m j t", t=PACK)
+        def quantize_w1(u):
+            grouped = w1_bf16[u % WB]
+            src = w1_raw[u % R1][:].rearrange("p j (m t) -> p m j t", t=PACK)
             dstv = grouped[:].rearrange("p t m j -> p m j t")
-            split = P - vector_m
+            split = P - VM[u]
             if split > 0:
                 nc.scalar.activation(dstv[:, 0:split], src[:, 0:split], COPY)
-            if vector_m > 0:
-                nc.vector.tensor_copy(dstv[:, split:P], src[:, split:P])
-            codes = code.tile([P, H], U32, name="w1_codes", align_bytes=64)
-            scales = code.tile([P, H], U8, name="w1_scales", align_bytes=64)
-            nc.vector.quantize_mx(
-                out=codes[:].bitcast(FP8X4), scales=scales[:], in_=grouped[:].rearrange("p t m j -> p (t m j)")
-            )
-            return codes, scales
+            end = P - S2 if u == 15 else P
+            if split < end:
+                nc.vector.tensor_copy(dstv[:, split:end], src[:, split:end])
+            if end < P:
+                nc.scalar.activation(dstv[:, end:P], src[:, end:P], COPY)
+            halves = 2 if u == 15 and SPLITQ else 1
+            for a in range(halves):
+                w = H // halves
+                nc.vector.quantize_mx(
+                    out=w1_codes[u % 6][:, a * w : (a + 1) * w].bitcast(FP8X4),
+                    scales=w1_scales[u % 6][:, a * w : (a + 1) * w],
+                    in_=grouped[:].rearrange("p t m j -> p (t m j)")[:, a * w * PACK : (a + 1) * w * PACK],
+                )
 
-        def first_layer(e, raws):
-            quantized = []
-            for o in range(PASSES):
-                last = e == E - 1 and o == PASSES - 1
-                quantized.append(quantize_w1(raws[o], VECTOR_M_LAST if last else VECTOR_M[o]))
+        def first_matmuls(e):
             slots = slice(e * C, (e + 1) * C)
-            acc = psum1.tile([P, PACK, C], F32, name="acc1")
             for t in range(PACK):
                 cols = slice(t * P, (t + 1) * P)
                 for o in range(PASSES):
-                    codes, scales = quantized[o]
+                    u = e * PASSES + o
                     nc.tensor.matmul_mx(
-                        out=acc[:, t, :],
-                        lhsT=codes[:, cols].bitcast(FP8X4),
-                        lhsT_scale=scales[:, cols],
+                        out=acc1[e % 3][:, t, :],
+                        lhsT=w1_codes[u % 6][:, cols].bitcast(FP8X4),
+                        lhsT_scale=w1_scales[u % 6][:, cols],
                         rhs=slot_words[o][:, slots].bitcast(FP8X4),
                         rhs_scale=slot_scales[4 * o : P, slots],
                         start=(o == 0),
                         stop=(o == PASSES - 1),
                     )
-            h_bf16 = work.tile([P, C, PACK], BF16, name="h_bf16", align_bytes=64)
-            nc.scalar.activation(h_bf16[:], acc[:].rearrange("p t s -> p s t"), RELU)
-            h_codes = code.tile([P, C], U32, name="h_codes", align_bytes=64)
-            h_scales = code.tile([P, C], U8, name="h_scales", align_bytes=64)
-            nc.vector.quantize_mx(
-                out=h_codes[:].bitcast(FP8X4), scales=h_scales[:], in_=h_bf16[:].rearrange("p s t -> p (s t)")
+
+        def hidden(e, u):
+            h_bf16 = h_last[:] if u is None else w1_raw[u % R1][:, 0, 0 : 2 * C].bitcast(BF16)
+            nc.scalar.activation(
+                h_bf16.rearrange("p (s t) -> p s t", t=PACK), acc1[e % 3][:].rearrange("p t s -> p s t"), RELU
             )
-            return h_codes, h_scales
+            nc.vector.quantize_mx(out=h_codes[e][:].bitcast(FP8X4), scales=h_scales[e][:], in_=h_bf16)
+
+        def w2_piece(e, c0, c1):
+            return w2_raw[e % 4][:, c0 * P * PACK : c1 * P * PACK].rearrange("p (j n) -> p j n", j=PACK)
 
         def load_w2(e, c0, c1):
-            raw = raw2.tile([P, PACK, (c1 - c0) * P], F32, name="w2_raw")
-            nc.sync.dma_start(raw[:], w2[e, :, c0 * P : c1 * P].rearrange("(p j) n -> p j n", j=PACK))
-            return raw
+            nc.sync.dma_start(w2_piece(e, c0, c1), w2[e, :, c0 * P : c1 * P].rearrange("(p j) n -> p j n", j=PACK))
 
-        def second_layer(e, h, raw, c0, c1, y_pair):
-            h_codes, h_scales = h
-            width = (c1 - c0) * P
-            grouped = work.tile([P, width, PACK], BF16, name="w2_bf16", align_bytes=64)
-            dstv = grouped[:].rearrange("p (g i) j -> p g j i", i=4)
-            src = raw[:].rearrange("p j (g i) -> p g j i", i=4)
-            if e in W2_ON_SCALAR:
+        def load_gate(pair, c0, c1):
+            cols = slice(pair * PAIR, (pair + 1) * PAIR)
+            nc.sync.dma_start(gate_sb[:, c0:c1, cols], gate_rows[:, c0:c1, cols])
+
+        def quantize_w2(e, c0, c1, engine):
+            grouped = w2_bf16[e % 4]
+            dstv = grouped[:, c0 * P : c1 * P, :].rearrange("p (g i) j -> p g j i", i=4)
+            src = w2_piece(e, c0, c1).rearrange("p j (g i) -> p g j i", i=4)
+            if engine == "S":
                 nc.scalar.activation(dstv, src, COPY)
             else:
                 nc.vector.tensor_copy(dstv, src)
-            codes = code.tile([P, width], U32, name="w2_codes", align_bytes=64)
-            scales = code.tile([P, width], U8, name="w2_scales", align_bytes=64)
-            for n0 in range(0, width, 256):
-                n1 = min(n0 + 256, width)
+            for a in range(c0, c1, 2):
+                cols = slice(a * P, min(a + 2, c1) * P)
                 nc.vector.quantize_mx(
-                    out=codes[:, n0:n1].bitcast(FP8X4),
-                    scales=scales[:, n0:n1],
-                    in_=grouped[:, n0:n1, :].rearrange("p n j -> p (n j)"),
+                    out=w2_codes[e % 4][:, cols].bitcast(FP8X4),
+                    scales=w2_scales[e % 4][:, cols],
+                    in_=grouped[:, cols, :].rearrange("p n j -> p (n j)"),
                 )
-            acc = psum2.tile([P, c1 - c0, C], F32, name="acc2")
-            for c in range(c1 - c0):
-                cols = slice(c * P, (c + 1) * P)
-                nc.tensor.matmul_mx(
-                    out=acc[:, c, :],
-                    lhsT=codes[:, cols].bitcast(FP8X4),
-                    lhsT_scale=scales[:, cols],
-                    rhs=h_codes[:].bitcast(FP8X4),
-                    rhs_scale=h_scales[:],
-                    start=True,
-                    stop=True,
-                )
-            half = slice((e % 2) * C, (e % 2 + 1) * C)
-            if GATE_FIRST:
-                nc.vector.tensor_tensor(y_pair[:, c0:c1, half], acc[:], gate_sb[:, c0:c1, e * C : (e + 1) * C], MULT)
-            else:
-                nc.scalar.copy(y_pair[:, c0:c1, half], acc[:])
 
-        def scatter(pair, c, y_pair):
-            window = out_sb[c][:].indirect(dst_list[:, pair * (PAIR // 16) : (pair + 1) * (PAIR // 16)])
-            if GATE_FIRST:
-                nc.vector.tensor_copy(window, y_pair[:, c, :])
+        def second_matmul(e, c):
+            bank = bank_of.setdefault((e // 2, c), len(bank_of) % 5)
+            cols = slice(c * P, (c + 1) * P)
+            nc.tensor.matmul_mx(
+                out=acc2[bank][:, (e % 2) * C : (e % 2 + 1) * C],
+                lhsT=w2_codes[e % 4][:, cols].bitcast(FP8X4),
+                lhsT_scale=w2_scales[e % 4][:, cols],
+                rhs=h_codes[e][:].bitcast(FP8X4),
+                rhs_scale=h_scales[e][:],
+                start=True,
+                stop=True,
+            )
+
+        def scatter(pair, c, u, slot):
+            if u is None:
+                y = y_last[len(y_used)][:]
+                y_used.append(y)
             else:
-                nc.vector.tensor_tensor(window, y_pair[:, c, :], gate_sb[:, c, pair * PAIR : (pair + 1) * PAIR], MULT)
+                y = w1_raw[u % R1][:, 1 + slot, 0:PAIR]
+            acc = acc2[bank_of[(pair, c)]]
+            window = out_sb[c][:].indirect(dst_list[:, pair * (PAIR // 16) : (pair + 1) * (PAIR // 16)])
+            weights = gate_sb[:, c, pair * PAIR : (pair + 1) * PAIR]
+            if GATE_FIRST:
+                nc.vector.tensor_tensor(y, acc[:], weights, MULT)
+                nc.vector.tensor_copy(window, y)
+            else:
+                nc.scalar.copy(y, acc[:])
+                nc.vector.tensor_tensor(window, y, weights, MULT)
 
         nc.vector.memset(tok_scales[:].bitcast(I32), 0)
-        load_words(0)
-        nc.sync.dma_start(src_list[:], offs)
-        raws = [load_w1(0, 0)]
-        for q in range(4):
-            load_scales(0, q)
-        load_words(1)
-        for q in range(4):
-            load_scales(1, q)
-        raws.append(load_w1(0, 1))
-        nc.sync.dma_start(dst_list[:], dst)
         for c in range(NT):
             nc.vector.memset(out_sb[c][:], 0.0)
-        for o in range(PASSES):
-            nc.vector.tensor_copy(slot_words[o][:], tok_words[o][:].bitcast(U32).indirect(src_list[:]))
+        for item in HEAD:
+            if item[0] == "x":
+                load_words(item[1])
+            elif item[0] == "offs":
+                nc.sync.dma_start(src_list[:], offs)
+            elif item[0] == "dst":
+                nc.sync.dma_start(dst_list[:], dst)
+            elif item[0] == "s":
+                for q in range(4):
+                    load_scales(item[1], q)
+            else:
+                load_w1(item[1])
+        nc.vector.tensor_copy(slot_words[0][:], tok_words[0][:].bitcast(U32).indirect(src_list[:]))
+        quantize_w1(0)
+        nc.vector.tensor_copy(slot_words[1][:], tok_words[1][:].bitcast(U32).indirect(src_list[:]))
         nc.vector.tensor_copy(slot_scales[:], tok_scales[:].indirect(src_list[:]))
+        quantize_w1(1)
+        first_matmuls(0)
 
-        h_prev = first_layer(0, raws)
-        early = S - PAIR
-        y_pair = None
-        for e in range(E):
-            h = h_prev
-            if e + 1 < E:
-                h_prev = first_layer(e + 1, [load_w1(e + 1, o) for o in range(PASSES)])
-            if e == 0:
-                nc.sync.dma_start(gate_sb[:, :, 0:early], gate_rows[:, :, 0:early])
-            if e == E - 2:
-                nc.sync.dma_start(gate_sb[:, :, early:S], gate_rows[:, :, early:S])
-            if e % 2 == 0:
-                y_pair = work.tile([P, NT, PAIR], F32, name="y_pair")
-            pieces = [(c, c + 1) for c in range(NT)] if e == E - 1 else [(0, NT)]
-            for c0, c1 in pieces:
-                second_layer(e, h, load_w2(e, c0, c1), c0, c1, y_pair)
-                if e % 2 == 1:
+        have_h, have_w, have_m, have_y = set(), set(), set(), set()
+
+        def ready_matmuls():
+            for e, c in sorted(have_w):
+                if e in have_h and (e, c) not in have_m:
+                    second_matmul(e, c)
+                    have_m.add((e, c))
+
+        for u in range(2, 16):
+            load_w1(u)
+            for e, c0, c1, uu, engine in PIECES:
+                if uu == u:
+                    load_w2(e, c0, c1)
+            for pair, c0, c1, uu in GL:
+                if uu == u:
+                    load_gate(pair, c0, c1)
+            quantize_w1(u)
+            if u % 2:
+                first_matmuls(u // 2)
+            for e in range(E - 1):
+                if RA[e] == u:
+                    hidden(e, u)
+                    have_h.add(e)
+            n = 0
+            for pair, c, uu in YA:
+                if uu == u:
+                    scatter(pair, c, u, n)
+                    n += 1
+                    have_y.add((pair, c))
+            for e, c0, c1, uu, engine in PIECES:
+                if uu == u:
+                    quantize_w2(e, c0, c1, engine)
                     for c in range(c0, c1):
-                        scatter(e // 2, c, y_pair)
-                        if e == E - 1:
-                            nc.sync.dma_start(out[c * P : (c + 1) * P, :], out_sb[c][:])
+                        have_w.add((e, c))
+            ready_matmuls()
+        for item in TAILLOADS:
+            if item[0] == "g":
+                load_gate(item[1], item[2], item[3])
+            else:
+                load_w2(item[1], item[2], item[3])
+        for item in TAIL:
+            if item[0] == "R":
+                hidden(E - 1, None)
+                have_h.add(E - 1)
+            elif item[0] == "D":
+                quantize_w2(item[1], item[2], item[3], item[4])
+                for c in range(item[2], item[3]):
+                    have_w.add((item[1], c))
+            else:
+                scatter(item[1], item[2], None, 0)
+                have_y.add((item[1], item[2]))
+                if all((pair, item[2]) in have_y for pair in range(4)):
+                    c = item[2]
+                    nc.sync.dma_start(out[c * P : (c + 1) * P, :], out_sb[c][:])
+            ready_matmuls()

@@ -27,15 +27,15 @@ WB = 4
 SPLITQ = True
 L15 = True
 S2 = 16
-GATE_FIRST = True
-VM = [0, 0] + [32] * 10 + [48, 64, 48, 64]
+GATE_FIRST = False
+VM = [0, 0] + [16, 32] * 5 + [16, 64, 48, 64]
 HEAD = [("x", 0), ("offs",), ("w", 0), ("s", 0), ("x", 1), ("s", 1), ("w", 1), ("dst",)]
-RA = [2, 4, 6, 8, 10, 12, 15]
-YA = [(p, c, 4 * p + 5 + c) for p in range(2) for c in range(3)]
-PIECES = [(0, 0, 3, 2, "V"), (1, 0, 3, 4, "V"), (2, 0, 3, 6, "V"), (3, 0, 3, 8, "V"), (4, 0, 2, 12, "S"), (5, 0, 2, 10, "V"), (6, 1, 2, 14, "V")]
-GL = [(0, 0, 3, 4), (1, 0, 3, 8), (2, 0, 1, 5)]
-TAILLOADS = [("w", 7, 0, 1), ("g", 2, 1, 2), ("w", 6, 0, 1), ("g", 3, 0, 1), ("w", 4, 2, 3), ("w", 7, 1, 2), ("g", 3, 1, 2), ("w", 5, 2, 3), ("w", 6, 2, 3), ("g", 3, 2, 3), ("w", 7, 2, 3), ("g", 2, 2, 3)]
-TAIL = [("D", 7, 0, 1, "S"), ("D", 6, 0, 1, "S"), ("R",), ("D", 4, 2, 3, "V"), ("D", 7, 1, 2, "S"), ("Y", 2, 1), ("Y", 2, 0), ("D", 5, 2, 3, "S"), ("D", 6, 2, 3, "S"), ("Y", 3, 0), ("D", 7, 2, 3, "S"), ("Y", 3, 1), ("Y", 2, 2), ("Y", 3, 2)]
+RA = [2, 4, 6, 8, 10, 12, 14]
+YA = [(p, c, 4 * p + 5 + c) for p in range(2) for c in range(3)] + [(2, 0, 13), (2, 1, 15)]
+PIECES = [(0, 0, 3, 2, "V"), (1, 0, 3, 4, "V"), (2, 0, 3, 6, "V"), (3, 0, 3, 8, "V"), (4, 0, 2, 10, "V"), (5, 0, 2, 12, "S")]
+GL = [(0, 0, 3, 4), (1, 0, 3, 8), (2, 0, 2, 12)]
+TAILLOADS = [("w", 6, 0, 1), ("w", 7, 0, 2), ("w", 7, 2, 3), ("w", 6, 1, 3), ("g", 3, 0, 3), ("w", 4, 2, 3), ("w", 5, 2, 3), ("g", 2, 2, 3)]
+TAIL = [("D", 6, 0, 1, "S"), ("D", 7, 0, 2, "S"), ("R",), ("D", 7, 2, 3, "S"), ("D", 6, 1, 3, "V"), ("Y", 3, 0), ("D", 4, 2, 3, "S"), ("D", 5, 2, 3, "S"), ("Y", 3, 1), ("Y", 3, 2), ("Y", 2, 2)]
 
 
 def tile_moe_two_mlp_relu_kernel(

@@ -19,23 +19,34 @@ MULT = mybir.AluOpType.mult
 
 P = 128
 PACK = 4
-PASSES = K // (P * PACK)
-NT = N // P
+K_PASS = P * PACK
+PASSES = K // K_PASS
+UNITS = E * PASSES
+LAST_UNIT = UNITS - 1
+ROW_TILES = N // P
 PAIR = 2 * C
-R1 = 9
-WB = 4
-SPLITQ = True
-L15 = True
-S2 = 16
-GATE_FIRST = False
-VM = [0, 0] + [16, 32] * 5 + [16, 64, 48, 64]
-HEAD = [("x", 0), ("offs",), ("w", 0), ("s", 0), ("x", 1), ("s", 1), ("w", 1), ("dst",)]
-RA = [2, 4, 6, 8, 10, 12, 14]
-YA = [(p, c, 4 * p + 5 + c) for p in range(2) for c in range(3)] + [(2, 0, 13), (2, 1, 15)]
-PIECES = [(0, 0, 3, 2, "V"), (1, 0, 3, 4, "V"), (2, 0, 3, 6, "V"), (3, 0, 3, 8, "V"), (4, 0, 2, 10, "V"), (5, 0, 2, 12, "S")]
-GL = [(0, 0, 3, 4), (1, 0, 3, 8), (2, 0, 2, 12)]
-TAILLOADS = [("w", 6, 0, 1), ("w", 7, 0, 2), ("w", 7, 2, 3), ("w", 6, 1, 3), ("g", 3, 0, 3), ("w", 4, 2, 3), ("w", 5, 2, 3), ("g", 2, 2, 3)]
-TAIL = [("D", 6, 0, 1, "S"), ("D", 7, 0, 2, "S"), ("R",), ("D", 7, 2, 3, "S"), ("D", 6, 1, 3, "V"), ("Y", 3, 0), ("D", 4, 2, 3, "S"), ("D", 5, 2, 3, "S"), ("Y", 3, 1), ("Y", 3, 2), ("Y", 2, 2)]
+PAIRS = E // 2
+LIST_ROWS = 16
+QUADRANT = 32
+SCALE_ROWS = 4
+
+W1_RAW_DEPTH = 9
+W1_BF16_DEPTH = 4
+W1_CODE_DEPTH = 6
+W2_DEPTH = 4
+ACC1_BANKS = 3
+ACC2_BANKS = 5
+
+VECTOR_SHARE = [0, 0] + [16, 32] * 5 + [16, 64, 48, 64]
+LAST_SCALAR_SHARE = 16
+
+STREAM_PIECES = {2 * e + 2: (e, 0, ROW_TILES if e < 4 else 2, e == 5) for e in range(6)}
+STREAM_GATES = {4 * pair + 4: (pair, 0, ROW_TILES if pair < 2 else 2) for pair in range(3)}
+STREAM_SCATTERS = {
+    **{4 * pair + 5 + c: (pair, c) for pair in range(2) for c in range(ROW_TILES)},
+    13: (2, 0),
+    LAST_UNIT: (2, 1),
+}
 
 
 def tile_moe_two_mlp_relu_kernel(
@@ -46,71 +57,71 @@ def tile_moe_two_mlp_relu_kernel(
         keep = ctx.enter_context(tc.tile_pool(name="keep", bufs=1))
         psum = ctx.enter_context(tc.psum_pool(name="psum", bufs=1))
 
-        def ring(pool, name, count, shape, dtype):
-            return [pool.tile(shape, dtype, name=f"{name}{i}", align_bytes=64) for i in range(count)]
+        def ring(name, count, shape, dtype):
+            return [keep.tile(shape, dtype, name=f"{name}{i}", align_bytes=64) for i in range(count)]
 
-        src_list = keep.tile([P, S // 16], U16, name="src_list")
-        dst_list = keep.tile([P, S // 16], U16, name="dst_list")
-        tok_words = ring(keep, "tok_words", PASSES, [P, T], I32)
+        src_list = keep.tile([P, S // LIST_ROWS], U16, name="src_list")
+        dst_list = keep.tile([P, S // LIST_ROWS], U16, name="dst_list")
+        tok_words = ring("tok_words", PASSES, [P, T], I32)
         tok_scales = keep.tile([P, T], U8, name="tok_scales")
-        slot_words = ring(keep, "slot_words", PASSES, [P, S], U32)
+        slot_words = ring("slot_words", PASSES, [P, S], U32)
         slot_scales = keep.tile([P, S], U8, name="slot_scales", align_bytes=64)
-        gate_sb = keep.tile([P, NT, S], F32, name="gate_sb")
-        out_sb = ring(keep, "out_sb", NT, [P, T], F32)
-        w1_raw = ring(keep, "w1_raw", R1, [P, PACK, H], F32)
-        w1_bf16 = ring(keep, "w1_bf16", WB, [P, PACK, P, PACK], BF16)
-        w1_codes = ring(keep, "w1_codes", 6, [P, H], U32)
-        w1_scales = ring(keep, "w1_scales", 6, [P, H], U8)
-        w2_raw = ring(keep, "w2_raw", 4, [P, PACK * N], F32)
-        w2_bf16 = ring(keep, "w2_bf16", 4, [P, N, PACK], BF16)
-        w2_codes = ring(keep, "w2_codes", 4, [P, N], U32)
-        w2_scales = ring(keep, "w2_scales", 4, [P, N], U8)
-        h_codes = ring(keep, "h_codes", E, [P, C], U32)
-        h_scales = ring(keep, "h_scales", E, [P, C], U8)
+        gate_sb = keep.tile([P, ROW_TILES, S], F32, name="gate_sb")
+        out_sb = ring("out_sb", ROW_TILES, [P, T], F32)
+        w1_raw = ring("w1_raw", W1_RAW_DEPTH, [P, PACK, H], F32)
+        w1_bf16 = ring("w1_bf16", W1_BF16_DEPTH, [P, PACK, P, PACK], BF16)
+        w1_codes = ring("w1_codes", W1_CODE_DEPTH, [P, H], U32)
+        w1_scales = ring("w1_scales", W1_CODE_DEPTH, [P, H], U8)
+        w2_raw = ring("w2_raw", W2_DEPTH, [P, PACK * N], F32)
+        w2_bf16 = ring("w2_bf16", W2_DEPTH, [P, N, PACK], BF16)
+        w2_codes = ring("w2_codes", W2_DEPTH, [P, N], U32)
+        w2_scales = ring("w2_scales", W2_DEPTH, [P, N], U8)
+        h_codes = ring("h_codes", E, [P, C], U32)
+        h_scales = ring("h_scales", E, [P, C], U8)
         h_last = keep.tile([P, C * PACK], BF16, name="h_last", align_bytes=64)
-        y_last = ring(keep, "y_last", 6, [P, PAIR], F32)
-        acc1 = [psum.tile([P, PACK, C], F32, name=f"acc1_{i}") for i in range(3)]
-        acc2 = [psum.tile([P, PAIR], F32, name=f"acc2_{i}") for i in range(5)]
+        y_last = ring("y_last", ROW_TILES + 1, [P, PAIR], F32)
+        acc1 = [psum.tile([P, PACK, C], F32, name=f"acc1_{i}") for i in range(ACC1_BANKS)]
+        acc2 = [psum.tile([P, PAIR], F32, name=f"acc2_{i}") for i in range(ACC2_BANKS)]
         gate_rows = gate.rearrange("(c p) s -> p c s", p=P)
         bank_of = {}
-        y_used = []
 
         def load_words(o):
             nc.sync.dma_start(tok_words[o][:], x_words[o].rearrange("p t r -> p (t r)").bitcast(I32))
 
-        def load_scales(o, q):
-            nc.sync.dma_start(
-                tok_scales[32 * q + 4 * o : 32 * q + 4 * o + 4, :].bitcast(I32),
-                x_scales[o, 4 * q : 4 * q + 4, :].bitcast(I32),
-            )
+        def load_scales(rows):
+            for r in rows:
+                for o in range(PASSES):
+                    nc.sync.dma_start(
+                        tok_scales[SCALE_ROWS * o + r : P : QUADRANT, :].bitcast(I32),
+                        x_scales[o, r::SCALE_ROWS, :].bitcast(I32),
+                    )
 
         def load_w1(u):
             e, o = divmod(u, PASSES)
-            rows = w1[e, o * 512 : (o + 1) * 512, :].rearrange("(p j) i -> p j i", j=PACK)
-            parts = 2 if u == 15 and L15 else 1
+            rows = w1[e, o * K_PASS : (o + 1) * K_PASS, :].rearrange("(p j) i -> p j i", j=PACK)
+            parts = 2 if u == LAST_UNIT else 1
             for a in range(parts):
                 cols = slice(a * H // parts, (a + 1) * H // parts)
-                nc.sync.dma_start(w1_raw[u % R1][:, :, cols], rows[:, :, cols])
+                nc.sync.dma_start(w1_raw[u % W1_RAW_DEPTH][:, :, cols], rows[:, :, cols])
 
         def quantize_w1(u):
-            grouped = w1_bf16[u % WB]
-            src = w1_raw[u % R1][:].rearrange("p j (m t) -> p m j t", t=PACK)
-            dstv = grouped[:].rearrange("p t m j -> p m j t")
-            split = P - VM[u]
-            if split > 0:
-                nc.scalar.activation(dstv[:, 0:split], src[:, 0:split], COPY)
-            end = P - S2 if u == 15 else P
-            if split < end:
-                nc.vector.tensor_copy(dstv[:, split:end], src[:, split:end])
-            if end < P:
-                nc.scalar.activation(dstv[:, end:P], src[:, end:P], COPY)
-            halves = 2 if u == 15 and SPLITQ else 1
-            for a in range(halves):
-                w = H // halves
+            grouped = w1_bf16[u % W1_BF16_DEPTH]
+            source = w1_raw[u % W1_RAW_DEPTH][:].rearrange("p j (m t) -> p m j t", t=PACK)
+            target = grouped[:].rearrange("p t m j -> p m j t")
+            vector_from = P - VECTOR_SHARE[u]
+            vector_to = P - LAST_SCALAR_SHARE if u == LAST_UNIT else P
+            nc.scalar.activation(target[:, 0:vector_from], source[:, 0:vector_from], COPY)
+            if vector_from < vector_to:
+                nc.vector.tensor_copy(target[:, vector_from:vector_to], source[:, vector_from:vector_to])
+            if vector_to < P:
+                nc.scalar.activation(target[:, vector_to:P], source[:, vector_to:P], COPY)
+            parts = 2 if u == LAST_UNIT else 1
+            width = H // parts
+            for a in range(parts):
                 nc.vector.quantize_mx(
-                    out=w1_codes[u % 6][:, a * w : (a + 1) * w].bitcast(FP8X4),
-                    scales=w1_scales[u % 6][:, a * w : (a + 1) * w],
-                    in_=grouped[:].rearrange("p t m j -> p (t m j)")[:, a * w * PACK : (a + 1) * w * PACK],
+                    out=w1_codes[u % W1_CODE_DEPTH][:, a * width : (a + 1) * width].bitcast(FP8X4),
+                    scales=w1_scales[u % W1_CODE_DEPTH][:, a * width : (a + 1) * width],
+                    in_=grouped[:].rearrange("p t m j -> p (t m j)")[:, a * width * PACK : (a + 1) * width * PACK],
                 )
 
         def first_matmuls(e):
@@ -120,24 +131,25 @@ def tile_moe_two_mlp_relu_kernel(
                 for o in range(PASSES):
                     u = e * PASSES + o
                     nc.tensor.matmul_mx(
-                        out=acc1[e % 3][:, t, :],
-                        lhsT=w1_codes[u % 6][:, cols].bitcast(FP8X4),
-                        lhsT_scale=w1_scales[u % 6][:, cols],
+                        out=acc1[e % ACC1_BANKS][:, t, :],
+                        lhsT=w1_codes[u % W1_CODE_DEPTH][:, cols].bitcast(FP8X4),
+                        lhsT_scale=w1_scales[u % W1_CODE_DEPTH][:, cols],
                         rhs=slot_words[o][:, slots].bitcast(FP8X4),
-                        rhs_scale=slot_scales[4 * o : P, slots],
+                        rhs_scale=slot_scales[SCALE_ROWS * o : P, slots],
                         start=(o == 0),
                         stop=(o == PASSES - 1),
                     )
 
-        def hidden(e, u):
-            h_bf16 = h_last[:] if u is None else w1_raw[u % R1][:, 0, 0 : 2 * C].bitcast(BF16)
+        def quantize_h(e, h_bf16):
             nc.scalar.activation(
-                h_bf16.rearrange("p (s t) -> p s t", t=PACK), acc1[e % 3][:].rearrange("p t s -> p s t"), RELU
+                h_bf16.rearrange("p (s t) -> p s t", t=PACK),
+                acc1[e % ACC1_BANKS][:].rearrange("p t s -> p s t"),
+                RELU,
             )
             nc.vector.quantize_mx(out=h_codes[e][:].bitcast(FP8X4), scales=h_scales[e][:], in_=h_bf16)
 
         def w2_piece(e, c0, c1):
-            return w2_raw[e % 4][:, c0 * P * PACK : c1 * P * PACK].rearrange("p (j n) -> p j n", j=PACK)
+            return w2_raw[e % W2_DEPTH][:, c0 * P * PACK : c1 * P * PACK].rearrange("p (j n) -> p j n", j=PACK)
 
         def load_w2(e, c0, c1):
             nc.sync.dma_start(w2_piece(e, c0, c1), w2[e, :, c0 * P : c1 * P].rearrange("(p j) n -> p j n", j=PACK))
@@ -146,66 +158,61 @@ def tile_moe_two_mlp_relu_kernel(
             cols = slice(pair * PAIR, (pair + 1) * PAIR)
             nc.sync.dma_start(gate_sb[:, c0:c1, cols], gate_rows[:, c0:c1, cols])
 
-        def quantize_w2(e, c0, c1, engine):
-            grouped = w2_bf16[e % 4]
-            dstv = grouped[:, c0 * P : c1 * P, :].rearrange("p (g i) j -> p g j i", i=4)
-            src = w2_piece(e, c0, c1).rearrange("p j (g i) -> p g j i", i=4)
-            if engine == "S":
-                nc.scalar.activation(dstv, src, COPY)
+        def quantize_w2(e, c0, c1, on_scalar):
+            grouped = w2_bf16[e % W2_DEPTH]
+            target = grouped[:, c0 * P : c1 * P, :].rearrange("p (g n) j -> p g j n", n=4)
+            source = w2_piece(e, c0, c1).rearrange("p j (g n) -> p g j n", n=4)
+            if on_scalar:
+                nc.scalar.activation(target, source, COPY)
             else:
-                nc.vector.tensor_copy(dstv, src)
-            for a in range(c0, c1, 2):
-                cols = slice(a * P, min(a + 2, c1) * P)
+                nc.vector.tensor_copy(target, source)
+            for c in range(c0, c1, 2):
+                cols = slice(c * P, min(c + 2, c1) * P)
                 nc.vector.quantize_mx(
-                    out=w2_codes[e % 4][:, cols].bitcast(FP8X4),
-                    scales=w2_scales[e % 4][:, cols],
+                    out=w2_codes[e % W2_DEPTH][:, cols].bitcast(FP8X4),
+                    scales=w2_scales[e % W2_DEPTH][:, cols],
                     in_=grouped[:, cols, :].rearrange("p n j -> p (n j)"),
                 )
 
-        def second_matmul(e, c):
-            bank = bank_of.setdefault((e // 2, c), len(bank_of) % 5)
-            cols = slice(c * P, (c + 1) * P)
-            nc.tensor.matmul_mx(
-                out=acc2[bank][:, (e % 2) * C : (e % 2 + 1) * C],
-                lhsT=w2_codes[e % 4][:, cols].bitcast(FP8X4),
-                lhsT_scale=w2_scales[e % 4][:, cols],
-                rhs=h_codes[e][:].bitcast(FP8X4),
-                rhs_scale=h_scales[e][:],
-                start=True,
-                stop=True,
+        def second_matmuls(e, c0, c1):
+            for c in range(c0, c1):
+                bank = bank_of.setdefault((e // 2, c), len(bank_of) % ACC2_BANKS)
+                cols = slice(c * P, (c + 1) * P)
+                nc.tensor.matmul_mx(
+                    out=acc2[bank][:, (e % 2) * C : (e % 2 + 1) * C],
+                    lhsT=w2_codes[e % W2_DEPTH][:, cols].bitcast(FP8X4),
+                    lhsT_scale=w2_scales[e % W2_DEPTH][:, cols],
+                    rhs=h_codes[e][:].bitcast(FP8X4),
+                    rhs_scale=h_scales[e][:],
+                    start=True,
+                    stop=True,
+                )
+
+        def scatter(pair, c, y):
+            columns = PAIR // LIST_ROWS
+            nc.scalar.copy(y, acc2[bank_of[(pair, c)]][:])
+            nc.vector.tensor_tensor(
+                out_sb[c][:].indirect(dst_list[:, pair * columns : (pair + 1) * columns]),
+                y,
+                gate_sb[:, c, pair * PAIR : (pair + 1) * PAIR],
+                MULT,
             )
 
-        def scatter(pair, c, u, slot):
-            if u is None:
-                y = y_last[len(y_used)][:]
-                y_used.append(y)
-            else:
-                y = w1_raw[u % R1][:, 1 + slot, 0:PAIR]
-            acc = acc2[bank_of[(pair, c)]]
-            window = out_sb[c][:].indirect(dst_list[:, pair * (PAIR // 16) : (pair + 1) * (PAIR // 16)])
-            weights = gate_sb[:, c, pair * PAIR : (pair + 1) * PAIR]
-            if GATE_FIRST:
-                nc.vector.tensor_tensor(y, acc[:], weights, MULT)
-                nc.vector.tensor_copy(window, y)
-            else:
-                nc.scalar.copy(y, acc[:])
-                nc.vector.tensor_tensor(window, y, weights, MULT)
+        def store(c):
+            nc.sync.dma_start(out[c * P : (c + 1) * P, :], out_sb[c][:])
 
         nc.vector.memset(tok_scales[:].bitcast(I32), 0)
-        for c in range(NT):
+        for c in range(ROW_TILES):
             nc.vector.memset(out_sb[c][:], 0.0)
-        for item in HEAD:
-            if item[0] == "x":
-                load_words(item[1])
-            elif item[0] == "offs":
-                nc.sync.dma_start(src_list[:], offs)
-            elif item[0] == "dst":
-                nc.sync.dma_start(dst_list[:], dst)
-            elif item[0] == "s":
-                for q in range(4):
-                    load_scales(item[1], q)
-            else:
-                load_w1(item[1])
+
+        load_words(0)
+        nc.sync.dma_start(src_list[:], offs)
+        load_w1(0)
+        load_scales((0, 1))
+        load_words(1)
+        load_scales((2, 3))
+        load_w1(1)
+        nc.sync.dma_start(dst_list[:], dst)
         nc.vector.tensor_copy(slot_words[0][:], tok_words[0][:].bitcast(U32).indirect(src_list[:]))
         quantize_w1(0)
         nc.vector.tensor_copy(slot_words[1][:], tok_words[1][:].bitcast(U32).indirect(src_list[:]))
@@ -213,58 +220,48 @@ def tile_moe_two_mlp_relu_kernel(
         quantize_w1(1)
         first_matmuls(0)
 
-        have_h, have_w, have_m, have_y = set(), set(), set(), set()
-
-        def ready_matmuls():
-            for e, c in sorted(have_w):
-                if e in have_h and (e, c) not in have_m:
-                    second_matmul(e, c)
-                    have_m.add((e, c))
-
-        for u in range(2, 16):
+        for u in range(PASSES, UNITS):
+            staging = w1_raw[u % W1_RAW_DEPTH]
             load_w1(u)
-            for e, c0, c1, uu, engine in PIECES:
-                if uu == u:
-                    load_w2(e, c0, c1)
-            for pair, c0, c1, uu in GL:
-                if uu == u:
-                    load_gate(pair, c0, c1)
+            if u in STREAM_PIECES:
+                load_w2(*STREAM_PIECES[u][:3])
+            if u in STREAM_GATES:
+                load_gate(*STREAM_GATES[u])
             quantize_w1(u)
-            if u % 2:
-                first_matmuls(u // 2)
-            for e in range(E - 1):
-                if RA[e] == u:
-                    hidden(e, u)
-                    have_h.add(e)
-            n = 0
-            for pair, c, uu in YA:
-                if uu == u:
-                    scatter(pair, c, u, n)
-                    n += 1
-                    have_y.add((pair, c))
-            for e, c0, c1, uu, engine in PIECES:
-                if uu == u:
-                    quantize_w2(e, c0, c1, engine)
-                    for c in range(c0, c1):
-                        have_w.add((e, c))
-            ready_matmuls()
-        for item in TAILLOADS:
-            if item[0] == "g":
-                load_gate(item[1], item[2], item[3])
+            if u % PASSES == PASSES - 1:
+                first_matmuls(u // PASSES)
             else:
-                load_w2(item[1], item[2], item[3])
-        for item in TAIL:
-            if item[0] == "R":
-                hidden(E - 1, None)
-                have_h.add(E - 1)
-            elif item[0] == "D":
-                quantize_w2(item[1], item[2], item[3], item[4])
-                for c in range(item[2], item[3]):
-                    have_w.add((item[1], c))
-            else:
-                scatter(item[1], item[2], None, 0)
-                have_y.add((item[1], item[2]))
-                if all((pair, item[2]) in have_y for pair in range(4)):
-                    c = item[2]
-                    nc.sync.dma_start(out[c * P : (c + 1) * P, :], out_sb[c][:])
-            ready_matmuls()
+                quantize_h(u // PASSES - 1, staging[:, 0, 0 : H // 2].bitcast(BF16))
+            if u in STREAM_SCATTERS:
+                scatter(*STREAM_SCATTERS[u], staging[:, 1, 0:PAIR])
+            if u in STREAM_PIECES:
+                quantize_w2(*STREAM_PIECES[u])
+                second_matmuls(*STREAM_PIECES[u][:3])
+
+        load_w2(6, 0, 1)
+        load_w2(7, 0, 2)
+        load_w2(7, 2, 3)
+        load_w2(6, 1, 3)
+        load_gate(3, 0, 3)
+        load_w2(4, 2, 3)
+        load_w2(5, 2, 3)
+        load_gate(2, 2, 3)
+        quantize_w2(6, 0, 1, True)
+        second_matmuls(6, 0, 1)
+        quantize_w2(7, 0, 2, True)
+        quantize_h(7, h_last[:])
+        second_matmuls(7, 0, 2)
+        quantize_w2(7, 2, 3, True)
+        second_matmuls(7, 2, 3)
+        quantize_w2(6, 1, 3, False)
+        second_matmuls(6, 1, 3)
+        scatter(3, 0, y_last[0][:])
+        store(0)
+        for e in (4, 5):
+            quantize_w2(e, 2, 3, True)
+            second_matmuls(e, 2, 3)
+        scatter(3, 1, y_last[1][:])
+        store(1)
+        scatter(3, 2, y_last[2][:])
+        scatter(2, 2, y_last[3][:])
+        store(2)

@@ -5,6 +5,7 @@ import concourse.mybir as mybir
 K, T, E, C, H, N = 1024, 2048, 8, 128, 512, 384
 S = E * C
 FLOPS = 2 * S * (K * H + H * N)
+BYTES = K * T + K // 32 * T + 4 * (E * H * (K + N) + 128 * S + N * T) + 2 * 2 * 8 * S
 
 F32 = mybir.dt.float32
 BF16 = mybir.dt.bfloat16
@@ -41,7 +42,7 @@ VECTOR_SHARE = [0, 0] + [16, 32] * 5 + [16, 64, 48, 64]
 LAST_SCALAR_SHARE = 16
 
 STREAM_PIECES = {2 * e + 2: (e, 0, ROW_TILES if e < 4 else 2, e == 5) for e in range(6)}
-STREAM_GATES = {4 * pair + 4: (pair, 0, ROW_TILES if pair < 2 else 2) for pair in range(3)}
+GATE_UNIT = 3
 STREAM_SCATTERS = {
     **{4 * pair + 5 + c: (pair, c) for pair in range(2) for c in range(ROW_TILES)},
     13: (2, 0),
@@ -66,7 +67,7 @@ def tile_moe_two_mlp_relu_kernel(
         tok_scales = keep.tile([P, T], U8, name="tok_scales")
         slot_words = ring("slot_words", PASSES, [P, S], U32)
         slot_scales = keep.tile([P, S], U8, name="slot_scales", align_bytes=64)
-        gate_sb = keep.tile([P, ROW_TILES, S], F32, name="gate_sb")
+        gate_sb = keep.tile([P, S], F32, name="gate_sb")
         out_sb = ring("out_sb", ROW_TILES, [P, T], F32)
         w1_raw = ring("w1_raw", W1_RAW_DEPTH, [P, PACK, H], F32)
         w1_bf16 = ring("w1_bf16", W1_BF16_DEPTH, [P, PACK, P, PACK], BF16)
@@ -82,7 +83,6 @@ def tile_moe_two_mlp_relu_kernel(
         y_last = ring("y_last", ROW_TILES + 1, [P, PAIR], F32)
         acc1 = [psum.tile([P, PACK, C], F32, name=f"acc1_{i}") for i in range(ACC1_BANKS)]
         acc2 = [psum.tile([P, PAIR], F32, name=f"acc2_{i}") for i in range(ACC2_BANKS)]
-        gate_rows = gate.rearrange("(c p) s -> p c s", p=P)
         bank_of = {}
 
         def load_words(o):
@@ -154,9 +154,9 @@ def tile_moe_two_mlp_relu_kernel(
         def load_w2(e, c0, c1):
             nc.sync.dma_start(w2_piece(e, c0, c1), w2[e, :, c0 * P : c1 * P].rearrange("(p j) n -> p j n", j=PACK))
 
-        def load_gate(pair, c0, c1):
-            cols = slice(pair * PAIR, (pair + 1) * PAIR)
-            nc.sync.dma_start(gate_sb[:, c0:c1, cols], gate_rows[:, c0:c1, cols])
+        def load_gate(pair0, pair1):
+            cols = slice(pair0 * PAIR, pair1 * PAIR)
+            nc.sync.dma_start(gate_sb[:, cols], gate[0:P, cols])
 
         def quantize_w2(e, c0, c1, on_scalar):
             grouped = w2_bf16[e % W2_DEPTH]
@@ -194,7 +194,7 @@ def tile_moe_two_mlp_relu_kernel(
             nc.vector.tensor_tensor(
                 out_sb[c][:].indirect(dst_list[:, pair * columns : (pair + 1) * columns]),
                 y,
-                gate_sb[:, c, pair * PAIR : (pair + 1) * PAIR],
+                gate_sb[:, pair * PAIR : (pair + 1) * PAIR],
                 MULT,
             )
 
@@ -225,8 +225,8 @@ def tile_moe_two_mlp_relu_kernel(
             load_w1(u)
             if u in STREAM_PIECES:
                 load_w2(*STREAM_PIECES[u][:3])
-            if u in STREAM_GATES:
-                load_gate(*STREAM_GATES[u])
+            if u == GATE_UNIT:
+                load_gate(0, PAIRS - 1)
             quantize_w1(u)
             if u % PASSES == PASSES - 1:
                 first_matmuls(u // PASSES)
@@ -242,10 +242,9 @@ def tile_moe_two_mlp_relu_kernel(
         load_w2(7, 0, 2)
         load_w2(7, 2, 3)
         load_w2(6, 1, 3)
-        load_gate(3, 0, 3)
+        load_gate(PAIRS - 1, PAIRS)
         load_w2(4, 2, 3)
         load_w2(5, 2, 3)
-        load_gate(2, 2, 3)
         quantize_w2(6, 0, 1, True)
         second_matmuls(6, 0, 1)
         quantize_w2(7, 0, 2, True)

@@ -1,11 +1,12 @@
 from contextlib import ExitStack
 
 import concourse.mybir as mybir
+from concourse.masks import make_identity
 
 K, T, E, C, H, N = 1024, 2048, 8, 128, 512, 384
 S = E * C
 FLOPS = 2 * S * (K * H + H * N)
-BYTES = K * T + K // 32 * T + 4 * (E * H * (K + N) + 128 * S + N * T) + 2 * 2 * 8 * S
+BYTES = K * T + K // 32 * T + 4 * (E * H * (K + N) + S + N * T) + 2 * 2 * 8 * S
 
 F32 = mybir.dt.float32
 BF16 = mybir.dt.bfloat16
@@ -42,7 +43,6 @@ VECTOR_SHARE = [0, 0] + [16, 32] * 5 + [16, 64, 48, 64]
 LAST_SCALAR_SHARE = 16
 
 STREAM_PIECES = {2 * e + 2: (e, 0, ROW_TILES if e < 4 else 2, e == 5) for e in range(6)}
-GATE_UNIT = 3
 STREAM_SCATTERS = {
     **{4 * pair + 5 + c: (pair, c) for pair in range(2) for c in range(ROW_TILES)},
     13: (2, 0),
@@ -67,6 +67,8 @@ def tile_moe_two_mlp_relu_kernel(
         tok_scales = keep.tile([P, T], U8, name="tok_scales")
         slot_words = ring("slot_words", PASSES, [P, S], U32)
         slot_scales = keep.tile([P, S], U8, name="slot_scales", align_bytes=64)
+        gate_row = keep.tile([P, S // P], F32, name="gate_row")
+        identity = keep.tile([P, P], F32, name="identity")
         gate_sb = keep.tile([P, S], F32, name="gate_sb")
         out_sb = ring("out_sb", ROW_TILES, [P, T], F32)
         w1_raw = ring("w1_raw", W1_RAW_DEPTH, [P, PACK, H], F32)
@@ -154,9 +156,14 @@ def tile_moe_two_mlp_relu_kernel(
         def load_w2(e, c0, c1):
             nc.sync.dma_start(w2_piece(e, c0, c1), w2[e, :, c0 * P : c1 * P].rearrange("(p j) n -> p j n", j=PACK))
 
-        def load_gate(pair0, pair1):
-            cols = slice(pair0 * PAIR, pair1 * PAIR)
-            nc.sync.dma_start(gate_sb[:, cols], gate[0:P, cols])
+        def spread_gate():
+            by_slot = gate_sb[:].rearrange("p (n q) -> p n q", n=P)
+            for half in range(2):
+                bank = acc1[1 + half]
+                for q in range(PACK):
+                    column = half * PACK + q
+                    nc.tensor.transpose(bank[:, q, :], gate_row[:, column : column + 1].to_broadcast([P, P]), identity[:])
+                nc.scalar.copy(by_slot[:, :, half * PACK : (half + 1) * PACK], bank[:].rearrange("p q n -> p n q"))
 
         def quantize_w2(e, c0, c1, on_scalar):
             grouped = w2_bf16[e % W2_DEPTH]
@@ -210,11 +217,14 @@ def tile_moe_two_mlp_relu_kernel(
         load_w1(0)
         load_scales((0, 1))
         load_words(1)
+        nc.sync.dma_start(gate_row[:], gate[0].rearrange("(n q) -> n q", n=P))
         load_scales((2, 3))
         load_w1(1)
         nc.sync.dma_start(dst_list[:], dst)
         nc.vector.tensor_copy(slot_words[0][:], tok_words[0][:].bitcast(U32).indirect(src_list[:]))
         quantize_w1(0)
+        make_identity(nc, identity[:])
+        spread_gate()
         nc.vector.tensor_copy(slot_words[1][:], tok_words[1][:].bitcast(U32).indirect(src_list[:]))
         nc.vector.tensor_copy(slot_scales[:], tok_scales[:].indirect(src_list[:]))
         quantize_w1(1)
@@ -225,8 +235,6 @@ def tile_moe_two_mlp_relu_kernel(
             load_w1(u)
             if u in STREAM_PIECES:
                 load_w2(*STREAM_PIECES[u][:3])
-            if u == GATE_UNIT:
-                load_gate(0, PAIRS - 1)
             quantize_w1(u)
             if u % PASSES == PASSES - 1:
                 first_matmuls(u // PASSES)
@@ -242,7 +250,6 @@ def tile_moe_two_mlp_relu_kernel(
         load_w2(7, 0, 2)
         load_w2(7, 2, 3)
         load_w2(6, 1, 3)
-        load_gate(PAIRS - 1, PAIRS)
         load_w2(4, 2, 3)
         load_w2(5, 2, 3)
         quantize_w2(6, 0, 1, True)

@@ -18,6 +18,7 @@ FP8X4 = mybir.dt.float8_e4m3fn_x4
 COPY = mybir.ActivationFunctionType.Copy
 RELU = mybir.ActivationFunctionType.Relu
 MULT = mybir.AluOpType.mult
+ADD = mybir.AluOpType.add
 
 P = 128
 PACK = 4
@@ -26,8 +27,6 @@ PASSES = K // K_PASS
 UNITS = E * PASSES
 LAST_UNIT = UNITS - 1
 ROW_TILES = N // P
-PAIR = 2 * C
-PAIRS = E // 2
 LIST_ROWS = 16
 QUADRANT = 32
 SCALE_ROWS = 4
@@ -36,18 +35,14 @@ W1_RAW_DEPTH = 9
 W1_BF16_DEPTH = 4
 W1_CODE_DEPTH = 6
 W2_DEPTH = 4
-ACC1_BANKS = 3
-ACC2_BANKS = 5
 
-VECTOR_SHARE = [0, 0] + [16, 32] * 5 + [16, 64, 48, 64]
-LAST_SCALAR_SHARE = 16
+GROUP_STARTS = [(0, 1, 3, 5, 7), (0, 1, 2, 4, 6), (0, 1, 3, 5)]
+GROUPS = [list(zip(starts, starts[1:] + (E,))) for starts in GROUP_STARTS]
+WIDEST = 3 * C
 
-STREAM_PIECES = {2 * e + 2: (e, 0, ROW_TILES if e < 4 else 2, e == 5) for e in range(6)}
-STREAM_SCATTERS = {
-    **{4 * pair + 5 + c: (pair, c) for pair in range(2) for c in range(ROW_TILES)},
-    13: (2, 0),
-    LAST_UNIT: (2, 1),
-}
+FIRST_SHARES = (0, 64)
+STREAM_SHARES = (40, 56, 64, 72)
+LAST_SHARES = (64, 84)
 
 
 def tile_moe_two_mlp_relu_kernel(
@@ -75,17 +70,18 @@ def tile_moe_two_mlp_relu_kernel(
         w1_bf16 = ring("w1_bf16", W1_BF16_DEPTH, [P, PACK, P, PACK], BF16)
         w1_codes = ring("w1_codes", W1_CODE_DEPTH, [P, H], U32)
         w1_scales = ring("w1_scales", W1_CODE_DEPTH, [P, H], U8)
-        w2_raw = ring("w2_raw", W2_DEPTH, [P, PACK * N], F32)
+        w2_raw = ring("w2_raw", W2_DEPTH, [P, PACK, N], F32)
         w2_bf16 = ring("w2_bf16", W2_DEPTH, [P, N, PACK], BF16)
         w2_codes = ring("w2_codes", W2_DEPTH, [P, N], U32)
         w2_scales = ring("w2_scales", W2_DEPTH, [P, N], U8)
         h_codes = ring("h_codes", E, [P, C], U32)
         h_scales = ring("h_scales", E, [P, C], U8)
         h_last = keep.tile([P, C * PACK], BF16, name="h_last", align_bytes=64)
-        y_last = ring("y_last", ROW_TILES + 1, [P, PAIR], F32)
-        acc1 = [psum.tile([P, PACK, C], F32, name=f"acc1_{i}") for i in range(ACC1_BANKS)]
-        acc2 = [psum.tile([P, PAIR], F32, name=f"acc2_{i}") for i in range(ACC2_BANKS)]
-        bank_of = {}
+        y_one = ring("y_one", ROW_TILES, [P, C], F32)
+        y_last = ring("y_last", ROW_TILES - 1, [P, WIDEST], F32)
+        zeros = keep.tile([P, C], F32, name="zeros")
+        acc1 = [psum.tile([P, PACK, C], F32, name=f"acc1_{i}") for i in range(2)]
+        acc2 = [[psum.tile([P, WIDEST], F32, name=f"acc2_{c}_{i}") for i in range(2)] for c in range(ROW_TILES)]
 
         def load_words(o):
             nc.sync.dma_start(tok_words[o][:], x_words[o].rearrange("p t r -> p (t r)").bitcast(I32))
@@ -101,23 +97,21 @@ def tile_moe_two_mlp_relu_kernel(
         def load_w1(u):
             e, o = divmod(u, PASSES)
             rows = w1[e, o * K_PASS : (o + 1) * K_PASS, :].rearrange("(p j) i -> p j i", j=PACK)
-            parts = 2 if u == LAST_UNIT else 1
-            for a in range(parts):
-                cols = slice(a * H // parts, (a + 1) * H // parts)
-                nc.sync.dma_start(w1_raw[u % W1_RAW_DEPTH][:, :, cols], rows[:, :, cols])
+            nc.sync.dma_start(w1_raw[u % W1_RAW_DEPTH][:], rows)
 
         def quantize_w1(u):
             grouped = w1_bf16[u % W1_BF16_DEPTH]
             source = w1_raw[u % W1_RAW_DEPTH][:].rearrange("p j (m t) -> p m j t", t=PACK)
             target = grouped[:].rearrange("p t m j -> p m j t")
-            vector_from = P - VECTOR_SHARE[u]
-            vector_to = P - LAST_SCALAR_SHARE if u == LAST_UNIT else P
-            nc.scalar.activation(target[:, 0:vector_from], source[:, 0:vector_from], COPY)
-            if vector_from < vector_to:
-                nc.vector.tensor_copy(target[:, vector_from:vector_to], source[:, vector_from:vector_to])
-            if vector_to < P:
-                nc.scalar.activation(target[:, vector_to:P], source[:, vector_to:P], COPY)
-            parts = 2 if u == LAST_UNIT else 1
+            share = STREAM_SHARES[u % len(STREAM_SHARES)]
+            if u < PASSES:
+                share = FIRST_SHARES[u]
+            elif u >= UNITS - PASSES:
+                share = LAST_SHARES[u % PASSES]
+            nc.scalar.activation(target[:, 0 : P - share], source[:, 0 : P - share], COPY)
+            if share:
+                nc.vector.tensor_copy(target[:, P - share : P], source[:, P - share : P])
+            parts = PACK if u == LAST_UNIT else 1
             width = H // parts
             for a in range(parts):
                 nc.vector.quantize_mx(
@@ -133,7 +127,7 @@ def tile_moe_two_mlp_relu_kernel(
                 for o in range(PASSES):
                     u = e * PASSES + o
                     nc.tensor.matmul_mx(
-                        out=acc1[e % ACC1_BANKS][:, t, :],
+                        out=acc1[e % 2][:, t, :],
                         lhsT=w1_codes[u % W1_CODE_DEPTH][:, cols].bitcast(FP8X4),
                         lhsT_scale=w1_scales[u % W1_CODE_DEPTH][:, cols],
                         rhs=slot_words[o][:, slots].bitcast(FP8X4),
@@ -145,34 +139,28 @@ def tile_moe_two_mlp_relu_kernel(
         def quantize_h(e, h_bf16):
             nc.scalar.activation(
                 h_bf16.rearrange("p (s t) -> p s t", t=PACK),
-                acc1[e % ACC1_BANKS][:].rearrange("p t s -> p s t"),
+                acc1[e % 2][:].rearrange("p t s -> p s t"),
                 RELU,
             )
             nc.vector.quantize_mx(out=h_codes[e][:].bitcast(FP8X4), scales=h_scales[e][:], in_=h_bf16)
 
-        def w2_piece(e, c0, c1):
-            return w2_raw[e % W2_DEPTH][:, c0 * P * PACK : c1 * P * PACK].rearrange("p (j n) -> p j n", j=PACK)
-
-        def load_w2(e, c0, c1):
-            nc.sync.dma_start(w2_piece(e, c0, c1), w2[e, :, c0 * P : c1 * P].rearrange("(p j) n -> p j n", j=PACK))
+        def load_w2(e):
+            nc.sync.dma_start(w2_raw[e % W2_DEPTH][:], w2[e].rearrange("(p j) n -> p j n", j=PACK))
 
         def spread_gate():
             by_slot = gate_sb[:].rearrange("p (n q) -> p n q", n=P)
             for half in range(2):
-                bank = acc1[1 + half]
+                bank = acc1[half]
                 for q in range(PACK):
                     column = half * PACK + q
                     nc.tensor.transpose(bank[:, q, :], gate_row[:, column : column + 1].to_broadcast([P, P]), identity[:])
                 nc.scalar.copy(by_slot[:, :, half * PACK : (half + 1) * PACK], bank[:].rearrange("p q n -> p n q"))
 
-        def quantize_w2(e, c0, c1, on_scalar):
+        def quantize_w2(e, c0, c1):
             grouped = w2_bf16[e % W2_DEPTH]
             target = grouped[:, c0 * P : c1 * P, :].rearrange("p (g n) j -> p g j n", n=4)
-            source = w2_piece(e, c0, c1).rearrange("p j (g n) -> p g j n", n=4)
-            if on_scalar:
-                nc.scalar.activation(target, source, COPY)
-            else:
-                nc.vector.tensor_copy(target, source)
+            source = w2_raw[e % W2_DEPTH][:, :, c0 * P : c1 * P].rearrange("p j (g n) -> p g j n", n=4)
+            nc.scalar.activation(target, source, COPY)
             for c in range(c0, c1, 2):
                 cols = slice(c * P, min(c + 2, c1) * P)
                 nc.vector.quantize_mx(
@@ -181,12 +169,16 @@ def tile_moe_two_mlp_relu_kernel(
                     in_=grouped[:, cols, :].rearrange("p n j -> p (n j)"),
                 )
 
+        def group_of(c, e):
+            return max(g for g, (first, end) in enumerate(GROUPS[c]) if first <= e)
+
         def second_matmuls(e, c0, c1):
             for c in range(c0, c1):
-                bank = bank_of.setdefault((e // 2, c), len(bank_of) % ACC2_BANKS)
+                g = group_of(c, e)
+                place = e - GROUPS[c][g][0]
                 cols = slice(c * P, (c + 1) * P)
                 nc.tensor.matmul_mx(
-                    out=acc2[bank][:, (e % 2) * C : (e % 2 + 1) * C],
+                    out=acc2[c][g % 2][:, place * C : (place + 1) * C],
                     lhsT=w2_codes[e % W2_DEPTH][:, cols].bitcast(FP8X4),
                     lhsT_scale=w2_scales[e % W2_DEPTH][:, cols],
                     rhs=h_codes[e][:].bitcast(FP8X4),
@@ -195,79 +187,81 @@ def tile_moe_two_mlp_relu_kernel(
                     stop=True,
                 )
 
-        def scatter(pair, c, y):
-            columns = PAIR // LIST_ROWS
-            nc.scalar.copy(y, acc2[bank_of[(pair, c)]][:])
-            nc.vector.tensor_tensor(
-                out_sb[c][:].indirect(dst_list[:, pair * columns : (pair + 1) * columns]),
-                y,
-                gate_sb[:, pair * PAIR : (pair + 1) * PAIR],
-                MULT,
-            )
+        def scatter(c, g, staging):
+            first, end = GROUPS[c][g]
+            width = (end - first) * C
+            sums = acc2[c][g % 2][:, 0:width]
+            y = staging[:, 0:width]
+            gates = gate_sb[:, first * C : end * C]
+            places = out_sb[c][:].indirect(dst_list[:, first * C // LIST_ROWS : end * C // LIST_ROWS])
+            if width == C:
+                nc.vector.tensor_tensor(y, sums, gates, MULT)
+                nc.vector.tensor_tensor(places, y, zeros[:], ADD)
+            else:
+                nc.scalar.copy(y, sums)
+                nc.vector.tensor_tensor(places, y, gates, MULT)
+
+        def ending(e, alone):
+            groups = [(c, group_of(c, e)) for c in range(ROW_TILES)]
+            return [(c, g) for c, g in groups if GROUPS[c][g][1] == e + 1 and (GROUPS[c][g][0] == e) == alone]
 
         def store(c):
             nc.sync.dma_start(out[c * P : (c + 1) * P, :], out_sb[c][:])
 
         nc.vector.memset(tok_scales[:].bitcast(I32), 0)
+        nc.vector.memset(zeros[:], 0.0)
         for c in range(ROW_TILES):
             nc.vector.memset(out_sb[c][:], 0.0)
 
         load_words(0)
         nc.sync.dma_start(src_list[:], offs)
-        load_w1(0)
         load_scales((0, 1))
         load_words(1)
         nc.sync.dma_start(gate_row[:], gate[0].rearrange("(n q) -> n q", n=P))
         load_scales((2, 3))
-        load_w1(1)
-        nc.sync.dma_start(dst_list[:], dst)
-        nc.vector.tensor_copy(slot_words[0][:], tok_words[0][:].bitcast(U32).indirect(src_list[:]))
-        quantize_w1(0)
+        for o in range(PASSES):
+            nc.vector.tensor_copy(slot_words[o][:], tok_words[o][:].bitcast(U32).indirect(src_list[:]))
+        nc.vector.tensor_copy(slot_scales[:], tok_scales[:].indirect(src_list[:]))
         make_identity(nc, identity[:])
         spread_gate()
-        nc.vector.tensor_copy(slot_words[1][:], tok_words[1][:].bitcast(U32).indirect(src_list[:]))
-        nc.vector.tensor_copy(slot_scales[:], tok_scales[:].indirect(src_list[:]))
-        quantize_w1(1)
-        first_matmuls(0)
 
-        for u in range(PASSES, UNITS):
-            staging = w1_raw[u % W1_RAW_DEPTH]
-            load_w1(u)
-            if u in STREAM_PIECES:
-                load_w2(*STREAM_PIECES[u][:3])
-            quantize_w1(u)
-            if u % PASSES == PASSES - 1:
-                first_matmuls(u // PASSES)
-            else:
-                quantize_h(u // PASSES - 1, staging[:, 0, 0 : H // 2].bitcast(BF16))
-            if u in STREAM_SCATTERS:
-                scatter(*STREAM_SCATTERS[u], staging[:, 1, 0:PAIR])
-            if u in STREAM_PIECES:
-                quantize_w2(*STREAM_PIECES[u])
-                second_matmuls(*STREAM_PIECES[u][:3])
+        for e in range(E):
+            unit_a, unit_b = PASSES * e, PASSES * e + 1
+            load_w1(unit_a)
+            load_w1(unit_b)
+            if e == 0:
+                nc.sync.dma_start(dst_list[:], dst)
+            load_w2(e)
+            quantize_w1(unit_a)
+            due = []
+            if e > 0:
+                quantize_h(e - 1, w1_raw[unit_a % W1_RAW_DEPTH][:, 0, 0 : H // 2].bitcast(BF16))
+                second_matmuls(e - 1, 0, ROW_TILES)
+                if e > 1:
+                    for c, g in ending(e - 1, True):
+                        scatter(c, g, y_one[c])
+                due = ending(e - 1, False)
+            quantize_w1(unit_b)
+            first_matmuls(e)
+            if e == 1:
+                spare = w1_bf16[unit_b % W1_BF16_DEPTH][:].rearrange("p t m j -> p (t m j)").bitcast(F32)
+                for c, g in ending(0, True):
+                    scatter(c, g, spare[:, c * C : (c + 1) * C])
+            for c, g in due[:1]:
+                scatter(c, g, w1_raw[unit_b % W1_RAW_DEPTH][:, 1, :])
+            if e < E - 1:
+                quantize_w2(e, 0, ROW_TILES)
+            for c, g in due[1:]:
+                scatter(c, g, w2_raw[e % W2_DEPTH][:, 0, :])
 
-        load_w2(6, 0, 1)
-        load_w2(7, 0, 2)
-        load_w2(7, 2, 3)
-        load_w2(6, 1, 3)
-        load_w2(4, 2, 3)
-        load_w2(5, 2, 3)
-        quantize_w2(6, 0, 1, True)
-        second_matmuls(6, 0, 1)
-        quantize_w2(7, 0, 2, True)
-        quantize_h(7, h_last[:])
-        second_matmuls(7, 0, 2)
-        quantize_w2(7, 2, 3, True)
-        second_matmuls(7, 2, 3)
-        quantize_w2(6, 1, 3, False)
-        second_matmuls(6, 1, 3)
-        scatter(3, 0, y_last[0][:])
+        last = E - 1
+        quantize_h(last, h_last[:])
+        quantize_w2(last, 0, 1)
+        second_matmuls(last, 0, 1)
+        scatter(0, group_of(0, last), y_one[0])
         store(0)
-        for e in (4, 5):
-            quantize_w2(e, 2, 3, True)
-            second_matmuls(e, 2, 3)
-        scatter(3, 1, y_last[1][:])
-        store(1)
-        scatter(3, 2, y_last[2][:])
-        scatter(2, 2, y_last[3][:])
-        store(2)
+        quantize_w2(last, 1, ROW_TILES)
+        second_matmuls(last, 1, ROW_TILES)
+        for c in range(1, ROW_TILES):
+            scatter(c, group_of(c, last), y_last[c - 1])
+            store(c)

@@ -32,7 +32,7 @@ QUADRANT = 32
 SCALE_ROWS = 4
 
 W1_RAW_DEPTH = 9
-W1_BF16_DEPTH = 4
+W1_BF16_DEPTH = 5
 W1_CODE_DEPTH = 6
 W2_DEPTH = 4
 
@@ -40,9 +40,9 @@ GROUP_STARTS = [(0, 1, 3, 5, 7), (0, 1, 2, 4, 6), (0, 1, 3, 5)]
 GROUPS = [list(zip(starts, starts[1:] + (E,))) for starts in GROUP_STARTS]
 WIDEST = 3 * C
 
-FIRST_SHARES = (0, 64)
-STREAM_SHARES = (40, 56, 64, 72)
-LAST_SHARES = (64, 84)
+FIRST_SHARES = (0, 32)
+STREAM_SHARES = (40, 64, 64, 72)
+LAST_SHARES = (64, 72)
 
 
 def tile_moe_two_mlp_relu_kernel(
@@ -78,7 +78,8 @@ def tile_moe_two_mlp_relu_kernel(
         h_scales = ring("h_scales", E, [P, C], U8)
         h_last = keep.tile([P, C * PACK], BF16, name="h_last", align_bytes=64)
         y_one = ring("y_one", ROW_TILES, [P, C], F32)
-        y_last = ring("y_last", ROW_TILES - 1, [P, WIDEST], F32)
+        y_last = ring("y_last", ROW_TILES, [P, WIDEST], F32)
+        y_second = keep.tile([P, WIDEST], F32, name="y_second")
         zeros = keep.tile([P, C], F32, name="zeros")
         acc1 = [psum.tile([P, PACK, C], F32, name=f"acc1_{i}") for i in range(2)]
         acc2 = [[psum.tile([P, WIDEST], F32, name=f"acc2_{c}_{i}") for i in range(2)] for c in range(ROW_TILES)]
@@ -252,16 +253,13 @@ def tile_moe_two_mlp_relu_kernel(
             if e < E - 1:
                 quantize_w2(e, 0, ROW_TILES)
             for c, g in due[1:]:
-                scatter(c, g, w2_raw[e % W2_DEPTH][:, 0, :])
+                scatter(c, g, y_second)
 
         last = E - 1
-        quantize_h(last, h_last[:])
-        quantize_w2(last, 0, 1)
-        second_matmuls(last, 0, 1)
-        scatter(0, group_of(0, last), y_one[0])
-        store(0)
-        quantize_w2(last, 1, ROW_TILES)
-        second_matmuls(last, 1, ROW_TILES)
-        for c in range(1, ROW_TILES):
-            scatter(c, group_of(c, last), y_last[c - 1])
+        for c in range(ROW_TILES):
+            quantize_w2(last, c, c + 1)
+            if c == 0:
+                quantize_h(last, h_last[:])
+            second_matmuls(last, c, c + 1)
+            scatter(c, group_of(c, last), y_last[c])
             store(c)

@@ -31,18 +31,15 @@ LIST_ROWS = 16
 QUADRANT = 32
 SCALE_ROWS = 4
 
-W1_RAW_DEPTH = 9
-W1_BF16_DEPTH = 5
-W1_CODE_DEPTH = 6
+W1_RAW_DEPTH = 4
+W1_BF16_DEPTH = 2
+W1_CODE_DEPTH = 3
 W2_DEPTH = 4
+LATE = 2
 
-GROUP_STARTS = [(0, 1, 3, 5, 7), (0, 1, 2, 4, 6), (0, 1, 3, 5)]
-GROUPS = [list(zip(starts, starts[1:] + (E,))) for starts in GROUP_STARTS]
-WIDEST = 3 * C
-
-FIRST_SHARES = (0, 32)
-STREAM_SHARES = (40, 64, 64, 72)
-LAST_SHARES = (64, 72)
+SHARES = (56, 48, 48, 48, 48, 48, 48, 8)
+MORE = (0, 0, 0, 0, 0, 0, 0, 88)
+PARTS = 2
 
 
 def tile_moe_two_mlp_relu_kernel(
@@ -66,23 +63,24 @@ def tile_moe_two_mlp_relu_kernel(
         identity = keep.tile([P, P], F32, name="identity")
         gate_sb = keep.tile([P, S], F32, name="gate_sb")
         out_sb = ring("out_sb", ROW_TILES, [P, T], F32)
-        w1_raw = ring("w1_raw", W1_RAW_DEPTH, [P, PACK, H], F32)
-        w1_bf16 = ring("w1_bf16", W1_BF16_DEPTH, [P, PACK, P, PACK], BF16)
-        w1_codes = ring("w1_codes", W1_CODE_DEPTH, [P, H], U32)
-        w1_scales = ring("w1_scales", W1_CODE_DEPTH, [P, H], U8)
+        w1_raw = ring("w1_raw", W1_RAW_DEPTH, [P, PASSES * PACK * H], F32)
+        w1_bf16 = ring("w1_bf16", W1_BF16_DEPTH, [P, PASSES * H * PACK], BF16)
+        w1_codes = ring("w1_codes", W1_CODE_DEPTH * PASSES, [P, H], U32)
+        w1_scales = ring("w1_scales", W1_CODE_DEPTH * PASSES, [P, H], U8)
         w2_raw = ring("w2_raw", W2_DEPTH, [P, PACK, N], F32)
         w2_bf16 = ring("w2_bf16", W2_DEPTH, [P, N, PACK], BF16)
         w2_codes = ring("w2_codes", W2_DEPTH, [P, N], U32)
         w2_scales = ring("w2_scales", W2_DEPTH, [P, N], U8)
+        h_bf16 = ring("h_bf16", 2, [P, C * PACK], BF16)
         h_codes = ring("h_codes", E, [P, C], U32)
         h_scales = ring("h_scales", E, [P, C], U8)
-        h_last = keep.tile([P, C * PACK], BF16, name="h_last", align_bytes=64)
-        y_one = ring("y_one", ROW_TILES, [P, C], F32)
-        y_last = ring("y_last", ROW_TILES, [P, WIDEST], F32)
-        y_second = keep.tile([P, WIDEST], F32, name="y_second")
+        y_one = ring("y_one", LATE, [P, C], F32)
+        y_last = ring("y_last", ROW_TILES, [P, 3 * C], F32)
         zeros = keep.tile([P, C], F32, name="zeros")
         acc1 = [psum.tile([P, PACK, C], F32, name=f"acc1_{i}") for i in range(2)]
-        acc2 = [[psum.tile([P, WIDEST], F32, name=f"acc2_{c}_{i}") for i in range(2)] for c in range(ROW_TILES)]
+        acc2 = [psum.tile([P, ROW_TILES, C], F32, name=f"acc2_{i}") for i in range(2)]
+        acc_one = [psum.tile([P, C], F32, name=f"acc_one{i}") for i in range(LATE)]
+        acc_last = [None] + [psum.tile([P, 3 * C], F32, name=f"acc_last{c}") for c in range(1, ROW_TILES)]
 
         def load_words(o):
             nc.sync.dma_start(tok_words[o][:], x_words[o].rearrange("p t r -> p (t r)").bitcast(I32))
@@ -95,30 +93,31 @@ def tile_moe_two_mlp_relu_kernel(
                         x_scales[o, r::SCALE_ROWS, :].bitcast(I32),
                     )
 
-        def load_w1(u):
-            e, o = divmod(u, PASSES)
-            rows = w1[e, o * K_PASS : (o + 1) * K_PASS, :].rearrange("(p j) i -> p j i", j=PACK)
-            nc.sync.dma_start(w1_raw[u % W1_RAW_DEPTH][:], rows)
+        def load_w1(e, o):
+            rows = w1[e, o * K_PASS : (o + 1) * K_PASS, :].rearrange("(p j) i -> p (j i)", j=PACK)
+            nc.sync.dma_start(w1_raw[e % W1_RAW_DEPTH][:, o * PACK * H : (o + 1) * PACK * H], rows)
 
-        def quantize_w1(u):
-            grouped = w1_bf16[u % W1_BF16_DEPTH]
-            source = w1_raw[u % W1_RAW_DEPTH][:].rearrange("p j (m t) -> p m j t", t=PACK)
-            target = grouped[:].rearrange("p t m j -> p m j t")
-            share = STREAM_SHARES[u % len(STREAM_SHARES)]
-            if u < PASSES:
-                share = FIRST_SHARES[u]
-            elif u >= UNITS - PASSES:
-                share = LAST_SHARES[u % PASSES]
-            nc.scalar.activation(target[:, 0 : P - share], source[:, 0 : P - share], COPY)
-            if share:
-                nc.vector.tensor_copy(target[:, P - share : P], source[:, P - share : P])
-            parts = PACK if u == LAST_UNIT else 1
+        def round_w1(e):
+            source = w1_raw[e % W1_RAW_DEPTH][:].rearrange("p (o j m t) -> p o m j t", o=PASSES, j=PACK, t=PACK)
+            target = w1_bf16[e % W1_BF16_DEPTH][:].rearrange("p (o t m j) -> p o m j t", o=PASSES, j=PACK, t=PACK)
+            cut = P - SHARES[e]
+            cut_b = cut - MORE[e]
+            nc.scalar.activation(target[:, 0, 0:cut], source[:, 0, 0:cut], COPY)
+            nc.scalar.activation(target[:, 1, 0:cut_b], source[:, 1, 0:cut_b], COPY)
+            nc.vector.tensor_copy(target[:, :, cut:P], source[:, :, cut:P])
+            if cut_b < cut:
+                nc.vector.tensor_copy(target[:, 1, cut_b:cut], source[:, 1, cut_b:cut])
+
+        def quantize_w1(e, o):
+            u = (e * PASSES + o) % (W1_CODE_DEPTH * PASSES)
+            parts = 1 if o == 0 else (PACK if e == E - 1 else PARTS)
             width = H // parts
             for a in range(parts):
+                first = o * H + a * width
                 nc.vector.quantize_mx(
-                    out=w1_codes[u % W1_CODE_DEPTH][:, a * width : (a + 1) * width].bitcast(FP8X4),
-                    scales=w1_scales[u % W1_CODE_DEPTH][:, a * width : (a + 1) * width],
-                    in_=grouped[:].rearrange("p t m j -> p (t m j)")[:, a * width * PACK : (a + 1) * width * PACK],
+                    out=w1_codes[u][:, a * width : (a + 1) * width].bitcast(FP8X4),
+                    scales=w1_scales[u][:, a * width : (a + 1) * width],
+                    in_=w1_bf16[e % W1_BF16_DEPTH][:, first * PACK : (first + width) * PACK],
                 )
 
         def first_matmuls(e):
@@ -126,24 +125,27 @@ def tile_moe_two_mlp_relu_kernel(
             for t in range(PACK):
                 cols = slice(t * P, (t + 1) * P)
                 for o in range(PASSES):
-                    u = e * PASSES + o
+                    u = (e * PASSES + o) % (W1_CODE_DEPTH * PASSES)
                     nc.tensor.matmul_mx(
                         out=acc1[e % 2][:, t, :],
-                        lhsT=w1_codes[u % W1_CODE_DEPTH][:, cols].bitcast(FP8X4),
-                        lhsT_scale=w1_scales[u % W1_CODE_DEPTH][:, cols],
+                        lhsT=w1_codes[u][:, cols].bitcast(FP8X4),
+                        lhsT_scale=w1_scales[u][:, cols],
                         rhs=slot_words[o][:, slots].bitcast(FP8X4),
                         rhs_scale=slot_scales[SCALE_ROWS * o : P, slots],
                         start=(o == 0),
                         stop=(o == PASSES - 1),
                     )
 
-        def quantize_h(e, h_bf16):
+        def relu_h(e):
+            h = h_bf16[e % 2]
             nc.scalar.activation(
-                h_bf16.rearrange("p (s t) -> p s t", t=PACK),
+                h[:].rearrange("p (s t) -> p s t", t=PACK),
                 acc1[e % 2][:].rearrange("p t s -> p s t"),
                 RELU,
             )
-            nc.vector.quantize_mx(out=h_codes[e][:].bitcast(FP8X4), scales=h_scales[e][:], in_=h_bf16)
+
+        def quantize_h(e):
+            nc.vector.quantize_mx(out=h_codes[e][:].bitcast(FP8X4), scales=h_scales[e][:], in_=h_bf16[e % 2][:])
 
         def load_w2(e):
             nc.sync.dma_start(w2_raw[e % W2_DEPTH][:], w2[e].rearrange("(p j) n -> p j n", j=PACK))
@@ -157,11 +159,14 @@ def tile_moe_two_mlp_relu_kernel(
                     nc.tensor.transpose(bank[:, q, :], gate_row[:, column : column + 1].to_broadcast([P, P]), identity[:])
                 nc.scalar.copy(by_slot[:, :, half * PACK : (half + 1) * PACK], bank[:].rearrange("p q n -> p n q"))
 
-        def quantize_w2(e, c0, c1):
+        def quantize_w2(e, c0, c1, on_vector=False):
             grouped = w2_bf16[e % W2_DEPTH]
             target = grouped[:, c0 * P : c1 * P, :].rearrange("p (g n) j -> p g j n", n=4)
             source = w2_raw[e % W2_DEPTH][:, :, c0 * P : c1 * P].rearrange("p j (g n) -> p g j n", n=4)
-            nc.scalar.activation(target, source, COPY)
+            if on_vector:
+                nc.vector.tensor_copy(target, source)
+            else:
+                nc.scalar.activation(target, source, COPY)
             for c in range(c0, c1, 2):
                 cols = slice(c * P, min(c + 2, c1) * P)
                 nc.vector.quantize_mx(
@@ -170,41 +175,29 @@ def tile_moe_two_mlp_relu_kernel(
                     in_=grouped[:, cols, :].rearrange("p n j -> p (n j)"),
                 )
 
-        def group_of(c, e):
-            return max(g for g, (first, end) in enumerate(GROUPS[c]) if first <= e)
+        def second_matmul(e, c, sums):
+            cols = slice(c * P, (c + 1) * P)
+            nc.tensor.matmul_mx(
+                out=sums,
+                lhsT=w2_codes[e % W2_DEPTH][:, cols].bitcast(FP8X4),
+                lhsT_scale=w2_scales[e % W2_DEPTH][:, cols],
+                rhs=h_codes[e][:].bitcast(FP8X4),
+                rhs_scale=h_scales[e][:],
+                start=True,
+                stop=True,
+            )
 
-        def second_matmuls(e, c0, c1):
-            for c in range(c0, c1):
-                g = group_of(c, e)
-                place = e - GROUPS[c][g][0]
-                cols = slice(c * P, (c + 1) * P)
-                nc.tensor.matmul_mx(
-                    out=acc2[c][g % 2][:, place * C : (place + 1) * C],
-                    lhsT=w2_codes[e % W2_DEPTH][:, cols].bitcast(FP8X4),
-                    lhsT_scale=w2_scales[e % W2_DEPTH][:, cols],
-                    rhs=h_codes[e][:].bitcast(FP8X4),
-                    rhs_scale=h_scales[e][:],
-                    start=True,
-                    stop=True,
-                )
+        def places(c, first, end):
+            return out_sb[c][:].indirect(dst_list[:, first * C // LIST_ROWS : end * C // LIST_ROWS])
 
-        def scatter(c, g, staging):
-            first, end = GROUPS[c][g]
-            width = (end - first) * C
-            sums = acc2[c][g % 2][:, 0:width]
-            y = staging[:, 0:width]
-            gates = gate_sb[:, first * C : end * C]
-            places = out_sb[c][:].indirect(dst_list[:, first * C // LIST_ROWS : end * C // LIST_ROWS])
-            if width == C:
-                nc.vector.tensor_tensor(y, sums, gates, MULT)
-                nc.vector.tensor_tensor(places, y, zeros[:], ADD)
-            else:
-                nc.scalar.copy(y, sums)
-                nc.vector.tensor_tensor(places, y, gates, MULT)
+        def scatter_one(e, c, y):
+            nc.vector.tensor_tensor(places(c, e, e + 1), y, zeros[:], ADD)
 
-        def ending(e, alone):
-            groups = [(c, group_of(c, e)) for c in range(ROW_TILES)]
-            return [(c, g) for c, g in groups if GROUPS[c][g][1] == e + 1 and (GROUPS[c][g][0] == e) == alone]
+        def early_tiles(e):
+            return ROW_TILES - 1 if e == E - LATE - 1 else ROW_TILES
+
+        def last_first(c):
+            return E - LATE - (c - 1)
 
         def store(c):
             nc.sync.dma_start(out[c * P : (c + 1) * P, :], out_sb[c][:])
@@ -227,39 +220,62 @@ def tile_moe_two_mlp_relu_kernel(
         spread_gate()
 
         for e in range(E):
-            unit_a, unit_b = PASSES * e, PASSES * e + 1
-            load_w1(unit_a)
-            load_w1(unit_b)
+            for o in range(PASSES):
+                load_w1(e, o)
             if e == 0:
                 nc.sync.dma_start(dst_list[:], dst)
-            load_w2(e)
-            quantize_w1(unit_a)
-            due = []
-            if e > 0:
-                quantize_h(e - 1, w1_raw[unit_a % W1_RAW_DEPTH][:, 0, 0 : H // 2].bitcast(BF16))
-                second_matmuls(e - 1, 0, ROW_TILES)
-                if e > 1:
-                    for c, g in ending(e - 1, True):
-                        scatter(c, g, y_one[c])
-                due = ending(e - 1, False)
-            quantize_w1(unit_b)
+            if e < E - LATE:
+                load_w2(e)
+            round_w1(e)
+            before = e - 1
+            if 0 <= before < E - LATE:
+                tiles = early_tiles(before)
+                y = w1_raw[e % W1_RAW_DEPTH][:].rearrange("p (o j i) -> p o j i", o=PASSES, j=PACK)[:, 1, 0:tiles, H - C : H]
+                gates = gate_sb[:, before * C : e * C].rearrange("p (c s) -> p c s", c=1).to_broadcast([P, tiles, C])
+                nc.vector.tensor_tensor(y, acc2[before % 2][:, 0:tiles, :], gates, MULT)
+            for o in range(PASSES):
+                quantize_w1(e, o)
             first_matmuls(e)
-            if e == 1:
-                spare = w1_bf16[unit_b % W1_BF16_DEPTH][:].rearrange("p t m j -> p (t m j)").bitcast(F32)
-                for c, g in ending(0, True):
-                    scatter(c, g, spare[:, c * C : (c + 1) * C])
-            for c, g in due[:1]:
-                scatter(c, g, w1_raw[unit_b % W1_RAW_DEPTH][:, 1, :])
-            if e < E - 1:
+            if 0 <= before < E - LATE:
+                for c in range(tiles):
+                    scatter_one(before, c, y[:, c, :])
+            if e < E - LATE:
                 quantize_w2(e, 0, ROW_TILES)
-            for c, g in due[1:]:
-                scatter(c, g, y_second)
+            if e == E - 1:
+                quantize_h(e - 1)
+            else:
+                relu_h(e)
+            if e < E - LATE:
+                quantize_h(e)
+            if e < E - LATE:
+                for c in range(ROW_TILES):
+                    if c < early_tiles(e):
+                        second_matmul(e, c, acc2[e % 2][:, c, :])
+                    else:
+                        second_matmul(e, c, acc_last[c][:, 0:C])
 
-        last = E - 1
-        for c in range(ROW_TILES):
-            quantize_w2(last, c, c + 1)
-            if c == 0:
-                quantize_h(last, h_last[:])
-            second_matmuls(last, c, c + 1)
-            scatter(c, group_of(c, last), y_last[c])
+        def gated(n, e):
+            second_matmul(e, 0, acc_one[n][:])
+            nc.vector.tensor_tensor(y_one[n][:], acc_one[n][:], gate_sb[:, e * C : (e + 1) * C], MULT)
+
+        for e in range(E - LATE, E):
+            load_w2(e)
+        quantize_w2(E - 2, 0, 1)
+        gated(0, E - 2)
+        quantize_w2(E - 2, 1, ROW_TILES)
+        quantize_w2(E - 1, 0, 1, True)
+        relu_h(E - 1)
+        quantize_h(E - 1)
+        scatter_one(E - 2, 0, y_one[0][:])
+        gated(1, E - 1)
+        quantize_w2(E - 1, 1, ROW_TILES)
+        scatter_one(E - 1, 0, y_one[1][:])
+        store(0)
+        for c in range(1, ROW_TILES):
+            first = last_first(c)
+            width = (E - first) * C
+            for e in range(E - LATE, E):
+                second_matmul(e, c, acc_last[c][:, (e - first) * C : (e - first + 1) * C])
+            nc.scalar.copy(y_last[c][:, 0:width], acc_last[c][:, 0:width])
+            nc.vector.tensor_tensor(places(c, first, E), y_last[c][:, 0:width], gate_sb[:, first * C : E * C], MULT)
             store(c)

@@ -37,9 +37,14 @@ W1_CODE_DEPTH = 3
 W2_DEPTH = 4
 LATE = 2
 
-SHARES = (56, 48, 48, 48, 48, 48, 48, 8)
-MORE = (0, 0, 0, 0, 0, 0, 0, 88)
-PARTS = 2
+SHARES = (8, 8, 8, 8, 8, 8, 8, 8)
+MORE = (96, 84, 84, 84, 84, 84, 84, 72)
+PARTS = 1
+GROUP_STARTS = [(0, 1, 2, 3, 4, 5, 6, 7), (0, 2, 4, 6), (0, 1, 3, 5)]
+GROUPS = [list(zip(starts, starts[1:] + (E,))) for starts in GROUP_STARTS]
+Y_PASS = 1
+Y_AT = 256
+LAST_PARTS = 2
 
 
 def tile_moe_two_mlp_relu_kernel(
@@ -68,19 +73,15 @@ def tile_moe_two_mlp_relu_kernel(
         w1_codes = ring("w1_codes", W1_CODE_DEPTH * PASSES, [P, H], U32)
         w1_scales = ring("w1_scales", W1_CODE_DEPTH * PASSES, [P, H], U8)
         w2_raw = ring("w2_raw", W2_DEPTH, [P, PACK, N], F32)
-        w2_bf16 = ring("w2_bf16", W2_DEPTH, [P, N, PACK], BF16)
-        w2_codes = ring("w2_codes", W2_DEPTH, [P, N], U32)
-        w2_scales = ring("w2_scales", W2_DEPTH, [P, N], U8)
-        h_bf16 = ring("h_bf16", 2, [P, C * PACK], BF16)
-        h_codes = ring("h_codes", E, [P, C], U32)
-        h_scales = ring("h_scales", E, [P, C], U8)
-        y_one = ring("y_one", LATE, [P, C], F32)
+        w2h_bf16 = ring("w2h_bf16", W2_DEPTH, [P, (N + C) * PACK], BF16)
+        w2h_codes = ring("w2h_codes", W2_DEPTH, [P, N + C], U32)
+        w2h_scales = ring("w2h_scales", W2_DEPTH, [P, N + C], U8)
+        y_one = keep.tile([P, 1, C], F32, name="y_one")
         y_last = ring("y_last", ROW_TILES, [P, 3 * C], F32)
         zeros = keep.tile([P, C], F32, name="zeros")
         acc1 = [psum.tile([P, PACK, C], F32, name=f"acc1_{i}") for i in range(2)]
-        acc2 = [psum.tile([P, ROW_TILES, C], F32, name=f"acc2_{i}") for i in range(2)]
-        acc_one = [psum.tile([P, C], F32, name=f"acc_one{i}") for i in range(LATE)]
-        acc_last = [None] + [psum.tile([P, 3 * C], F32, name=f"acc_last{c}") for c in range(1, ROW_TILES)]
+        acc_one = [psum.tile([P, ROW_TILES, C], F32, name=f"acc_one{i}") for i in range(2)]
+        acc_group = [None] + [[psum.tile([P, 3 * C], F32, name=f"acc_group{c}_{i}") for i in range(2)] for c in range(1, ROW_TILES)]
 
         def load_words(o):
             nc.sync.dma_start(tok_words[o][:], x_words[o].rearrange("p t r -> p (t r)").bitcast(I32))
@@ -104,13 +105,13 @@ def tile_moe_two_mlp_relu_kernel(
             cut_b = cut - MORE[e]
             nc.scalar.activation(target[:, 0, 0:cut], source[:, 0, 0:cut], COPY)
             nc.scalar.activation(target[:, 1, 0:cut_b], source[:, 1, 0:cut_b], COPY)
-            nc.vector.tensor_copy(target[:, :, cut:P], source[:, :, cut:P])
             if cut_b < cut:
                 nc.vector.tensor_copy(target[:, 1, cut_b:cut], source[:, 1, cut_b:cut])
+            nc.vector.tensor_copy(target[:, :, cut:P], source[:, :, cut:P])
 
         def quantize_w1(e, o):
             u = (e * PASSES + o) % (W1_CODE_DEPTH * PASSES)
-            parts = 1 if o == 0 else (PACK if e == E - 1 else PARTS)
+            parts = 1 if o == 0 else (LAST_PARTS if e == E - 1 else PARTS)
             width = H // parts
             for a in range(parts):
                 first = o * H + a * width
@@ -137,15 +138,18 @@ def tile_moe_two_mlp_relu_kernel(
                     )
 
         def relu_h(e):
-            h = h_bf16[e % 2]
             nc.scalar.activation(
-                h[:].rearrange("p (s t) -> p s t", t=PACK),
+                w2h_bf16[e % W2_DEPTH][:, 0 : C * PACK].rearrange("p (s t) -> p s t", t=PACK),
                 acc1[e % 2][:].rearrange("p t s -> p s t"),
                 RELU,
             )
 
-        def quantize_h(e):
-            nc.vector.quantize_mx(out=h_codes[e][:].bitcast(FP8X4), scales=h_scales[e][:], in_=h_bf16[e % 2][:])
+        def quantize_w2h(e, first, end):
+            nc.vector.quantize_mx(
+                out=w2h_codes[e % W2_DEPTH][:, first:end].bitcast(FP8X4),
+                scales=w2h_scales[e % W2_DEPTH][:, first:end],
+                in_=w2h_bf16[e % W2_DEPTH][:, first * PACK : end * PACK],
+            )
 
         def load_w2(e):
             nc.sync.dma_start(w2_raw[e % W2_DEPTH][:], w2[e].rearrange("(p j) n -> p j n", j=PACK))
@@ -159,30 +163,35 @@ def tile_moe_two_mlp_relu_kernel(
                     nc.tensor.transpose(bank[:, q, :], gate_row[:, column : column + 1].to_broadcast([P, P]), identity[:])
                 nc.scalar.copy(by_slot[:, :, half * PACK : (half + 1) * PACK], bank[:].rearrange("p q n -> p n q"))
 
-        def quantize_w2(e, c0, c1, on_vector=False):
-            grouped = w2_bf16[e % W2_DEPTH]
-            target = grouped[:, c0 * P : c1 * P, :].rearrange("p (g n) j -> p g j n", n=4)
+        def round_w2(e, c0, c1, on_vector=False):
+            grouped = w2h_bf16[e % W2_DEPTH][:, (C + c0 * P) * PACK : (C + c1 * P) * PACK]
+            target = grouped.rearrange("p (g n j) -> p g j n", n=4, j=PACK)
             source = w2_raw[e % W2_DEPTH][:, :, c0 * P : c1 * P].rearrange("p j (g n) -> p g j n", n=4)
             if on_vector:
                 nc.vector.tensor_copy(target, source)
             else:
                 nc.scalar.activation(target, source, COPY)
-            for c in range(c0, c1, 2):
-                cols = slice(c * P, min(c + 2, c1) * P)
-                nc.vector.quantize_mx(
-                    out=w2_codes[e % W2_DEPTH][:, cols].bitcast(FP8X4),
-                    scales=w2_scales[e % W2_DEPTH][:, cols],
-                    in_=grouped[:, cols, :].rearrange("p n j -> p (n j)"),
-                )
 
-        def second_matmul(e, c, sums):
-            cols = slice(c * P, (c + 1) * P)
+        def group_of(c, e):
+            return max(g for g, (first, end) in enumerate(GROUPS[c]) if first <= e)
+
+        def alone(c, e):
+            return GROUPS[c][group_of(c, e)] == (e, e + 1)
+
+        def second_matmul(e, c):
+            g = group_of(c, e)
+            place = e - GROUPS[c][g][0]
+            if alone(c, e):
+                sums = acc_one[e % 2][:, [x for x in range(ROW_TILES) if alone(x, e)].index(c), :]
+            else:
+                sums = acc_group[c][g % 2][:, place * C : (place + 1) * C]
+            cols = slice(C + c * P, C + (c + 1) * P)
             nc.tensor.matmul_mx(
                 out=sums,
-                lhsT=w2_codes[e % W2_DEPTH][:, cols].bitcast(FP8X4),
-                lhsT_scale=w2_scales[e % W2_DEPTH][:, cols],
-                rhs=h_codes[e][:].bitcast(FP8X4),
-                rhs_scale=h_scales[e][:],
+                lhsT=w2h_codes[e % W2_DEPTH][:, cols].bitcast(FP8X4),
+                lhsT_scale=w2h_scales[e % W2_DEPTH][:, cols],
+                rhs=w2h_codes[e % W2_DEPTH][:, 0:C].bitcast(FP8X4),
+                rhs_scale=w2h_scales[e % W2_DEPTH][:, 0:C],
                 start=True,
                 stop=True,
             )
@@ -190,14 +199,21 @@ def tile_moe_two_mlp_relu_kernel(
         def places(c, first, end):
             return out_sb[c][:].indirect(dst_list[:, first * C // LIST_ROWS : end * C // LIST_ROWS])
 
+        def times_gate(e, y):
+            count = y.shape[1]
+            gates = gate_sb[:, e * C : (e + 1) * C].rearrange("p (c s) -> p c s", c=1).to_broadcast([P, count, C])
+            nc.vector.tensor_tensor(y, acc_one[e % 2][:, 0:count, :], gates, MULT)
+
         def scatter_one(e, c, y):
             nc.vector.tensor_tensor(places(c, e, e + 1), y, zeros[:], ADD)
 
-        def early_tiles(e):
-            return ROW_TILES - 1 if e == E - LATE - 1 else ROW_TILES
+        def copy_group(c, g, staging):
+            first, end = GROUPS[c][g]
+            nc.scalar.copy(staging[:, 0 : (end - first) * C], acc_group[c][g % 2][:, 0 : (end - first) * C])
 
-        def last_first(c):
-            return E - LATE - (c - 1)
+        def scatter_group(c, g, staging):
+            first, end = GROUPS[c][g]
+            nc.vector.tensor_tensor(places(c, first, end), staging[:, 0 : (end - first) * C], gate_sb[:, first * C : end * C], MULT)
 
         def store(c):
             nc.sync.dma_start(out[c * P : (c + 1) * P, :], out_sb[c][:])
@@ -228,54 +244,62 @@ def tile_moe_two_mlp_relu_kernel(
                 load_w2(e)
             round_w1(e)
             before = e - 1
+            singles, groups = [], []
+            raw = w1_raw[e % W1_RAW_DEPTH][:].rearrange("p (o j i) -> p o j i", o=PASSES, j=PACK)
             if 0 <= before < E - LATE:
-                tiles = early_tiles(before)
-                y = w1_raw[e % W1_RAW_DEPTH][:].rearrange("p (o j i) -> p o j i", o=PASSES, j=PACK)[:, 1, 0:tiles, H - C : H]
-                gates = gate_sb[:, before * C : e * C].rearrange("p (c s) -> p c s", c=1).to_broadcast([P, tiles, C])
-                nc.vector.tensor_tensor(y, acc2[before % 2][:, 0:tiles, :], gates, MULT)
+                singles = [c for c in range(ROW_TILES) if alone(c, before)]
+                groups = [(c, group_of(c, before)) for c in range(ROW_TILES) if c not in singles]
+                groups = [(c, g) for c, g in groups if GROUPS[c][g][1] == e]
+            single = before
+            if e == E - 2:
+                singles = []
+            elif e == E - 1:
+                single, singles = e - 2, [0]
+            if singles:
+                y = raw[:, 1, 0 : len(singles), Y_AT : Y_AT + C]
+                times_gate(single, y)
+            for n, (c, g) in enumerate(groups):
+                copy_group(c, g, raw[:, Y_PASS, PACK - 1 - n, :])
             for o in range(PASSES):
                 quantize_w1(e, o)
             first_matmuls(e)
-            if 0 <= before < E - LATE:
-                for c in range(tiles):
-                    scatter_one(before, c, y[:, c, :])
+            for n, c in enumerate(singles):
+                scatter_one(single, c, y[:, n, :])
+            for n, (c, g) in enumerate(groups):
+                scatter_group(c, g, raw[:, Y_PASS, PACK - 1 - n, :])
             if e < E - LATE:
-                quantize_w2(e, 0, ROW_TILES)
-            if e == E - 1:
-                quantize_h(e - 1)
-            else:
+                round_w2(e, 0, ROW_TILES)
                 relu_h(e)
-            if e < E - LATE:
-                quantize_h(e)
-            if e < E - LATE:
+                quantize_w2h(e, 0, N + C)
                 for c in range(ROW_TILES):
-                    if c < early_tiles(e):
-                        second_matmul(e, c, acc2[e % 2][:, c, :])
-                    else:
-                        second_matmul(e, c, acc_last[c][:, 0:C])
-
-        def gated(n, e):
-            second_matmul(e, 0, acc_one[n][:])
-            nc.vector.tensor_tensor(y_one[n][:], acc_one[n][:], gate_sb[:, e * C : (e + 1) * C], MULT)
+                    second_matmul(e, c)
+            elif e == E - 2:
+                relu_h(e)
 
         for e in range(E - LATE, E):
             load_w2(e)
-        quantize_w2(E - 2, 0, 1)
-        gated(0, E - 2)
-        quantize_w2(E - 2, 1, ROW_TILES)
-        quantize_w2(E - 1, 0, 1, True)
+        round_w2(E - 2, 0, 1)
+        quantize_w2h(E - 2, 0, C + P)
+        second_matmul(E - 2, 0)
+        round_w2(E - 2, 1, ROW_TILES)
+        round_w2(E - 1, 0, 1, True)
+        y = w2_raw[(E - 1) % W2_DEPTH][:, 0:1, 0:C]
+        times_gate(E - 2, y)
+        quantize_w2h(E - 2, C + P, C + N)
         relu_h(E - 1)
-        quantize_h(E - 1)
-        scatter_one(E - 2, 0, y_one[0][:])
-        gated(1, E - 1)
-        quantize_w2(E - 1, 1, ROW_TILES)
-        scatter_one(E - 1, 0, y_one[1][:])
+        quantize_w2h(E - 1, 0, C + P)
+        scatter_one(E - 2, 0, y[:, 0, :])
+        second_matmul(E - 1, 0)
+        round_w2(E - 1, 1, 2)
+        quantize_w2h(E - 1, C + P, C + 2 * P)
+        times_gate(E - 1, y_one[:])
+        round_w2(E - 1, 2, 3)
+        quantize_w2h(E - 1, C + 2 * P, C + 3 * P)
+        scatter_one(E - 1, 0, y_one[:, 0, :])
         store(0)
         for c in range(1, ROW_TILES):
-            first = last_first(c)
-            width = (E - first) * C
             for e in range(E - LATE, E):
-                second_matmul(e, c, acc_last[c][:, (e - first) * C : (e - first + 1) * C])
-            nc.scalar.copy(y_last[c][:, 0:width], acc_last[c][:, 0:width])
-            nc.vector.tensor_tensor(places(c, first, E), y_last[c][:, 0:width], gate_sb[:, first * C : E * C], MULT)
+                second_matmul(e, c)
+            copy_group(c, group_of(c, E - 1), y_last[c])
+            scatter_group(c, group_of(c, E - 1), y_last[c])
             store(c)

@@ -38,8 +38,8 @@ W2_DEPTH = 4
 LATE = 2
 
 SHARES = (8, 8, 8, 8, 8, 8, 8, 8)
-MORE = (96, 84, 84, 84, 84, 84, 84, 72)
-PARTS = 1
+MORE = (96, 92, 92, 92, 92, 92, 92, 72)
+PARTS = 2
 GROUP_STARTS = [(0, 1, 2, 3, 4, 5, 6, 7), (0, 2, 4, 6), (0, 1, 3, 5)]
 GROUPS = [list(zip(starts, starts[1:] + (E,))) for starts in GROUP_STARTS]
 Y_PASS = 1
@@ -220,8 +220,10 @@ def tile_moe_two_mlp_relu_kernel(
 
         nc.vector.memset(tok_scales[:].bitcast(I32), 0)
         nc.vector.memset(zeros[:], 0.0)
-        for c in range(ROW_TILES):
-            nc.vector.memset(out_sb[c][:], 0.0)
+        nc.vector.memset(out_sb[0][:], 0.0)
+        for c in range(1, ROW_TILES):
+            repeated = zeros[:].rearrange("p (a s) -> p a s", a=1).to_broadcast([P, T // C, C])
+            nc.scalar.copy(out_sb[c][:].rearrange("p (a s) -> p a s", s=C), repeated)
 
         load_words(0)
         nc.sync.dma_start(src_list[:], offs)

@@ -35,16 +35,19 @@ W1_RAW_DEPTH = 4
 W1_BF16_DEPTH = 2
 W1_CODE_DEPTH = 3
 W2_DEPTH = 4
+W2_RAW_DEPTH = 3
 LATE = 2
 
 SHARES = (8, 8, 8, 8, 8, 8, 8, 8)
-MORE = (96, 92, 92, 92, 92, 92, 92, 72)
+MORE = (96, 72, 72, 72, 72, 72, 88, 76)
 PARTS = 2
-GROUP_STARTS = [(0, 1, 2, 3, 4, 5, 6, 7), (0, 2, 4, 6), (0, 1, 3, 5)]
+GROUP_STARTS = [(0, 1, 2, 3, 4, 5, 6, 7), (0, 1, 2, 3, 4, 5, 6), (0, 1, 2, 3, 4, 5)]
 GROUPS = [list(zip(starts, starts[1:] + (E,))) for starts in GROUP_STARTS]
+KEEP = 2
+WARM_UPS = 4
 Y_PASS = 1
 Y_AT = 256
-LAST_PARTS = 2
+LAST_PARTS = 4
 
 
 def tile_moe_two_mlp_relu_kernel(
@@ -72,7 +75,11 @@ def tile_moe_two_mlp_relu_kernel(
         w1_bf16 = ring("w1_bf16", W1_BF16_DEPTH, [P, PASSES * H * PACK], BF16)
         w1_codes = ring("w1_codes", W1_CODE_DEPTH * PASSES, [P, H], U32)
         w1_scales = ring("w1_scales", W1_CODE_DEPTH * PASSES, [P, H], U8)
-        w2_raw = ring("w2_raw", W2_DEPTH, [P, PACK, N], F32)
+        w2_raw = ring("w2_raw", W2_RAW_DEPTH, [P, PACK * N], F32)
+        late_raw = keep.tile([P, LATE * PACK * N], F32, name="late_raw", align_bytes=64)
+        late_bf16 = keep.tile([P, LATE * P * PACK], BF16, name="late_bf16", align_bytes=64)
+        late_codes = keep.tile([P, LATE * P], U32, name="late_codes", align_bytes=64)
+        late_scales = keep.tile([P, LATE * P], U8, name="late_scales", align_bytes=64)
         w2h_bf16 = ring("w2h_bf16", W2_DEPTH, [P, (N + C) * PACK], BF16)
         w2h_codes = ring("w2h_codes", W2_DEPTH, [P, N + C], U32)
         w2h_scales = ring("w2h_scales", W2_DEPTH, [P, N + C], U8)
@@ -81,7 +88,8 @@ def tile_moe_two_mlp_relu_kernel(
         zeros = keep.tile([P, C], F32, name="zeros")
         acc1 = [psum.tile([P, PACK, C], F32, name=f"acc1_{i}") for i in range(2)]
         acc_one = [psum.tile([P, ROW_TILES, C], F32, name=f"acc_one{i}") for i in range(2)]
-        acc_group = [None] + [[psum.tile([P, 3 * C], F32, name=f"acc_group{c}_{i}") for i in range(2)] for c in range(1, ROW_TILES)]
+        acc_group = [None] + [[psum.tile([P, 3 * C], F32, name=f"acc_group{c}")] * 2 for c in range(1, ROW_TILES)]
+        unread = psum.tile([P, K_PASS], F32, name="unread")
 
         def load_words(o):
             nc.sync.dma_start(tok_words[o][:], x_words[o].rearrange("p t r -> p (t r)").bitcast(I32))
@@ -137,22 +145,32 @@ def tile_moe_two_mlp_relu_kernel(
                         stop=(o == PASSES - 1),
                     )
 
-        def relu_h(e):
+        def relu_h(e, h=None):
+            if h is None:
+                h = w2h_bf16[e % W2_DEPTH][:, 0 : C * PACK]
             nc.scalar.activation(
-                w2h_bf16[e % W2_DEPTH][:, 0 : C * PACK].rearrange("p (s t) -> p s t", t=PACK),
+                h.rearrange("p (s t) -> p s t", t=PACK),
                 acc1[e % 2][:].rearrange("p t s -> p s t"),
                 RELU,
             )
 
-        def quantize_w2h(e, first, end):
+        def quantize_w2h(e, first, end, source=None):
             nc.vector.quantize_mx(
                 out=w2h_codes[e % W2_DEPTH][:, first:end].bitcast(FP8X4),
                 scales=w2h_scales[e % W2_DEPTH][:, first:end],
-                in_=w2h_bf16[e % W2_DEPTH][:, first * PACK : end * PACK],
+                in_=w2h_bf16[e % W2_DEPTH][:, first * PACK : end * PACK] if source is None else source,
             )
 
-        def load_w2(e):
-            nc.sync.dma_start(w2_raw[e % W2_DEPTH][:], w2[e].rearrange("(p j) n -> p j n", j=PACK))
+        def raw_w2(e):
+            if e < E - LATE:
+                return w2_raw[e % W2_RAW_DEPTH][:]
+            n = e - (E - LATE)
+            return late_raw[:, n * PACK * N : (n + 1) * PACK * N]
+
+        def load_w2(e, c0=0, c1=ROW_TILES):
+            cols = slice(c0 * P, c1 * P)
+            rows = w2[e].rearrange("(p j) n -> p j n", j=PACK)
+            nc.sync.dma_start(raw_w2(e).rearrange("p (j n) -> p j n", j=PACK)[:, :, cols], rows[:, :, cols])
 
         def spread_gate():
             by_slot = gate_sb[:].rearrange("p (n q) -> p n q", n=P)
@@ -163,10 +181,11 @@ def tile_moe_two_mlp_relu_kernel(
                     nc.tensor.transpose(bank[:, q, :], gate_row[:, column : column + 1].to_broadcast([P, P]), identity[:])
                 nc.scalar.copy(by_slot[:, :, half * PACK : (half + 1) * PACK], bank[:].rearrange("p q n -> p n q"))
 
-        def round_w2(e, c0, c1, on_vector=False):
-            grouped = w2h_bf16[e % W2_DEPTH][:, (C + c0 * P) * PACK : (C + c1 * P) * PACK]
+        def round_w2(e, c0, c1, on_vector=False, grouped=None):
+            if grouped is None:
+                grouped = w2h_bf16[e % W2_DEPTH][:, (C + c0 * P) * PACK : (C + c1 * P) * PACK]
             target = grouped.rearrange("p (g n j) -> p g j n", n=4, j=PACK)
-            source = w2_raw[e % W2_DEPTH][:, :, c0 * P : c1 * P].rearrange("p j (g n) -> p g j n", n=4)
+            source = raw_w2(e).rearrange("p (j g n) -> p g j n", j=PACK, n=4)[:, c0 * P // 4 : c1 * P // 4]
             if on_vector:
                 nc.vector.tensor_copy(target, source)
             else:
@@ -185,11 +204,13 @@ def tile_moe_two_mlp_relu_kernel(
                 sums = acc_one[e % 2][:, [x for x in range(ROW_TILES) if alone(x, e)].index(c), :]
             else:
                 sums = acc_group[c][g % 2][:, place * C : (place + 1) * C]
-            cols = slice(C + c * P, C + (c + 1) * P)
+            codes, scales, first = w2h_codes[e % W2_DEPTH], w2h_scales[e % W2_DEPTH], C + c * P
+            if e >= E - LATE and c == ROW_TILES - 1:
+                codes, scales, first = late_codes, late_scales, (e - E + LATE) * P
             nc.tensor.matmul_mx(
                 out=sums,
-                lhsT=w2h_codes[e % W2_DEPTH][:, cols].bitcast(FP8X4),
-                lhsT_scale=w2h_scales[e % W2_DEPTH][:, cols],
+                lhsT=codes[:, first : first + P].bitcast(FP8X4),
+                lhsT_scale=scales[:, first : first + P],
                 rhs=w2h_codes[e % W2_DEPTH][:, 0:C].bitcast(FP8X4),
                 rhs_scale=w2h_scales[e % W2_DEPTH][:, 0:C],
                 start=True,
@@ -199,10 +220,10 @@ def tile_moe_two_mlp_relu_kernel(
         def places(c, first, end):
             return out_sb[c][:].indirect(dst_list[:, first * C // LIST_ROWS : end * C // LIST_ROWS])
 
-        def times_gate(e, y):
+        def times_gate(e, y, skip=0):
             count = y.shape[1]
             gates = gate_sb[:, e * C : (e + 1) * C].rearrange("p (c s) -> p c s", c=1).to_broadcast([P, count, C])
-            nc.vector.tensor_tensor(y, acc_one[e % 2][:, 0:count, :], gates, MULT)
+            nc.vector.tensor_tensor(y, acc_one[e % 2][:, skip : skip + count, :], gates, MULT)
 
         def scatter_one(e, c, y):
             nc.vector.tensor_tensor(places(c, e, e + 1), y, zeros[:], ADD)
@@ -252,19 +273,32 @@ def tile_moe_two_mlp_relu_kernel(
                 singles = [c for c in range(ROW_TILES) if alone(c, before)]
                 groups = [(c, group_of(c, before)) for c in range(ROW_TILES) if c not in singles]
                 groups = [(c, g) for c, g in groups if GROUPS[c][g][1] == e]
-            single = before
+            single, skip = before, 0
             if e == E - 2:
-                singles = []
+                singles = singles[:KEEP]
             elif e == E - 1:
-                single, singles = e - 2, [0]
+                single, skip = e - 2, KEEP
+                singles = [c for c in range(ROW_TILES) if alone(c, single)][KEEP:]
             if singles:
                 y = raw[:, 1, 0 : len(singles), Y_AT : Y_AT + C]
-                times_gate(single, y)
+                times_gate(single, y, skip)
             for n, (c, g) in enumerate(groups):
                 copy_group(c, g, raw[:, Y_PASS, PACK - 1 - n, :])
             for o in range(PASSES):
                 quantize_w1(e, o)
             first_matmuls(e)
+            if e == E - 2:
+                u = (e * PASSES + 1) % (W1_CODE_DEPTH * PASSES)
+                for n in range(WARM_UPS):
+                    nc.tensor.matmul_mx(
+                        out=unread[:],
+                        lhsT=w1_codes[u][:, H - P : H].bitcast(FP8X4),
+                        lhsT_scale=w1_scales[u][:, H - P : H],
+                        rhs=slot_words[0][:, 0:K_PASS].bitcast(FP8X4),
+                        rhs_scale=slot_scales[:, 0:K_PASS],
+                        start=True,
+                        stop=True,
+                    )
             for n, c in enumerate(singles):
                 scatter_one(single, c, y[:, n, :])
             for n, (c, g) in enumerate(groups):
@@ -275,29 +309,35 @@ def tile_moe_two_mlp_relu_kernel(
                 quantize_w2h(e, 0, N + C)
                 for c in range(ROW_TILES):
                     second_matmul(e, c)
-            elif e == E - 2:
-                relu_h(e)
 
-        for e in range(E - LATE, E):
-            load_w2(e)
+        load_w2(E - 2)
+        load_w2(E - 1, 0, 1)
+        load_w2(E - 1, 1, ROW_TILES)
+        h_before = raw[:, 1, PACK - 1, 0 : C * PACK // 2].bitcast(BF16)
+        relu_h(E - 2, h_before)
+        quantize_w2h(E - 2, 0, C, h_before)
         round_w2(E - 2, 0, 1)
-        quantize_w2h(E - 2, 0, C + P)
+        quantize_w2h(E - 2, C, C + P)
         second_matmul(E - 2, 0)
-        round_w2(E - 2, 1, ROW_TILES)
-        round_w2(E - 1, 0, 1, True)
-        y = w2_raw[(E - 1) % W2_DEPTH][:, 0:1, 0:C]
+        round_w2(E - 2, 1, 2)
+        quantize_w2h(E - 2, C + P, C + 2 * P)
+        shared = w2h_bf16[(E - 2) % W2_DEPTH][:, 0 : (C + P) * PACK]
+        round_w2(E - 1, 0, 1, True, shared[:, C * PACK :])
+        y = w2h_bf16[(E - 2) % W2_DEPTH][:, (C + P) * PACK : (C + P) * PACK + 2 * C].bitcast(F32).rearrange("p (c s) -> p c s", c=1)
         times_gate(E - 2, y)
-        quantize_w2h(E - 2, C + P, C + N)
-        relu_h(E - 1)
-        quantize_w2h(E - 1, 0, C + P)
+        relu_h(E - 1, shared[:, 0 : C * PACK])
+        quantize_w2h(E - 1, 0, C + P, shared)
         scatter_one(E - 2, 0, y[:, 0, :])
         second_matmul(E - 1, 0)
         round_w2(E - 1, 1, 2)
         quantize_w2h(E - 1, C + P, C + 2 * P)
         times_gate(E - 1, y_one[:])
-        round_w2(E - 1, 2, 3)
-        quantize_w2h(E - 1, C + 2 * P, C + 3 * P)
         scatter_one(E - 1, 0, y_one[:, 0, :])
+        nc.scalar.copy(
+            late_bf16[:].rearrange("p (e g n j) -> p e g j n", e=LATE, n=4, j=PACK),
+            late_raw[:].rearrange("p (e j g n) -> p e g j n", e=LATE, j=PACK, n=4)[:, :, 2 * P // 4 :],
+        )
+        nc.vector.quantize_mx(out=late_codes[:].bitcast(FP8X4), scales=late_scales[:], in_=late_bf16[:])
         store(0)
         for c in range(1, ROW_TILES):
             for e in range(E - LATE, E):

@@ -24,30 +24,32 @@ P = 128
 PACK = 4
 K_PASS = P * PACK
 PASSES = K // K_PASS
-UNITS = E * PASSES
-LAST_UNIT = UNITS - 1
 ROW_TILES = N // P
 LIST_ROWS = 16
 QUADRANT = 32
 SCALE_ROWS = 4
+RUN = 4
+ALIGN = 256
+
+LATE = 2
+EARLY = E - LATE
+BEFORE_LAST, LAST = E - 2, E - 1
+CLOSING_FIRST = {1: EARLY, 2: EARLY - 1}
 
 W1_RAW_DEPTH = 4
 W1_BF16_DEPTH = 2
 W1_CODE_DEPTH = 3
-W2_DEPTH = 4
 W2_RAW_DEPTH = 3
-LATE = 2
+W2H_DEPTH = 4
 
-SHARES = (8, 8, 8, 8, 8, 8, 8, 8)
-MORE = (96, 72, 72, 72, 72, 72, 88, 76)
-PARTS = 2
-GROUP_STARTS = [(0, 1, 2, 3, 4, 5, 6, 7), (0, 1, 2, 3, 4, 5, 6), (0, 1, 2, 3, 4, 5)]
-GROUPS = [list(zip(starts, starts[1:] + (E,))) for starts in GROUP_STARTS]
-KEEP = 2
+BOTH_PASSES = 8
+FIRST_SHARE = 96
+STREAM_SHARE = 80
+BEFORE_LAST_SHARE = 92
+LAST_SHARE = 76
+PASS1_SHARES = (FIRST_SHARE,) + (STREAM_SHARE,) * (EARLY - 1) + (BEFORE_LAST_SHARE, LAST_SHARE)
+Y_COLUMN = 256
 WARM_UPS = 4
-Y_PASS = 1
-Y_AT = 256
-LAST_PARTS = 4
 
 
 def tile_moe_two_mlp_relu_kernel(
@@ -58,37 +60,41 @@ def tile_moe_two_mlp_relu_kernel(
         keep = ctx.enter_context(tc.tile_pool(name="keep", bufs=1))
         psum = ctx.enter_context(tc.psum_pool(name="psum", bufs=1))
 
-        def ring(name, count, shape, dtype):
-            return [keep.tile(shape, dtype, name=f"{name}{i}", align_bytes=64) for i in range(count)]
+        def one(name, shape, dtype):
+            return keep.tile(shape, dtype, name=name, align_bytes=ALIGN)
 
-        src_list = keep.tile([P, S // LIST_ROWS], U16, name="src_list")
-        dst_list = keep.tile([P, S // LIST_ROWS], U16, name="dst_list")
+        def ring(name, count, shape, dtype):
+            return [one(f"{name}{i}", shape, dtype) for i in range(count)]
+
+        src_list = one("src_list", [P, S // LIST_ROWS], U16)
+        dst_list = one("dst_list", [P, S // LIST_ROWS], U16)
         tok_words = ring("tok_words", PASSES, [P, T], I32)
-        tok_scales = keep.tile([P, T], U8, name="tok_scales")
+        tok_scales = one("tok_scales", [P, T], U8)
         slot_words = ring("slot_words", PASSES, [P, S], U32)
-        slot_scales = keep.tile([P, S], U8, name="slot_scales", align_bytes=64)
-        gate_row = keep.tile([P, S // P], F32, name="gate_row")
-        identity = keep.tile([P, P], F32, name="identity")
-        gate_sb = keep.tile([P, S], F32, name="gate_sb")
+        slot_scales = one("slot_scales", [P, S], U8)
+        gate_row = one("gate_row", [P, S // P], F32)
+        identity = one("identity", [P, P], F32)
+        gate_sb = one("gate_sb", [P, S], F32)
+        zeros = one("zeros", [P, C], F32)
         out_sb = ring("out_sb", ROW_TILES, [P, T], F32)
         w1_raw = ring("w1_raw", W1_RAW_DEPTH, [P, PASSES * PACK * H], F32)
         w1_bf16 = ring("w1_bf16", W1_BF16_DEPTH, [P, PASSES * H * PACK], BF16)
         w1_codes = ring("w1_codes", W1_CODE_DEPTH * PASSES, [P, H], U32)
         w1_scales = ring("w1_scales", W1_CODE_DEPTH * PASSES, [P, H], U8)
         w2_raw = ring("w2_raw", W2_RAW_DEPTH, [P, PACK * N], F32)
-        late_raw = keep.tile([P, LATE * PACK * N], F32, name="late_raw", align_bytes=64)
-        late_bf16 = keep.tile([P, LATE * P * PACK], BF16, name="late_bf16", align_bytes=64)
-        late_codes = keep.tile([P, LATE * P], U32, name="late_codes", align_bytes=64)
-        late_scales = keep.tile([P, LATE * P], U8, name="late_scales", align_bytes=64)
-        w2h_bf16 = ring("w2h_bf16", W2_DEPTH, [P, (N + C) * PACK], BF16)
-        w2h_codes = ring("w2h_codes", W2_DEPTH, [P, N + C], U32)
-        w2h_scales = ring("w2h_scales", W2_DEPTH, [P, N + C], U8)
-        y_one = keep.tile([P, 1, C], F32, name="y_one")
-        y_last = ring("y_last", ROW_TILES, [P, 3 * C], F32)
-        zeros = keep.tile([P, C], F32, name="zeros")
+        w2h_bf16 = ring("w2h_bf16", W2H_DEPTH, [P, (C + N) * PACK], BF16)
+        w2h_codes = ring("w2h_codes", W2H_DEPTH, [P, C + N], U32)
+        w2h_scales = ring("w2h_scales", W2H_DEPTH, [P, C + N], U8)
+        late_raw = one("late_raw", [P, LATE * PACK * N], F32)
+        late_bf16 = one("late_bf16", [P, LATE * P * PACK], BF16)
+        late_codes = one("late_codes", [P, LATE * P], U32)
+        late_scales = one("late_scales", [P, LATE * P], U8)
+        y_last = one("y_last", [P, 1, C], F32)
+        closing_width = {c: (E - first) * C for c, first in CLOSING_FIRST.items()}
+        y_closing = {c: one(f"y_closing{c}", [P, width], F32) for c, width in closing_width.items()}
         acc1 = [psum.tile([P, PACK, C], F32, name=f"acc1_{i}") for i in range(2)]
-        acc_one = [psum.tile([P, ROW_TILES, C], F32, name=f"acc_one{i}") for i in range(2)]
-        acc_group = [None] + [[psum.tile([P, 3 * C], F32, name=f"acc_group{c}")] * 2 for c in range(1, ROW_TILES)]
+        acc2 = [psum.tile([P, ROW_TILES, C], F32, name=f"acc2_{i}") for i in range(2)]
+        acc_closing = {c: psum.tile([P, width], F32, name=f"acc_closing{c}") for c, width in closing_width.items()}
         unread = psum.tile([P, K_PASS], F32, name="unread")
 
         def load_words(o):
@@ -102,76 +108,6 @@ def tile_moe_two_mlp_relu_kernel(
                         x_scales[o, r::SCALE_ROWS, :].bitcast(I32),
                     )
 
-        def load_w1(e, o):
-            rows = w1[e, o * K_PASS : (o + 1) * K_PASS, :].rearrange("(p j) i -> p (j i)", j=PACK)
-            nc.sync.dma_start(w1_raw[e % W1_RAW_DEPTH][:, o * PACK * H : (o + 1) * PACK * H], rows)
-
-        def round_w1(e):
-            source = w1_raw[e % W1_RAW_DEPTH][:].rearrange("p (o j m t) -> p o m j t", o=PASSES, j=PACK, t=PACK)
-            target = w1_bf16[e % W1_BF16_DEPTH][:].rearrange("p (o t m j) -> p o m j t", o=PASSES, j=PACK, t=PACK)
-            cut = P - SHARES[e]
-            cut_b = cut - MORE[e]
-            nc.scalar.activation(target[:, 0, 0:cut], source[:, 0, 0:cut], COPY)
-            nc.scalar.activation(target[:, 1, 0:cut_b], source[:, 1, 0:cut_b], COPY)
-            if cut_b < cut:
-                nc.vector.tensor_copy(target[:, 1, cut_b:cut], source[:, 1, cut_b:cut])
-            nc.vector.tensor_copy(target[:, :, cut:P], source[:, :, cut:P])
-
-        def quantize_w1(e, o):
-            u = (e * PASSES + o) % (W1_CODE_DEPTH * PASSES)
-            parts = 1 if o == 0 else (LAST_PARTS if e == E - 1 else PARTS)
-            width = H // parts
-            for a in range(parts):
-                first = o * H + a * width
-                nc.vector.quantize_mx(
-                    out=w1_codes[u][:, a * width : (a + 1) * width].bitcast(FP8X4),
-                    scales=w1_scales[u][:, a * width : (a + 1) * width],
-                    in_=w1_bf16[e % W1_BF16_DEPTH][:, first * PACK : (first + width) * PACK],
-                )
-
-        def first_matmuls(e):
-            slots = slice(e * C, (e + 1) * C)
-            for t in range(PACK):
-                cols = slice(t * P, (t + 1) * P)
-                for o in range(PASSES):
-                    u = (e * PASSES + o) % (W1_CODE_DEPTH * PASSES)
-                    nc.tensor.matmul_mx(
-                        out=acc1[e % 2][:, t, :],
-                        lhsT=w1_codes[u][:, cols].bitcast(FP8X4),
-                        lhsT_scale=w1_scales[u][:, cols],
-                        rhs=slot_words[o][:, slots].bitcast(FP8X4),
-                        rhs_scale=slot_scales[SCALE_ROWS * o : P, slots],
-                        start=(o == 0),
-                        stop=(o == PASSES - 1),
-                    )
-
-        def relu_h(e, h=None):
-            if h is None:
-                h = w2h_bf16[e % W2_DEPTH][:, 0 : C * PACK]
-            nc.scalar.activation(
-                h.rearrange("p (s t) -> p s t", t=PACK),
-                acc1[e % 2][:].rearrange("p t s -> p s t"),
-                RELU,
-            )
-
-        def quantize_w2h(e, first, end, source=None):
-            nc.vector.quantize_mx(
-                out=w2h_codes[e % W2_DEPTH][:, first:end].bitcast(FP8X4),
-                scales=w2h_scales[e % W2_DEPTH][:, first:end],
-                in_=w2h_bf16[e % W2_DEPTH][:, first * PACK : end * PACK] if source is None else source,
-            )
-
-        def raw_w2(e):
-            if e < E - LATE:
-                return w2_raw[e % W2_RAW_DEPTH][:]
-            n = e - (E - LATE)
-            return late_raw[:, n * PACK * N : (n + 1) * PACK * N]
-
-        def load_w2(e, c0=0, c1=ROW_TILES):
-            cols = slice(c0 * P, c1 * P)
-            rows = w2[e].rearrange("(p j) n -> p j n", j=PACK)
-            nc.sync.dma_start(raw_w2(e).rearrange("p (j n) -> p j n", j=PACK)[:, :, cols], rows[:, :, cols])
-
         def spread_gate():
             by_slot = gate_sb[:].rearrange("p (n q) -> p n q", n=P)
             for half in range(2):
@@ -181,38 +117,111 @@ def tile_moe_two_mlp_relu_kernel(
                     nc.tensor.transpose(bank[:, q, :], gate_row[:, column : column + 1].to_broadcast([P, P]), identity[:])
                 nc.scalar.copy(by_slot[:, :, half * PACK : (half + 1) * PACK], bank[:].rearrange("p q n -> p n q"))
 
-        def round_w2(e, c0, c1, on_vector=False, grouped=None):
-            if grouped is None:
-                grouped = w2h_bf16[e % W2_DEPTH][:, (C + c0 * P) * PACK : (C + c1 * P) * PACK]
-            target = grouped.rearrange("p (g n j) -> p g j n", n=4, j=PACK)
-            source = raw_w2(e).rearrange("p (j g n) -> p g j n", j=PACK, n=4)[:, c0 * P // 4 : c1 * P // 4]
-            if on_vector:
-                nc.vector.tensor_copy(target, source)
-            else:
-                nc.scalar.activation(target, source, COPY)
+        def load_w1(e, o):
+            rows = w1[e, o * K_PASS : (o + 1) * K_PASS, :].rearrange("(p j) i -> p (j i)", j=PACK)
+            nc.sync.dma_start(w1_raw[e % W1_RAW_DEPTH][:, o * PACK * H : (o + 1) * PACK * H], rows)
 
-        def group_of(c, e):
-            return max(g for g, (first, end) in enumerate(GROUPS[c]) if first <= e)
+        def round_w1(e):
+            source = w1_raw[e % W1_RAW_DEPTH][:].rearrange("p (o j m t) -> p o m j t", o=PASSES, j=PACK, t=PACK)
+            target = w1_bf16[e % W1_BF16_DEPTH][:].rearrange("p (o t m j) -> p o m j t", o=PASSES, j=PACK, t=PACK)
+            cut0 = P - BOTH_PASSES
+            cut1 = cut0 - PASS1_SHARES[e]
+            nc.scalar.activation(target[:, 0, 0:cut0], source[:, 0, 0:cut0], COPY)
+            nc.scalar.activation(target[:, 1, 0:cut1], source[:, 1, 0:cut1], COPY)
+            nc.vector.tensor_copy(target[:, 1, cut1:cut0], source[:, 1, cut1:cut0])
+            nc.vector.tensor_copy(target[:, :, cut0:P], source[:, :, cut0:P])
 
-        def alone(c, e):
-            return GROUPS[c][group_of(c, e)] == (e, e + 1)
+        def w1_slot(e, o):
+            return e % W1_CODE_DEPTH * PASSES + o
+
+        def quantize_w1(e, o, parts):
+            width = H // parts
+            for a in range(parts):
+                cols = slice(a * width, (a + 1) * width)
+                first = o * H + a * width
+                nc.vector.quantize_mx(
+                    out=w1_codes[w1_slot(e, o)][:, cols].bitcast(FP8X4),
+                    scales=w1_scales[w1_slot(e, o)][:, cols],
+                    in_=w1_bf16[e % W1_BF16_DEPTH][:, first * PACK : (first + width) * PACK],
+                )
+
+        def first_matmuls(e):
+            slots = slice(e * C, (e + 1) * C)
+            for t in range(PACK):
+                cols = slice(t * P, (t + 1) * P)
+                for o in range(PASSES):
+                    nc.tensor.matmul_mx(
+                        out=acc1[e % 2][:, t, :],
+                        lhsT=w1_codes[w1_slot(e, o)][:, cols].bitcast(FP8X4),
+                        lhsT_scale=w1_scales[w1_slot(e, o)][:, cols],
+                        rhs=slot_words[o][:, slots].bitcast(FP8X4),
+                        rhs_scale=slot_scales[SCALE_ROWS * o : P, slots],
+                        start=(o == 0),
+                        stop=(o == PASSES - 1),
+                    )
+
+        def warm_up(e):
+            for n in range(WARM_UPS):
+                nc.tensor.matmul_mx(
+                    out=unread[:],
+                    lhsT=w1_codes[w1_slot(e, 1)][:, H - P : H].bitcast(FP8X4),
+                    lhsT_scale=w1_scales[w1_slot(e, 1)][:, H - P : H],
+                    rhs=slot_words[0][:, 0:K_PASS].bitcast(FP8X4),
+                    rhs_scale=slot_scales[:, 0:K_PASS],
+                    start=True,
+                    stop=True,
+                )
+
+        def relu_h(e, h):
+            nc.scalar.activation(
+                h.rearrange("p (s t) -> p s t", t=PACK),
+                acc1[e % 2][:].rearrange("p t s -> p s t"),
+                RELU,
+            )
+
+        def raw_w2(e):
+            if e < EARLY:
+                return w2_raw[e % W2_RAW_DEPTH][:]
+            return late_raw[:, (e - EARLY) * PACK * N : (e - EARLY + 1) * PACK * N]
+
+        def load_w2(e, c0, c1):
+            cols = slice(c0 * P, c1 * P)
+            rows = w2[e].rearrange("(p j) n -> p j n", j=PACK)
+            nc.sync.dma_start(raw_w2(e).rearrange("p (j n) -> p j n", j=PACK)[:, :, cols], rows[:, :, cols])
+
+        def w2h_values(e, first, end):
+            return w2h_bf16[e % W2H_DEPTH][:, first * PACK : end * PACK]
+
+        def w2_views(e, c0, c1, values):
+            target = values.rearrange("p (g n j) -> p g j n", n=RUN, j=PACK)
+            source = raw_w2(e).rearrange("p (j g n) -> p g j n", j=PACK, n=RUN)
+            return target, source[:, c0 * P // RUN : c1 * P // RUN]
+
+        def quantize_w2h(e, first, end, values):
+            nc.vector.quantize_mx(
+                out=w2h_codes[e % W2H_DEPTH][:, first:end].bitcast(FP8X4),
+                scales=w2h_scales[e % W2H_DEPTH][:, first:end],
+                in_=values,
+            )
+
+        def closing(e, c):
+            return c in CLOSING_FIRST and e >= CLOSING_FIRST[c]
 
         def second_matmul(e, c):
-            g = group_of(c, e)
-            place = e - GROUPS[c][g][0]
-            if alone(c, e):
-                sums = acc_one[e % 2][:, [x for x in range(ROW_TILES) if alone(x, e)].index(c), :]
+            if closing(e, c):
+                place = e - CLOSING_FIRST[c]
+                sums = acc_closing[c][:, place * C : (place + 1) * C]
             else:
-                sums = acc_group[c][g % 2][:, place * C : (place + 1) * C]
-            codes, scales, first = w2h_codes[e % W2_DEPTH], w2h_scales[e % W2_DEPTH], C + c * P
-            if e >= E - LATE and c == ROW_TILES - 1:
-                codes, scales, first = late_codes, late_scales, (e - E + LATE) * P
+                sums = acc2[e % 2][:, c, :]
+            codes, scales, first = w2h_codes[e % W2H_DEPTH], w2h_scales[e % W2H_DEPTH], C + c * P
+            if e >= EARLY and c == ROW_TILES - 1:
+                codes, scales, first = late_codes, late_scales, (e - EARLY) * P
             nc.tensor.matmul_mx(
                 out=sums,
                 lhsT=codes[:, first : first + P].bitcast(FP8X4),
                 lhsT_scale=scales[:, first : first + P],
-                rhs=w2h_codes[e % W2_DEPTH][:, 0:C].bitcast(FP8X4),
-                rhs_scale=w2h_scales[e % W2_DEPTH][:, 0:C],
+                rhs=w2h_codes[e % W2H_DEPTH][:, 0:C].bitcast(FP8X4),
+                rhs_scale=w2h_scales[e % W2H_DEPTH][:, 0:C],
                 start=True,
                 stop=True,
             )
@@ -220,21 +229,13 @@ def tile_moe_two_mlp_relu_kernel(
         def places(c, first, end):
             return out_sb[c][:].indirect(dst_list[:, first * C // LIST_ROWS : end * C // LIST_ROWS])
 
-        def times_gate(e, y, skip=0):
+        def times_gate(e, y):
             count = y.shape[1]
             gates = gate_sb[:, e * C : (e + 1) * C].rearrange("p (c s) -> p c s", c=1).to_broadcast([P, count, C])
-            nc.vector.tensor_tensor(y, acc_one[e % 2][:, skip : skip + count, :], gates, MULT)
+            nc.vector.tensor_tensor(y, acc2[e % 2][:, 0:count, :], gates, MULT)
 
         def scatter_one(e, c, y):
             nc.vector.tensor_tensor(places(c, e, e + 1), y, zeros[:], ADD)
-
-        def copy_group(c, g, staging):
-            first, end = GROUPS[c][g]
-            nc.scalar.copy(staging[:, 0 : (end - first) * C], acc_group[c][g % 2][:, 0 : (end - first) * C])
-
-        def scatter_group(c, g, staging):
-            first, end = GROUPS[c][g]
-            nc.vector.tensor_tensor(places(c, first, end), staging[:, 0 : (end - first) * C], gate_sb[:, first * C : end * C], MULT)
 
         def store(c):
             nc.sync.dma_start(out[c * P : (c + 1) * P, :], out_sb[c][:])
@@ -242,8 +243,8 @@ def tile_moe_two_mlp_relu_kernel(
         nc.vector.memset(tok_scales[:].bitcast(I32), 0)
         nc.vector.memset(zeros[:], 0.0)
         nc.vector.memset(out_sb[0][:], 0.0)
+        repeated = zeros[:].rearrange("p (a s) -> p a s", a=1).to_broadcast([P, T // C, C])
         for c in range(1, ROW_TILES):
-            repeated = zeros[:].rearrange("p (a s) -> p a s", a=1).to_broadcast([P, T // C, C])
             nc.scalar.copy(out_sb[c][:].rearrange("p (a s) -> p a s", s=C), repeated)
 
         load_words(0)
@@ -263,85 +264,63 @@ def tile_moe_two_mlp_relu_kernel(
                 load_w1(e, o)
             if e == 0:
                 nc.sync.dma_start(dst_list[:], dst)
-            if e < E - LATE:
-                load_w2(e)
+            if e < EARLY:
+                load_w2(e, 0, ROW_TILES)
             round_w1(e)
-            before = e - 1
-            singles, groups = [], []
-            raw = w1_raw[e % W1_RAW_DEPTH][:].rearrange("p (o j i) -> p o j i", o=PASSES, j=PACK)
-            if 0 <= before < E - LATE:
-                singles = [c for c in range(ROW_TILES) if alone(c, before)]
-                groups = [(c, group_of(c, before)) for c in range(ROW_TILES) if c not in singles]
-                groups = [(c, g) for c, g in groups if GROUPS[c][g][1] == e]
-            single, skip = before, 0
-            if e == E - 2:
-                singles = singles[:KEEP]
-            elif e == E - 1:
-                single, skip = e - 2, KEEP
-                singles = [c for c in range(ROW_TILES) if alone(c, single)][KEEP:]
-            if singles:
-                y = raw[:, 1, 0 : len(singles), Y_AT : Y_AT + C]
-                times_gate(single, y, skip)
-            for n, (c, g) in enumerate(groups):
-                copy_group(c, g, raw[:, Y_PASS, PACK - 1 - n, :])
-            for o in range(PASSES):
-                quantize_w1(e, o)
+            pass1_raw = w1_raw[e % W1_RAW_DEPTH][:, PACK * H :].rearrange("p (j i) -> p j i", j=PACK)
+            due = [c for c in range(ROW_TILES) if 0 < e <= EARLY and not closing(e - 1, c)]
+            if due:
+                y = pass1_raw[:, 0 : len(due), Y_COLUMN : Y_COLUMN + C]
+                times_gate(e - 1, y)
+            quantize_w1(e, 0, 1)
+            quantize_w1(e, 1, PACK if e == LAST else 2)
             first_matmuls(e)
-            if e == E - 2:
-                u = (e * PASSES + 1) % (W1_CODE_DEPTH * PASSES)
-                for n in range(WARM_UPS):
-                    nc.tensor.matmul_mx(
-                        out=unread[:],
-                        lhsT=w1_codes[u][:, H - P : H].bitcast(FP8X4),
-                        lhsT_scale=w1_scales[u][:, H - P : H],
-                        rhs=slot_words[0][:, 0:K_PASS].bitcast(FP8X4),
-                        rhs_scale=slot_scales[:, 0:K_PASS],
-                        start=True,
-                        stop=True,
-                    )
-            for n, c in enumerate(singles):
-                scatter_one(single, c, y[:, n, :])
-            for n, (c, g) in enumerate(groups):
-                scatter_group(c, g, raw[:, Y_PASS, PACK - 1 - n, :])
-            if e < E - LATE:
-                round_w2(e, 0, ROW_TILES)
-                relu_h(e)
-                quantize_w2h(e, 0, N + C)
+            if e == BEFORE_LAST:
+                warm_up(e)
+            for c in due:
+                scatter_one(e - 1, c, y[:, c, :])
+            if e < EARLY:
+                nc.scalar.activation(*w2_views(e, 0, ROW_TILES, w2h_values(e, C, C + N)), COPY)
+                relu_h(e, w2h_values(e, 0, C))
+                quantize_w2h(e, 0, C + N, w2h_values(e, 0, C + N))
                 for c in range(ROW_TILES):
                     second_matmul(e, c)
 
-        load_w2(E - 2)
-        load_w2(E - 1, 0, 1)
-        load_w2(E - 1, 1, ROW_TILES)
-        h_before = raw[:, 1, PACK - 1, 0 : C * PACK // 2].bitcast(BF16)
-        relu_h(E - 2, h_before)
-        quantize_w2h(E - 2, 0, C, h_before)
-        round_w2(E - 2, 0, 1)
-        quantize_w2h(E - 2, C, C + P)
-        second_matmul(E - 2, 0)
-        round_w2(E - 2, 1, 2)
-        quantize_w2h(E - 2, C + P, C + 2 * P)
-        shared = w2h_bf16[(E - 2) % W2_DEPTH][:, 0 : (C + P) * PACK]
-        round_w2(E - 1, 0, 1, True, shared[:, C * PACK :])
-        y = w2h_bf16[(E - 2) % W2_DEPTH][:, (C + P) * PACK : (C + P) * PACK + 2 * C].bitcast(F32).rearrange("p (c s) -> p c s", c=1)
-        times_gate(E - 2, y)
-        relu_h(E - 1, shared[:, 0 : C * PACK])
-        quantize_w2h(E - 1, 0, C + P, shared)
-        scatter_one(E - 2, 0, y[:, 0, :])
-        second_matmul(E - 1, 0)
-        round_w2(E - 1, 1, 2)
-        quantize_w2h(E - 1, C + P, C + 2 * P)
-        times_gate(E - 1, y_one[:])
-        scatter_one(E - 1, 0, y_one[:, 0, :])
+        load_w2(BEFORE_LAST, 0, ROW_TILES)
+        load_w2(LAST, 0, 1)
+        load_w2(LAST, 1, ROW_TILES)
+        h_before = pass1_raw[:, PACK - 1, 0 : C * PACK // 2].bitcast(BF16)
+        relu_h(BEFORE_LAST, h_before)
+        quantize_w2h(BEFORE_LAST, 0, C, h_before)
+        tile0 = w2h_values(BEFORE_LAST, C, C + P)
+        tile1 = w2h_values(BEFORE_LAST, C + P, C + 2 * P)
+        nc.scalar.activation(*w2_views(BEFORE_LAST, 0, 1, tile0), COPY)
+        quantize_w2h(BEFORE_LAST, C, C + P, tile0)
+        second_matmul(BEFORE_LAST, 0)
+        nc.scalar.activation(*w2_views(BEFORE_LAST, 1, 2, tile1), COPY)
+        quantize_w2h(BEFORE_LAST, C + P, C + 2 * P, tile1)
+        nc.vector.tensor_copy(*w2_views(LAST, 0, 1, tile0))
+        y_before = tile1[:, 0 : 2 * C].bitcast(F32).rearrange("p (c s) -> p c s", c=1)
+        times_gate(BEFORE_LAST, y_before)
+        relu_h(LAST, w2h_values(BEFORE_LAST, 0, C))
+        quantize_w2h(LAST, 0, C + P, w2h_values(BEFORE_LAST, 0, C + P))
+        scatter_one(BEFORE_LAST, 0, y_before[:, 0, :])
+        second_matmul(LAST, 0)
+        last_tile1 = w2h_values(LAST, C + P, C + 2 * P)
+        nc.scalar.activation(*w2_views(LAST, 1, 2, last_tile1), COPY)
+        quantize_w2h(LAST, C + P, C + 2 * P, last_tile1)
+        times_gate(LAST, y_last[:])
+        scatter_one(LAST, 0, y_last[:, 0, :])
         nc.scalar.copy(
-            late_bf16[:].rearrange("p (e g n j) -> p e g j n", e=LATE, n=4, j=PACK),
-            late_raw[:].rearrange("p (e j g n) -> p e g j n", e=LATE, j=PACK, n=4)[:, :, 2 * P // 4 :],
+            late_bf16[:].rearrange("p (e g n j) -> p e g j n", e=LATE, n=RUN, j=PACK),
+            late_raw[:].rearrange("p (e j g n) -> p e g j n", e=LATE, j=PACK, n=RUN)[:, :, 2 * P // RUN :],
         )
         nc.vector.quantize_mx(out=late_codes[:].bitcast(FP8X4), scales=late_scales[:], in_=late_bf16[:])
         store(0)
-        for c in range(1, ROW_TILES):
-            for e in range(E - LATE, E):
+
+        for c, first in CLOSING_FIRST.items():
+            for e in range(EARLY, E):
                 second_matmul(e, c)
-            copy_group(c, group_of(c, E - 1), y_last[c])
-            scatter_group(c, group_of(c, E - 1), y_last[c])
+            nc.scalar.copy(y_closing[c][:], acc_closing[c][:])
+            nc.vector.tensor_tensor(places(c, first, E), y_closing[c][:], gate_sb[:, first * C : E * C], MULT)
             store(c)

@@ -45,11 +45,13 @@ W2H_DEPTH = 4
 BOTH_PASSES = 8
 FIRST_SHARE = 96
 STREAM_SHARE = 80
-BEFORE_LAST_SHARE = 92
-LAST_SHARE = 76
+BEFORE_LAST_SHARE = 72
+LAST_SHARE = 60
+LAST_PASS0_SHARE = 36
 PASS1_SHARES = (FIRST_SHARE,) + (STREAM_SHARE,) * (EARLY - 1) + (BEFORE_LAST_SHARE, LAST_SHARE)
-Y_COLUMN = 256
+Y_COLUMN = 320
 WARM_UPS = 4
+FRONT = P * PACK // 2
 
 
 def tile_moe_two_mlp_relu_kernel(
@@ -58,6 +60,7 @@ def tile_moe_two_mlp_relu_kernel(
     nc = tc.nc
     with ExitStack() as ctx:
         keep = ctx.enter_context(tc.tile_pool(name="keep", bufs=1))
+        shared = ctx.enter_context(tc.tile_pool(name="shared", bufs=1))
         psum = ctx.enter_context(tc.psum_pool(name="psum", bufs=1))
 
         def one(name, shape, dtype):
@@ -77,7 +80,7 @@ def tile_moe_two_mlp_relu_kernel(
         gate_sb = one("gate_sb", [P, S], F32)
         zeros = one("zeros", [P, C], F32)
         out_sb = ring("out_sb", ROW_TILES, [P, T], F32)
-        w1_raw = ring("w1_raw", W1_RAW_DEPTH, [P, PASSES * PACK * H], F32)
+        w1_raw = ring("w1_raw", W1_RAW_DEPTH, [P, FRONT + PASSES * PACK * H], F32)
         w1_bf16 = ring("w1_bf16", W1_BF16_DEPTH, [P, PASSES * H * PACK], BF16)
         w1_codes = ring("w1_codes", W1_CODE_DEPTH * PASSES, [P, H], U32)
         w1_scales = ring("w1_scales", W1_CODE_DEPTH * PASSES, [P, H], U8)
@@ -85,13 +88,21 @@ def tile_moe_two_mlp_relu_kernel(
         w2h_bf16 = ring("w2h_bf16", W2H_DEPTH, [P, (C + N) * PACK], BF16)
         w2h_codes = ring("w2h_codes", W2H_DEPTH, [P, C + N], U32)
         w2h_scales = ring("w2h_scales", W2H_DEPTH, [P, C + N], U8)
-        late_raw = one("late_raw", [P, LATE * PACK * N], F32)
-        late_bf16 = one("late_bf16", [P, LATE * P * PACK], BF16)
-        late_codes = one("late_codes", [P, LATE * P], U32)
-        late_scales = one("late_scales", [P, LATE * P], U8)
+        late_first = {0: EARLY, **CLOSING_FIRST}
+        last_stage = one("late_stage", [P, P * PACK // 2 + P * PACK], F32)
+        late_raw = {
+            0: one("late_raw0", [P, PACK * P], F32),
+            1: shared.tile([P, LATE * PACK * P], F32, name="late_raw1", align_bytes=ALIGN, offset=0),
+            2: one("late_raw2", [P, (LATE + 1) * PACK * P], F32),
+        }
+        late_bf16 = {c: one(f"late_bf16{c}", [P, (E - first) * P * PACK], BF16) for c, first in CLOSING_FIRST.items()}
+        late_codes = {c: one(f"late_codes{c}", [P, (E - first) * P], U32) for c, first in CLOSING_FIRST.items()}
+        late_scales = {c: one(f"late_scales{c}", [P, (E - first) * P], U8) for c, first in CLOSING_FIRST.items()}
+        last_scales = one("last_scales", [P, P + C], U8)
+        operands = {}
         y_last = one("y_last", [P, 1, C], F32)
         closing_width = {c: (E - first) * C for c, first in CLOSING_FIRST.items()}
-        y_closing = {c: one(f"y_closing{c}", [P, width], F32) for c, width in closing_width.items()}
+        y_closing = {1: late_raw[2][:, LATE * PACK * P : LATE * PACK * P + closing_width[1]], 2: one("y_closing2", [P, closing_width[2]], F32)[:]}
         acc1 = [psum.tile([P, PACK, C], F32, name=f"acc1_{i}") for i in range(2)]
         acc2 = [psum.tile([P, ROW_TILES, C], F32, name=f"acc2_{i}") for i in range(2)]
         acc_closing = {c: psum.tile([P, width], F32, name=f"acc_closing{c}") for c, width in closing_width.items()}
@@ -119,17 +130,22 @@ def tile_moe_two_mlp_relu_kernel(
 
         def load_w1(e, o):
             rows = w1[e, o * K_PASS : (o + 1) * K_PASS, :].rearrange("(p j) i -> p (j i)", j=PACK)
-            nc.sync.dma_start(w1_raw[e % W1_RAW_DEPTH][:, o * PACK * H : (o + 1) * PACK * H], rows)
+            nc.sync.dma_start(w1_raw[e % W1_RAW_DEPTH][:, FRONT + o * PACK * H : FRONT + (o + 1) * PACK * H], rows)
 
         def round_w1(e):
-            source = w1_raw[e % W1_RAW_DEPTH][:].rearrange("p (o j m t) -> p o m j t", o=PASSES, j=PACK, t=PACK)
+            source = w1_raw[e % W1_RAW_DEPTH][:, FRONT:].rearrange("p (o j m t) -> p o m j t", o=PASSES, j=PACK, t=PACK)
             target = w1_bf16[e % W1_BF16_DEPTH][:].rearrange("p (o t m j) -> p o m j t", o=PASSES, j=PACK, t=PACK)
             cut0 = P - BOTH_PASSES
             cut1 = cut0 - PASS1_SHARES[e]
-            nc.scalar.activation(target[:, 0, 0:cut0], source[:, 0, 0:cut0], COPY)
+            if e == LAST:
+                cut = cut0 - LAST_PASS0_SHARE
+                nc.scalar.activation(target[:, 0, 0:cut], source[:, 0, 0:cut], COPY)
+                nc.vector.tensor_copy(target[:, 0, cut:cut0], source[:, 0, cut:cut0])
+            else:
+                nc.scalar.activation(target[:, 0, 0:cut0], source[:, 0, 0:cut0], COPY)
             nc.scalar.activation(target[:, 1, 0:cut1], source[:, 1, 0:cut1], COPY)
-            nc.vector.tensor_copy(target[:, 1, cut1:cut0], source[:, 1, cut1:cut0])
             nc.vector.tensor_copy(target[:, :, cut0:P], source[:, :, cut0:P])
+            nc.vector.tensor_copy(target[:, 1, cut1:cut0], source[:, 1, cut1:cut0])
 
         def w1_slot(e, o):
             return e % W1_CODE_DEPTH * PASSES + o
@@ -147,17 +163,17 @@ def tile_moe_two_mlp_relu_kernel(
 
         def first_matmuls(e):
             slots = slice(e * C, (e + 1) * C)
-            for t in range(PACK):
-                cols = slice(t * P, (t + 1) * P)
-                for o in range(PASSES):
+            for o in range(PASSES):
+                for t in range(PACK):
+                    cols = slice(t * P, (t + 1) * P)
                     nc.tensor.matmul_mx(
                         out=acc1[e % 2][:, t, :],
                         lhsT=w1_codes[w1_slot(e, o)][:, cols].bitcast(FP8X4),
                         lhsT_scale=w1_scales[w1_slot(e, o)][:, cols],
                         rhs=slot_words[o][:, slots].bitcast(FP8X4),
                         rhs_scale=slot_scales[SCALE_ROWS * o : P, slots],
-                        start=(o == 0),
-                        stop=(o == PASSES - 1),
+                        start=(o == 0 and t == 0),
+                        stop=(o == PASSES - 1 and t == PACK - 1),
                     )
 
         def warm_up(e):
@@ -180,9 +196,7 @@ def tile_moe_two_mlp_relu_kernel(
             )
 
         def raw_w2(e):
-            if e < EARLY:
-                return w2_raw[e % W2_RAW_DEPTH][:]
-            return late_raw[:, (e - EARLY) * PACK * N : (e - EARLY + 1) * PACK * N]
+            return w2_raw[e % W2_RAW_DEPTH][:]
 
         def load_w2(e, c0, c1):
             cols = slice(c0 * P, c1 * P)
@@ -204,6 +218,27 @@ def tile_moe_two_mlp_relu_kernel(
                 in_=values,
             )
 
+        def late_piece(e, c):
+            if (e, c) == (LAST, 0):
+                return last_stage[:, P * PACK // 2 :]
+            place = e - late_first[c]
+            return late_raw[c][:, place * PACK * P : (place + 1) * PACK * P]
+
+        def load_late(e, c):
+            rows = w2[e].rearrange("(p j) n -> p j n", j=PACK)[:, :, c * P : (c + 1) * P]
+            nc.sync.dma_start(late_piece(e, c).rearrange("p (j n) -> p j n", j=PACK), rows)
+
+        def late_views(e, c, values):
+            target = values.rearrange("p (g n j) -> p g j n", n=RUN, j=PACK)
+            return target, late_piece(e, c).rearrange("p (j g n) -> p g j n", j=PACK, n=RUN)
+
+        def quantize_late(c, first, end):
+            nc.vector.quantize_mx(
+                out=late_codes[c][:, first:end].bitcast(FP8X4),
+                scales=late_scales[c][:, first:end],
+                in_=late_bf16[c][:, first * PACK : end * PACK],
+            )
+
         def closing(e, c):
             return c in CLOSING_FIRST and e >= CLOSING_FIRST[c]
 
@@ -214,14 +249,16 @@ def tile_moe_two_mlp_relu_kernel(
             else:
                 sums = acc2[e % 2][:, c, :]
             codes, scales, first = w2h_codes[e % W2H_DEPTH], w2h_scales[e % W2H_DEPTH], C + c * P
-            if e >= EARLY and c == ROW_TILES - 1:
-                codes, scales, first = late_codes, late_scales, (e - EARLY) * P
+            if closing(e, c):
+                codes, scales, first = late_codes[c], late_scales[c], (e - CLOSING_FIRST[c]) * P
+            weights = operands.get((e, c), (codes[:, first : first + P], scales[:, first : first + P]))
+            h = operands.get((e, "h"), (w2h_codes[e % W2H_DEPTH][:, 0:C], w2h_scales[e % W2H_DEPTH][:, 0:C]))
             nc.tensor.matmul_mx(
                 out=sums,
-                lhsT=codes[:, first : first + P].bitcast(FP8X4),
-                lhsT_scale=scales[:, first : first + P],
-                rhs=w2h_codes[e % W2H_DEPTH][:, 0:C].bitcast(FP8X4),
-                rhs_scale=w2h_scales[e % W2H_DEPTH][:, 0:C],
+                lhsT=weights[0].bitcast(FP8X4),
+                lhsT_scale=weights[1],
+                rhs=h[0].bitcast(FP8X4),
+                rhs_scale=h[1],
                 start=True,
                 stop=True,
             )
@@ -264,10 +301,11 @@ def tile_moe_two_mlp_relu_kernel(
                 load_w1(e, o)
             if e == 0:
                 nc.sync.dma_start(dst_list[:], dst)
-            if e < EARLY:
-                load_w2(e, 0, ROW_TILES)
+            tiles = len([c for c in range(ROW_TILES) if e < late_first[c]])
+            if tiles:
+                load_w2(e, 0, tiles)
             round_w1(e)
-            pass1_raw = w1_raw[e % W1_RAW_DEPTH][:, PACK * H :].rearrange("p (j i) -> p j i", j=PACK)
+            pass1_raw = w1_raw[e % W1_RAW_DEPTH][:, FRONT + PACK * H :].rearrange("p (j i) -> p j i", j=PACK)
             due = [c for c in range(ROW_TILES) if 0 < e <= EARLY and not closing(e - 1, c)]
             if due:
                 y = pass1_raw[:, 0 : len(due), Y_COLUMN : Y_COLUMN + C]
@@ -280,47 +318,55 @@ def tile_moe_two_mlp_relu_kernel(
             for c in due:
                 scatter_one(e - 1, c, y[:, c, :])
             if e < EARLY:
-                nc.scalar.activation(*w2_views(e, 0, ROW_TILES, w2h_values(e, C, C + N)), COPY)
+                nc.scalar.activation(*w2_views(e, 0, tiles, w2h_values(e, C, C + tiles * P)), COPY)
                 relu_h(e, w2h_values(e, 0, C))
-                quantize_w2h(e, 0, C + N, w2h_values(e, 0, C + N))
-                for c in range(ROW_TILES):
+                if tiles == ROW_TILES:
+                    quantize_w2h(e, 0, C + N, w2h_values(e, 0, C + N))
+                else:
+                    quantize_w2h(e, C + P, C + 2 * P, w2h_values(e, C + P, C + 2 * P))
+                    quantize_w2h(e, 0, C + P, w2h_values(e, 0, C + P))
+                for c in range(tiles):
                     second_matmul(e, c)
 
-        load_w2(BEFORE_LAST, 0, ROW_TILES)
-        load_w2(LAST, 0, 1)
-        load_w2(LAST, 1, ROW_TILES)
-        h_before = pass1_raw[:, PACK - 1, 0 : C * PACK // 2].bitcast(BF16)
-        relu_h(BEFORE_LAST, h_before)
-        quantize_w2h(BEFORE_LAST, 0, C, h_before)
-        tile0 = w2h_values(BEFORE_LAST, C, C + P)
-        tile1 = w2h_values(BEFORE_LAST, C + P, C + 2 * P)
-        nc.scalar.activation(*w2_views(BEFORE_LAST, 0, 1, tile0), COPY)
-        quantize_w2h(BEFORE_LAST, C, C + P, tile0)
+        for c in range(ROW_TILES):
+            for e in range(late_first[c], E):
+                load_late(e, c)
+        before_values = w1_raw[LAST % W1_RAW_DEPTH][:, 0 : 2 * FRONT].bitcast(BF16)
+        relu_h(BEFORE_LAST, before_values[:, P * PACK :])
+        nc.scalar.activation(*late_views(BEFORE_LAST, 0, before_values[:, 0 : P * PACK]), COPY)
+        last_values = last_stage[:, 0 : (P + C) * PACK // 2].bitcast(BF16)
+        nc.scalar.activation(*late_views(LAST, 0, last_values[:, 0 : P * PACK]), COPY)
+        quantize_w2h(BEFORE_LAST, 0, P + C, before_values)
+        codes, scales = w2h_codes[BEFORE_LAST % W2H_DEPTH], w2h_scales[BEFORE_LAST % W2H_DEPTH]
+        operands[BEFORE_LAST, 0] = (codes[:, 0:P], scales[:, 0:P])
+        operands[BEFORE_LAST, "h"] = (codes[:, P : P + C], scales[:, P : P + C])
         second_matmul(BEFORE_LAST, 0)
-        nc.scalar.activation(*w2_views(BEFORE_LAST, 1, 2, tile1), COPY)
-        quantize_w2h(BEFORE_LAST, C + P, C + 2 * P, tile1)
-        nc.vector.tensor_copy(*w2_views(LAST, 0, 1, tile0))
-        y_before = tile1[:, 0 : 2 * C].bitcast(F32).rearrange("p (c s) -> p c s", c=1)
-        times_gate(BEFORE_LAST, y_before)
-        relu_h(LAST, w2h_values(BEFORE_LAST, 0, C))
-        quantize_w2h(LAST, 0, C + P, w2h_values(BEFORE_LAST, 0, C + P))
-        scatter_one(BEFORE_LAST, 0, y_before[:, 0, :])
+        relu_h(LAST, last_values[:, P * PACK :])
+        nc.vector.tensor_copy(
+            late_bf16[1][:].rearrange("p (e g n j) -> p e g j n", e=LATE, n=RUN, j=PACK),
+            late_raw[1][:].rearrange("p (e j g n) -> p e g j n", e=LATE, j=PACK, n=RUN),
+        )
+        y_before = shared.tile([P, 1, C], F32, name="y_before", align_bytes=ALIGN, offset=0)
+        last_codes = shared.tile([P, P + C], U32, name="last_codes", align_bytes=ALIGN, offset=4 * C)
+        times_gate(BEFORE_LAST, y_before[:])
+        quantize_late(1, 0, LATE * P)
+        nc.vector.quantize_mx(out=last_codes[:].bitcast(FP8X4), scales=last_scales[:], in_=last_values)
+        operands[LAST, 0] = (last_codes[:, 0:P], last_scales[:, 0:P])
+        operands[LAST, "h"] = (last_codes[:, P:], last_scales[:, P:])
         second_matmul(LAST, 0)
-        last_tile1 = w2h_values(LAST, C + P, C + 2 * P)
-        nc.scalar.activation(*w2_views(LAST, 1, 2, last_tile1), COPY)
-        quantize_w2h(LAST, C + P, C + 2 * P, last_tile1)
+        scatter_one(BEFORE_LAST, 0, y_before[:, 0, :])
         times_gate(LAST, y_last[:])
         scatter_one(LAST, 0, y_last[:, 0, :])
-        nc.scalar.copy(
-            late_bf16[:].rearrange("p (e g n j) -> p e g j n", e=LATE, n=RUN, j=PACK),
-            late_raw[:].rearrange("p (e j g n) -> p e g j n", e=LATE, j=PACK, n=RUN)[:, :, 2 * P // RUN :],
-        )
-        nc.vector.quantize_mx(out=late_codes[:].bitcast(FP8X4), scales=late_scales[:], in_=late_bf16[:])
         store(0)
+        for e in range(late_first[2], E):
+            place = e - late_first[2]
+            nc.scalar.activation(*late_views(e, 2, late_bf16[2][:, place * PACK * P : (place + 1) * PACK * P]), COPY)
+        quantize_late(2, 0, LATE * P)
+        quantize_late(2, LATE * P, (LATE + 1) * P)
 
         for c, first in CLOSING_FIRST.items():
-            for e in range(EARLY, E):
+            for e in range(first, E):
                 second_matmul(e, c)
-            nc.scalar.copy(y_closing[c][:], acc_closing[c][:])
-            nc.vector.tensor_tensor(places(c, first, E), y_closing[c][:], gate_sb[:, first * C : E * C], MULT)
+            nc.scalar.copy(y_closing[c], acc_closing[c][:])
+            nc.vector.tensor_tensor(places(c, first, E), y_closing[c], gate_sb[:, first * C : E * C], MULT)
             store(c)

@@ -44,7 +44,7 @@ W2H_DEPTH = 4
 
 BOTH_PASSES = 8
 FIRST_SHARE = 96
-STREAM_SHARE = 80
+STREAM_SHARE = 68
 BEFORE_LAST_SHARE = 72
 LAST_SHARE = 60
 LAST_PASS0_SHARE = 36

@@ -35,6 +35,8 @@ LATE = 2
 EARLY = E - LATE
 BEFORE_LAST, LAST = E - 2, E - 1
 CLOSING_FIRST = {1: EARLY, 2: EARLY - 1}
+LATE_FIRST = {0: EARLY, **CLOSING_FIRST}
+PIECE = PACK * P
 
 W1_RAW_DEPTH = 4
 W1_BF16_DEPTH = 2
@@ -50,8 +52,7 @@ LAST_SHARE = 60
 LAST_PASS0_SHARE = 36
 PASS1_SHARES = (FIRST_SHARE,) + (STREAM_SHARE,) * (EARLY - 1) + (BEFORE_LAST_SHARE, LAST_SHARE)
 Y_COLUMN = 320
-WARM_UPS = 4
-FRONT = P * PACK // 2
+FRONT = PIECE // 2
 
 
 def tile_moe_two_mlp_relu_kernel(
@@ -88,25 +89,22 @@ def tile_moe_two_mlp_relu_kernel(
         w2h_bf16 = ring("w2h_bf16", W2H_DEPTH, [P, (C + N) * PACK], BF16)
         w2h_codes = ring("w2h_codes", W2H_DEPTH, [P, C + N], U32)
         w2h_scales = ring("w2h_scales", W2H_DEPTH, [P, C + N], U8)
-        late_first = {0: EARLY, **CLOSING_FIRST}
-        last_stage = one("late_stage", [P, P * PACK // 2 + P * PACK], F32)
+        late_stage = one("late_stage", [P, FRONT + PIECE], F32)
         late_raw = {
-            0: one("late_raw0", [P, PACK * P], F32),
-            1: shared.tile([P, LATE * PACK * P], F32, name="late_raw1", align_bytes=ALIGN, offset=0),
-            2: one("late_raw2", [P, (LATE + 1) * PACK * P], F32),
+            0: one("late_raw0", [P, PIECE], F32),
+            1: shared.tile([P, (E - LATE_FIRST[1]) * PIECE], F32, name="late_raw1", align_bytes=ALIGN, offset=0),
+            2: one("late_raw2", [P, (E - LATE_FIRST[2]) * PIECE], F32),
         }
-        late_bf16 = {c: one(f"late_bf16{c}", [P, (E - first) * P * PACK], BF16) for c, first in CLOSING_FIRST.items()}
+        late_bf16 = {c: one(f"late_bf16{c}", [P, (E - first) * PIECE], BF16) for c, first in CLOSING_FIRST.items()}
         late_codes = {c: one(f"late_codes{c}", [P, (E - first) * P], U32) for c, first in CLOSING_FIRST.items()}
         late_scales = {c: one(f"late_scales{c}", [P, (E - first) * P], U8) for c, first in CLOSING_FIRST.items()}
         last_scales = one("last_scales", [P, P + C], U8)
-        operands = {}
         y_last = one("y_last", [P, 1, C], F32)
         closing_width = {c: (E - first) * C for c, first in CLOSING_FIRST.items()}
-        y_closing = {1: late_raw[2][:, LATE * PACK * P : LATE * PACK * P + closing_width[1]], 2: one("y_closing2", [P, closing_width[2]], F32)[:]}
+        y_closing2 = one("y_closing2", [P, closing_width[2]], F32)
         acc1 = [psum.tile([P, PACK, C], F32, name=f"acc1_{i}") for i in range(2)]
         acc2 = [psum.tile([P, ROW_TILES, C], F32, name=f"acc2_{i}") for i in range(2)]
         acc_closing = {c: psum.tile([P, width], F32, name=f"acc_closing{c}") for c, width in closing_width.items()}
-        unread = psum.tile([P, K_PASS], F32, name="unread")
 
         def load_words(o):
             nc.sync.dma_start(tok_words[o][:], x_words[o].rearrange("p t r -> p (t r)").bitcast(I32))
@@ -176,18 +174,6 @@ def tile_moe_two_mlp_relu_kernel(
                         stop=(o == PASSES - 1 and t == PACK - 1),
                     )
 
-        def warm_up(e):
-            for n in range(WARM_UPS):
-                nc.tensor.matmul_mx(
-                    out=unread[:],
-                    lhsT=w1_codes[w1_slot(e, 1)][:, H - P : H].bitcast(FP8X4),
-                    lhsT_scale=w1_scales[w1_slot(e, 1)][:, H - P : H],
-                    rhs=slot_words[0][:, 0:K_PASS].bitcast(FP8X4),
-                    rhs_scale=slot_scales[:, 0:K_PASS],
-                    start=True,
-                    stop=True,
-                )
-
         def relu_h(e, h):
             nc.scalar.activation(
                 h.rearrange("p (s t) -> p s t", t=PACK),
@@ -195,21 +181,20 @@ def tile_moe_two_mlp_relu_kernel(
                 RELU,
             )
 
-        def raw_w2(e):
-            return w2_raw[e % W2_RAW_DEPTH][:]
+        def w2_rows(e, first, end):
+            return w2[e].rearrange("(p j) n -> p j n", j=PACK)[:, :, first * P : end * P]
 
-        def load_w2(e, c0, c1):
-            cols = slice(c0 * P, c1 * P)
-            rows = w2[e].rearrange("(p j) n -> p j n", j=PACK)
-            nc.sync.dma_start(raw_w2(e).rearrange("p (j n) -> p j n", j=PACK)[:, :, cols], rows[:, :, cols])
+        def load_w2(e, tiles):
+            raw = w2_raw[e % W2_RAW_DEPTH][:].rearrange("p (j n) -> p j n", j=PACK)
+            nc.sync.dma_start(raw[:, :, 0 : tiles * P], w2_rows(e, 0, tiles))
 
         def w2h_values(e, first, end):
             return w2h_bf16[e % W2H_DEPTH][:, first * PACK : end * PACK]
 
-        def w2_views(e, c0, c1, values):
+        def round_w2(values, raw, tiles):
             target = values.rearrange("p (g n j) -> p g j n", n=RUN, j=PACK)
-            source = raw_w2(e).rearrange("p (j g n) -> p g j n", j=PACK, n=RUN)
-            return target, source[:, c0 * P // RUN : c1 * P // RUN]
+            source = raw.rearrange("p (j g n) -> p g j n", j=PACK, n=RUN)
+            nc.scalar.activation(target, source[:, 0 : tiles * P // RUN], COPY)
 
         def quantize_w2h(e, first, end, values):
             nc.vector.quantize_mx(
@@ -220,17 +205,12 @@ def tile_moe_two_mlp_relu_kernel(
 
         def late_piece(e, c):
             if (e, c) == (LAST, 0):
-                return last_stage[:, P * PACK // 2 :]
-            place = e - late_first[c]
-            return late_raw[c][:, place * PACK * P : (place + 1) * PACK * P]
+                return late_stage[:, FRONT:]
+            place = e - LATE_FIRST[c]
+            return late_raw[c][:, place * PIECE : (place + 1) * PIECE]
 
         def load_late(e, c):
-            rows = w2[e].rearrange("(p j) n -> p j n", j=PACK)[:, :, c * P : (c + 1) * P]
-            nc.sync.dma_start(late_piece(e, c).rearrange("p (j n) -> p j n", j=PACK), rows)
-
-        def late_views(e, c, values):
-            target = values.rearrange("p (g n j) -> p g j n", n=RUN, j=PACK)
-            return target, late_piece(e, c).rearrange("p (j g n) -> p g j n", j=PACK, n=RUN)
+            nc.sync.dma_start(late_piece(e, c).rearrange("p (j n) -> p j n", j=PACK), w2_rows(e, c, c + 1))
 
         def quantize_late(c, first, end):
             nc.vector.quantize_mx(
@@ -242,23 +222,24 @@ def tile_moe_two_mlp_relu_kernel(
         def closing(e, c):
             return c in CLOSING_FIRST and e >= CLOSING_FIRST[c]
 
+        quantised = {e: (w2h_codes[e % W2H_DEPTH], w2h_scales[e % W2H_DEPTH]) for e in range(LAST)}
+
         def second_matmul(e, c):
+            h_codes, h_scales = quantised[e]
+            h_first = 0 if e < EARLY else P
             if closing(e, c):
                 place = e - CLOSING_FIRST[c]
                 sums = acc_closing[c][:, place * C : (place + 1) * C]
+                codes, scales, first = late_codes[c], late_scales[c], place * P
             else:
                 sums = acc2[e % 2][:, c, :]
-            codes, scales, first = w2h_codes[e % W2H_DEPTH], w2h_scales[e % W2H_DEPTH], C + c * P
-            if closing(e, c):
-                codes, scales, first = late_codes[c], late_scales[c], (e - CLOSING_FIRST[c]) * P
-            weights = operands.get((e, c), (codes[:, first : first + P], scales[:, first : first + P]))
-            h = operands.get((e, "h"), (w2h_codes[e % W2H_DEPTH][:, 0:C], w2h_scales[e % W2H_DEPTH][:, 0:C]))
+                codes, scales, first = h_codes, h_scales, (C + c * P if e < EARLY else 0)
             nc.tensor.matmul_mx(
                 out=sums,
-                lhsT=weights[0].bitcast(FP8X4),
-                lhsT_scale=weights[1],
-                rhs=h[0].bitcast(FP8X4),
-                rhs_scale=h[1],
+                lhsT=codes[:, first : first + P].bitcast(FP8X4),
+                lhsT_scale=scales[:, first : first + P],
+                rhs=h_codes[:, h_first : h_first + C].bitcast(FP8X4),
+                rhs_scale=h_scales[:, h_first : h_first + C],
                 start=True,
                 stop=True,
             )
@@ -301,24 +282,22 @@ def tile_moe_two_mlp_relu_kernel(
                 load_w1(e, o)
             if e == 0:
                 nc.sync.dma_start(dst_list[:], dst)
-            tiles = len([c for c in range(ROW_TILES) if e < late_first[c]])
+            tiles = len([c for c in range(ROW_TILES) if e < LATE_FIRST[c]])
             if tiles:
-                load_w2(e, 0, tiles)
+                load_w2(e, tiles)
             round_w1(e)
-            pass1_raw = w1_raw[e % W1_RAW_DEPTH][:, FRONT + PACK * H :].rearrange("p (j i) -> p j i", j=PACK)
             due = [c for c in range(ROW_TILES) if 0 < e <= EARLY and not closing(e - 1, c)]
             if due:
+                pass1_raw = w1_raw[e % W1_RAW_DEPTH][:, FRONT + PACK * H :].rearrange("p (j i) -> p j i", j=PACK)
                 y = pass1_raw[:, 0 : len(due), Y_COLUMN : Y_COLUMN + C]
                 times_gate(e - 1, y)
             quantize_w1(e, 0, 1)
             quantize_w1(e, 1, PACK if e == LAST else 2)
             first_matmuls(e)
-            if e == BEFORE_LAST:
-                warm_up(e)
             for c in due:
                 scatter_one(e - 1, c, y[:, c, :])
             if e < EARLY:
-                nc.scalar.activation(*w2_views(e, 0, tiles, w2h_values(e, C, C + tiles * P)), COPY)
+                round_w2(w2h_values(e, C, C + tiles * P), w2_raw[e % W2_RAW_DEPTH][:], tiles)
                 relu_h(e, w2h_values(e, 0, C))
                 if tiles == ROW_TILES:
                     quantize_w2h(e, 0, C + N, w2h_values(e, 0, C + N))
@@ -329,41 +308,40 @@ def tile_moe_two_mlp_relu_kernel(
                     second_matmul(e, c)
 
         for c in range(ROW_TILES):
-            for e in range(late_first[c], E):
+            for e in range(LATE_FIRST[c], E):
                 load_late(e, c)
+
         before_values = w1_raw[LAST % W1_RAW_DEPTH][:, 0 : 2 * FRONT].bitcast(BF16)
-        relu_h(BEFORE_LAST, before_values[:, P * PACK :])
-        nc.scalar.activation(*late_views(BEFORE_LAST, 0, before_values[:, 0 : P * PACK]), COPY)
-        last_values = last_stage[:, 0 : (P + C) * PACK // 2].bitcast(BF16)
-        nc.scalar.activation(*late_views(LAST, 0, last_values[:, 0 : P * PACK]), COPY)
+        last_values = late_stage[:, 0 : 2 * FRONT].bitcast(BF16)
+        relu_h(BEFORE_LAST, before_values[:, PIECE:])
+        round_w2(before_values[:, 0:PIECE], late_piece(BEFORE_LAST, 0), 1)
+        round_w2(last_values[:, 0:PIECE], late_piece(LAST, 0), 1)
         quantize_w2h(BEFORE_LAST, 0, P + C, before_values)
-        codes, scales = w2h_codes[BEFORE_LAST % W2H_DEPTH], w2h_scales[BEFORE_LAST % W2H_DEPTH]
-        operands[BEFORE_LAST, 0] = (codes[:, 0:P], scales[:, 0:P])
-        operands[BEFORE_LAST, "h"] = (codes[:, P : P + C], scales[:, P : P + C])
         second_matmul(BEFORE_LAST, 0)
-        relu_h(LAST, last_values[:, P * PACK :])
+        relu_h(LAST, last_values[:, PIECE:])
         nc.vector.tensor_copy(
             late_bf16[1][:].rearrange("p (e g n j) -> p e g j n", e=LATE, n=RUN, j=PACK),
             late_raw[1][:].rearrange("p (e j g n) -> p e g j n", e=LATE, j=PACK, n=RUN),
         )
         y_before = shared.tile([P, 1, C], F32, name="y_before", align_bytes=ALIGN, offset=0)
         last_codes = shared.tile([P, P + C], U32, name="last_codes", align_bytes=ALIGN, offset=4 * C)
+        quantised[LAST] = (last_codes, last_scales)
         times_gate(BEFORE_LAST, y_before[:])
         quantize_late(1, 0, LATE * P)
         nc.vector.quantize_mx(out=last_codes[:].bitcast(FP8X4), scales=last_scales[:], in_=last_values)
-        operands[LAST, 0] = (last_codes[:, 0:P], last_scales[:, 0:P])
-        operands[LAST, "h"] = (last_codes[:, P:], last_scales[:, P:])
         second_matmul(LAST, 0)
         scatter_one(BEFORE_LAST, 0, y_before[:, 0, :])
         times_gate(LAST, y_last[:])
         scatter_one(LAST, 0, y_last[:, 0, :])
         store(0)
-        for e in range(late_first[2], E):
-            place = e - late_first[2]
-            nc.scalar.activation(*late_views(e, 2, late_bf16[2][:, place * PACK * P : (place + 1) * PACK * P]), COPY)
-        quantize_late(2, 0, LATE * P)
-        quantize_late(2, LATE * P, (LATE + 1) * P)
 
+        for e in range(LATE_FIRST[2], E):
+            place = e - LATE_FIRST[2]
+            round_w2(late_bf16[2][:, place * PIECE : (place + 1) * PIECE], late_piece(e, 2), 1)
+        quantize_late(2, 0, 2 * P)
+        quantize_late(2, 2 * P, 3 * P)
+
+        y_closing = {1: late_piece(LAST, 2)[:, 0 : closing_width[1]], 2: y_closing2[:]}
         for c, first in CLOSING_FIRST.items():
             for e in range(first, E):
                 second_matmul(e, c)

@@ -30,29 +30,25 @@ QUADRANT = 32
 SCALE_ROWS = 4
 RUN = 4
 ALIGN = 256
-
-LATE = 2
-EARLY = E - LATE
-BEFORE_LAST, LAST = E - 2, E - 1
-CLOSING_FIRST = {1: EARLY, 2: EARLY - 1}
-LATE_FIRST = {0: EARLY, **CLOSING_FIRST}
+UNIT = PACK * H
 PIECE = PACK * P
-
-W1_RAW_DEPTH = 4
-W1_BF16_DEPTH = 2
-W1_CODE_DEPTH = 3
+SLOTS = 4
+CODE_DEPTH = 6
 W2_RAW_DEPTH = 3
 W2H_DEPTH = 4
-
-BOTH_PASSES = 8
-FIRST_SHARE = 96
-STREAM_SHARE = 68
-BEFORE_LAST_SHARE = 72
-LAST_SHARE = 60
-LAST_PASS0_SHARE = 36
-PASS1_SHARES = (FIRST_SHARE,) + (STREAM_SHARE,) * (EARLY - 1) + (BEFORE_LAST_SHARE, LAST_SHARE)
+HOLD = 8
+CUT1 = (24, 52, 52, 52, 52, 68)
+CUT0 = (80, 80, 80, 80, 88, 88)
+CUT0_6 = 88
+CUT0_7 = 60
+CUT_A = 64
+CUT1_6 = 112
+V60 = True
+CUT_B = 84
+EARLY0 = (120, 120, 120, 120, 120, 96)
 Y_COLUMN = 320
-FRONT = PIECE // 2
+STREAM = 6
+WHOLE = 0
 
 
 def tile_moe_two_mlp_relu_kernel(
@@ -81,30 +77,28 @@ def tile_moe_two_mlp_relu_kernel(
         gate_sb = one("gate_sb", [P, S], F32)
         zeros = one("zeros", [P, C], F32)
         out_sb = ring("out_sb", ROW_TILES, [P, T], F32)
-        w1_raw = ring("w1_raw", W1_RAW_DEPTH, [P, FRONT + PASSES * PACK * H], F32)
-        w1_bf16 = ring("w1_bf16", W1_BF16_DEPTH, [P, PASSES * H * PACK], BF16)
-        w1_codes = ring("w1_codes", W1_CODE_DEPTH * PASSES, [P, H], U32)
-        w1_scales = ring("w1_scales", W1_CODE_DEPTH * PASSES, [P, H], U8)
+        w1_raw = ring("w1_raw", 2, [P, SLOTS * UNIT], F32)
+        w1_bf16 = one("w1_bf16", [P, SLOTS * UNIT], BF16)
+        w1_codes = ring("w1_codes", CODE_DEPTH, [P, H], U32)
+        w1_scales = ring("w1_scales", CODE_DEPTH, [P, H], U8)
         w2_raw = ring("w2_raw", W2_RAW_DEPTH, [P, PACK * N], F32)
         w2h_bf16 = ring("w2h_bf16", W2H_DEPTH, [P, (C + N) * PACK], BF16)
         w2h_codes = ring("w2h_codes", W2H_DEPTH, [P, C + N], U32)
         w2h_scales = ring("w2h_scales", W2H_DEPTH, [P, C + N], U8)
-        late_stage = one("late_stage", [P, FRONT + PIECE], F32)
-        late_raw = {
-            0: one("late_raw0", [P, PIECE], F32),
-            1: shared.tile([P, (E - LATE_FIRST[1]) * PIECE], F32, name="late_raw1", align_bytes=ALIGN, offset=0),
-            2: one("late_raw2", [P, (E - LATE_FIRST[2]) * PIECE], F32),
-        }
-        late_bf16 = {c: one(f"late_bf16{c}", [P, (E - first) * PIECE], BF16) for c, first in CLOSING_FIRST.items()}
-        late_codes = {c: one(f"late_codes{c}", [P, (E - first) * P], U32) for c, first in CLOSING_FIRST.items()}
-        late_scales = {c: one(f"late_scales{c}", [P, (E - first) * P], U8) for c, first in CLOSING_FIRST.items()}
+        late = [(6, 0), (7, 0), (6, 1), (7, 1), (5, 2), (6, 2), (7, 2)]
+        late_raw = {ec: one("late_raw%d%d" % ec, [P, PIECE], F32)[:] for ec in late if ec not in ((7, 0), (6, 1))}
+        stage70 = one("stage70", [P, PIECE // 2 + PIECE], F32)
+        late_raw[7, 0] = stage70[:, PIECE // 2 :]
+        late_raw[6, 1] = shared.tile([P, PIECE], F32, name="late_raw61", align_bytes=ALIGN, offset=0)[:]
         last_scales = one("last_scales", [P, P + C], U8)
-        y_last = one("y_last", [P, 1, C], F32)
-        closing_width = {c: (E - first) * C for c, first in CLOSING_FIRST.items()}
-        y_closing2 = one("y_closing2", [P, closing_width[2]], F32)
+        first = {1: 6, 2: 5}
+        late_bf16 = {c: one(f"late_bf16{c}", [P, (E - f) * PIECE], BF16) for c, f in first.items()}
+        late_codes = {c: one(f"late_codes{c}", [P, (E - f) * P], U32) for c, f in first.items()}
+        late_scales = {c: one(f"late_scales{c}", [P, (E - f) * P], U8) for c, f in first.items()}
+        y_closing2 = one("y_closing2", [P, (E - first[2]) * C], F32)
         acc1 = [psum.tile([P, PACK, C], F32, name=f"acc1_{i}") for i in range(2)]
         acc2 = [psum.tile([P, ROW_TILES, C], F32, name=f"acc2_{i}") for i in range(2)]
-        acc_closing = {c: psum.tile([P, width], F32, name=f"acc_closing{c}") for c, width in closing_width.items()}
+        acc_closing = {c: psum.tile([P, (E - f) * C], F32, name=f"acc_closing{c}") for c, f in first.items()}
 
         def load_words(o):
             nc.sync.dma_start(tok_words[o][:], x_words[o].rearrange("p t r -> p (t r)").bitcast(I32))
@@ -126,53 +120,70 @@ def tile_moe_two_mlp_relu_kernel(
                     nc.tensor.transpose(bank[:, q, :], gate_row[:, column : column + 1].to_broadcast([P, P]), identity[:])
                 nc.scalar.copy(by_slot[:, :, half * PACK : (half + 1) * PACK], bank[:].rearrange("p q n -> p n q"))
 
-        def load_w1(e, o):
-            rows = w1[e, o * K_PASS : (o + 1) * K_PASS, :].rearrange("(p j) i -> p (j i)", j=PACK)
-            nc.sync.dma_start(w1_raw[e % W1_RAW_DEPTH][:, FRONT + o * PACK * H : FRONT + (o + 1) * PACK * H], rows)
+        def raw(g, count=1):
+            return w1_raw[g // SLOTS % 2][:, g % SLOTS * UNIT : (g % SLOTS + count) * UNIT]
 
-        def round_w1(e):
-            source = w1_raw[e % W1_RAW_DEPTH][:, FRONT:].rearrange("p (o j m t) -> p o m j t", o=PASSES, j=PACK, t=PACK)
-            target = w1_bf16[e % W1_BF16_DEPTH][:].rearrange("p (o t m j) -> p o m j t", o=PASSES, j=PACK, t=PACK)
-            cut0 = P - BOTH_PASSES
-            cut1 = cut0 - PASS1_SHARES[e]
-            if e == LAST:
-                cut = cut0 - LAST_PASS0_SHARE
-                nc.scalar.activation(target[:, 0, 0:cut], source[:, 0, 0:cut], COPY)
-                nc.vector.tensor_copy(target[:, 0, cut:cut0], source[:, 0, cut:cut0])
+        def rounded(g, count=1):
+            return w1_bf16[:, g % SLOTS * UNIT : (g % SLOTS + count) * UNIT]
+
+        def load_w1(g, first_column=0, end_column=H):
+            rows = w1[g // PASSES, g % PASSES * K_PASS : (g % PASSES + 1) * K_PASS, :]
+            if end_column - first_column == H:
+                nc.sync.dma_start(raw(g), rows.rearrange("(p j) i -> p (j i)", j=PACK))
             else:
-                nc.scalar.activation(target[:, 0, 0:cut0], source[:, 0, 0:cut0], COPY)
-            nc.scalar.activation(target[:, 1, 0:cut1], source[:, 1, 0:cut1], COPY)
-            nc.vector.tensor_copy(target[:, :, cut0:P], source[:, :, cut0:P])
-            nc.vector.tensor_copy(target[:, 1, cut1:cut0], source[:, 1, cut1:cut0])
+                nc.sync.dma_start(
+                    raw(g).rearrange("p (j i) -> p j i", j=PACK)[:, :, first_column:end_column],
+                    rows.rearrange("(p j) i -> p j i", j=PACK)[:, :, first_column:end_column],
+                )
 
-        def w1_slot(e, o):
-            return e % W1_CODE_DEPTH * PASSES + o
+        def load_w1_whole(e):
+            nc.sync.dma_start(
+                raw(PASSES * e, PASSES).rearrange("p (o x) -> p o x", o=PASSES),
+                w1[e].rearrange("(o p j) i -> p o (j i)", o=PASSES, j=PACK),
+            )
 
-        def quantize_w1(e, o, parts):
+        def round_w1(on_vector, g, m0, m1, count=1):
+            source = raw(g, count).rearrange("p (o j m t) -> p o m j t", o=count, j=PACK, t=PACK)
+            target = rounded(g, count).rearrange("p (o t m j) -> p o m j t", o=count, j=PACK, t=PACK)
+            if not on_vector:
+                nc.scalar.activation(target[:, 0, m0:m1], source[:, 0, m0:m1], COPY)
+            elif count == 1:
+                nc.vector.tensor_copy(target[:, 0, m0:m1], source[:, 0, m0:m1])
+            else:
+                nc.vector.tensor_copy(target[:, :, m0:m1], source[:, :, m0:m1])
+
+        def codes_of(g):
+            return w1_codes[g % CODE_DEPTH]
+
+        def round_pair(g, m0, m1, t0):
+            source = raw(g).rearrange("p (j m t) -> p m j t", j=PACK, t=PACK)
+            target = rounded(g).rearrange("p (t m j) -> p m j t", j=PACK, t=PACK)
+            nc.vector.tensor_copy(target[:, m0:m1, :, t0 : t0 + 2], source[:, m0:m1, :, t0 : t0 + 2])
+
+        def quantize_w1(g, parts):
             width = H // parts
             for a in range(parts):
                 cols = slice(a * width, (a + 1) * width)
-                first = o * H + a * width
                 nc.vector.quantize_mx(
-                    out=w1_codes[w1_slot(e, o)][:, cols].bitcast(FP8X4),
-                    scales=w1_scales[w1_slot(e, o)][:, cols],
-                    in_=w1_bf16[e % W1_BF16_DEPTH][:, first * PACK : (first + width) * PACK],
+                    out=codes_of(g)[:, cols].bitcast(FP8X4),
+                    scales=w1_scales[g % CODE_DEPTH][:, cols],
+                    in_=rounded(g)[:, a * width * PACK : (a + 1) * width * PACK],
                 )
 
-        def first_matmuls(e):
+        def first_matmuls(g):
+            e, o = divmod(g, PASSES)
             slots = slice(e * C, (e + 1) * C)
-            for o in range(PASSES):
-                for t in range(PACK):
-                    cols = slice(t * P, (t + 1) * P)
-                    nc.tensor.matmul_mx(
-                        out=acc1[e % 2][:, t, :],
-                        lhsT=w1_codes[w1_slot(e, o)][:, cols].bitcast(FP8X4),
-                        lhsT_scale=w1_scales[w1_slot(e, o)][:, cols],
-                        rhs=slot_words[o][:, slots].bitcast(FP8X4),
-                        rhs_scale=slot_scales[SCALE_ROWS * o : P, slots],
-                        start=(o == 0 and t == 0),
-                        stop=(o == PASSES - 1 and t == PACK - 1),
-                    )
+            for t in range(PACK):
+                cols = slice(t * P, (t + 1) * P)
+                nc.tensor.matmul_mx(
+                    out=acc1[e % 2][:, t, :],
+                    lhsT=codes_of(g)[:, cols].bitcast(FP8X4),
+                    lhsT_scale=w1_scales[g % CODE_DEPTH][:, cols],
+                    rhs=slot_words[o][:, slots].bitcast(FP8X4),
+                    rhs_scale=slot_scales[SCALE_ROWS * o : P, slots],
+                    start=(o == 0 and t == 0),
+                    stop=(o == PASSES - 1 and t == PACK - 1),
+                )
 
         def relu_h(e, h):
             nc.scalar.activation(
@@ -181,76 +192,71 @@ def tile_moe_two_mlp_relu_kernel(
                 RELU,
             )
 
-        def w2_rows(e, first, end):
-            return w2[e].rearrange("(p j) n -> p j n", j=PACK)[:, :, first * P : end * P]
+        def w2_rows(e, c0, c1):
+            return w2[e].rearrange("(p j) n -> p j n", j=PACK)[:, :, c0 * P : c1 * P]
 
         def load_w2(e, tiles):
-            raw = w2_raw[e % W2_RAW_DEPTH][:].rearrange("p (j n) -> p j n", j=PACK)
-            nc.sync.dma_start(raw[:, :, 0 : tiles * P], w2_rows(e, 0, tiles))
+            target = w2_raw[e % W2_RAW_DEPTH][:].rearrange("p (j n) -> p j n", j=PACK)
+            nc.sync.dma_start(target[:, :, 0 : tiles * P], w2_rows(e, 0, tiles))
 
-        def w2h_values(e, first, end):
-            return w2h_bf16[e % W2H_DEPTH][:, first * PACK : end * PACK]
+        def w2h_values(e, a, b):
+            return w2h_bf16[e % W2H_DEPTH][:, a * PACK : b * PACK]
 
-        def round_w2(values, raw, tiles):
+        def round_w2(on_vector, values, source, tiles):
             target = values.rearrange("p (g n j) -> p g j n", n=RUN, j=PACK)
-            source = raw.rearrange("p (j g n) -> p g j n", j=PACK, n=RUN)
-            nc.scalar.activation(target, source[:, 0 : tiles * P // RUN], COPY)
+            source = source.rearrange("p (j g n) -> p g j n", j=PACK, n=RUN)[:, 0 : tiles * P // RUN]
+            if on_vector:
+                nc.vector.tensor_copy(target, source)
+            else:
+                nc.scalar.activation(target, source, COPY)
 
-        def quantize_w2h(e, first, end, values):
+        def quantize_w2h(e, a, b):
             nc.vector.quantize_mx(
-                out=w2h_codes[e % W2H_DEPTH][:, first:end].bitcast(FP8X4),
-                scales=w2h_scales[e % W2H_DEPTH][:, first:end],
-                in_=values,
+                out=w2h_codes[e % W2H_DEPTH][:, a:b].bitcast(FP8X4),
+                scales=w2h_scales[e % W2H_DEPTH][:, a:b],
+                in_=w2h_values(e, a, b),
             )
 
-        def late_piece(e, c):
-            if (e, c) == (LAST, 0):
-                return late_stage[:, FRONT:]
-            place = e - LATE_FIRST[c]
-            return late_raw[c][:, place * PIECE : (place + 1) * PIECE]
+        def late_values(e, c):
+            return late_bf16[c][:, (e - first[c]) * PIECE : (e - first[c] + 1) * PIECE]
 
-        def load_late(e, c):
-            nc.sync.dma_start(late_piece(e, c).rearrange("p (j n) -> p j n", j=PACK), w2_rows(e, c, c + 1))
-
-        def quantize_late(c, first, end):
+        def quantize_late(c, e0, e1):
+            a, b = (e0 - first[c]) * P, (e1 - first[c]) * P
             nc.vector.quantize_mx(
-                out=late_codes[c][:, first:end].bitcast(FP8X4),
-                scales=late_scales[c][:, first:end],
-                in_=late_bf16[c][:, first * PACK : end * PACK],
+                out=late_codes[c][:, a:b].bitcast(FP8X4),
+                scales=late_scales[c][:, a:b],
+                in_=late_bf16[c][:, a * PACK : b * PACK],
             )
 
-        def closing(e, c):
-            return c in CLOSING_FIRST and e >= CLOSING_FIRST[c]
-
-        quantised = {e: (w2h_codes[e % W2H_DEPTH], w2h_scales[e % W2H_DEPTH]) for e in range(LAST)}
+        quantised = {e: (w2h_codes[e % W2H_DEPTH], w2h_scales[e % W2H_DEPTH]) for e in range(E - 1)}
 
         def second_matmul(e, c):
             h_codes, h_scales = quantised[e]
-            h_first = 0 if e < EARLY else P
-            if closing(e, c):
-                place = e - CLOSING_FIRST[c]
+            h0 = 0 if e < 6 else P
+            if c in first and e >= first[c]:
+                place = e - first[c]
                 sums = acc_closing[c][:, place * C : (place + 1) * C]
-                codes, scales, first = late_codes[c], late_scales[c], place * P
+                codes, scales, a = late_codes[c], late_scales[c], place * P
             else:
                 sums = acc2[e % 2][:, c, :]
-                codes, scales, first = h_codes, h_scales, (C + c * P if e < EARLY else 0)
+                codes, scales, a = h_codes, h_scales, (C + c * P if e < 6 else 0)
             nc.tensor.matmul_mx(
                 out=sums,
-                lhsT=codes[:, first : first + P].bitcast(FP8X4),
-                lhsT_scale=scales[:, first : first + P],
-                rhs=h_codes[:, h_first : h_first + C].bitcast(FP8X4),
-                rhs_scale=h_scales[:, h_first : h_first + C],
+                lhsT=codes[:, a : a + P].bitcast(FP8X4),
+                lhsT_scale=scales[:, a : a + P],
+                rhs=h_codes[:, h0 : h0 + C].bitcast(FP8X4),
+                rhs_scale=h_scales[:, h0 : h0 + C],
                 start=True,
                 stop=True,
             )
 
-        def places(c, first, end):
-            return out_sb[c][:].indirect(dst_list[:, first * C // LIST_ROWS : end * C // LIST_ROWS])
+        def places(c, e0, e1):
+            return out_sb[c][:].indirect(dst_list[:, e0 * C // LIST_ROWS : e1 * C // LIST_ROWS])
 
-        def times_gate(e, y):
+        def times_gate(e, y, c0=0):
             count = y.shape[1]
             gates = gate_sb[:, e * C : (e + 1) * C].rearrange("p (c s) -> p c s", c=1).to_broadcast([P, count, C])
-            nc.vector.tensor_tensor(y, acc2[e % 2][:, 0:count, :], gates, MULT)
+            nc.vector.tensor_tensor(y, acc2[e % 2][:, c0 : c0 + count, :], gates, MULT)
 
         def scatter_one(e, c, y):
             nc.vector.tensor_tensor(places(c, e, e + 1), y, zeros[:], ADD)
@@ -277,74 +283,133 @@ def tile_moe_two_mlp_relu_kernel(
         make_identity(nc, identity[:])
         spread_gate()
 
-        for e in range(E):
-            for o in range(PASSES):
-                load_w1(e, o)
+        for e in range(6):
+            g = PASSES * e
+            tiles = ROW_TILES if e < 5 else 2
+            if e < WHOLE:
+                load_w1_whole(e)
+            else:
+                load_w1(g)
+                load_w1(g + 1)
             if e == 0:
                 nc.sync.dma_start(dst_list[:], dst)
-            tiles = len([c for c in range(ROW_TILES) if e < LATE_FIRST[c]])
-            if tiles:
-                load_w2(e, tiles)
-            round_w1(e)
-            due = [c for c in range(ROW_TILES) if 0 < e <= EARLY and not closing(e - 1, c)]
-            if due:
-                pass1_raw = w1_raw[e % W1_RAW_DEPTH][:, FRONT + PACK * H :].rearrange("p (j i) -> p j i", j=PACK)
-                y = pass1_raw[:, 0 : len(due), Y_COLUMN : Y_COLUMN + C]
+            load_w2(e, tiles)
+            if e < STREAM:
+                round_w1(False, g, 0, EARLY0[e])
+                if EARLY0[e] < P - HOLD:
+                    round_w1(True, g, EARLY0[e], P - HOLD)
+                round_w1(False, g + 1, 0, CUT1[e])
+                round_w1(True, g, P - HOLD, P, 2)
+                round_w1(True, g + 1, CUT1[e], P - HOLD)
+                early = False
+            else:
+                round_w1(False, g, 0, CUT0[e])
+                round_w1(True, g, CUT0[e], P)
+                quantize_w1(g, 1)
+                first_matmuls(g)
+                round_w1(False, g + 1, 0, CUT1[e])
+                round_w1(True, g + 1, CUT1[e], P)
+                early = True
+            if e > 0:
+                y = raw(g + 1).rearrange("p (j i) -> p j i", j=PACK)[:, 0:ROW_TILES, Y_COLUMN : Y_COLUMN + C]
                 times_gate(e - 1, y)
-            quantize_w1(e, 0, 1)
-            quantize_w1(e, 1, PACK if e == LAST else 2)
-            first_matmuls(e)
-            for c in due:
-                scatter_one(e - 1, c, y[:, c, :])
-            if e < EARLY:
-                round_w2(w2h_values(e, C, C + tiles * P), w2_raw[e % W2_RAW_DEPTH][:], tiles)
-                relu_h(e, w2h_values(e, 0, C))
-                if tiles == ROW_TILES:
-                    quantize_w2h(e, 0, C + N, w2h_values(e, 0, C + N))
-                else:
-                    quantize_w2h(e, C + P, C + 2 * P, w2h_values(e, C + P, C + 2 * P))
-                    quantize_w2h(e, 0, C + P, w2h_values(e, 0, C + P))
-                for c in range(tiles):
-                    second_matmul(e, c)
+            if not early:
+                quantize_w1(g, 1)
+                first_matmuls(g)
+            quantize_w1(g + 1, 2)
+            first_matmuls(g + 1)
+            if e > 0:
+                for c in range(ROW_TILES):
+                    scatter_one(e - 1, c, y[:, c, :])
+            round_w2(False, w2h_values(e, C, C + tiles * P), w2_raw[e % W2_RAW_DEPTH][:], tiles)
+            relu_h(e, w2h_values(e, 0, C))
+            if tiles == ROW_TILES:
+                quantize_w2h(e, 0, C + N)
+            else:
+                quantize_w2h(e, C + P, C + 2 * P)
+                quantize_w2h(e, 0, C + P)
+            for c in range(tiles):
+                second_matmul(e, c)
 
-        for c in range(ROW_TILES):
-            for e in range(LATE_FIRST[c], E):
-                load_late(e, c)
+        load_w1(12)
+        load_w1(13)
+        load_w1(14)
+        load_w1(15, 0, H // 2)
+        load_w1(15, H // 2, H)
+        for e, c in late:
+            nc.sync.dma_start(late_raw[e, c].rearrange("p (j n) -> p j n", j=PACK), w2_rows(e, c, c + 1))
 
-        before_values = w1_raw[LAST % W1_RAW_DEPTH][:, 0 : 2 * FRONT].bitcast(BF16)
-        last_values = late_stage[:, 0 : 2 * FRONT].bitcast(BF16)
-        relu_h(BEFORE_LAST, before_values[:, PIECE:])
-        round_w2(before_values[:, 0:PIECE], late_piece(BEFORE_LAST, 0), 1)
-        round_w2(last_values[:, 0:PIECE], late_piece(LAST, 0), 1)
-        quantize_w2h(BEFORE_LAST, 0, P + C, before_values)
-        second_matmul(BEFORE_LAST, 0)
-        relu_h(LAST, last_values[:, PIECE:])
+        round_w1(False, 12, 0, CUT0_6)
+        if CUT0_6 < P - HOLD:
+            round_w1(True, 12, CUT0_6, P - HOLD)
+        round_w1(False, 13, 0, CUT1_6)
+        round_w1(True, 12, P - HOLD, P, 2)
+        if CUT1_6 < P - 2 * HOLD:
+            round_w1(True, 13, CUT1_6, P - 2 * HOLD)
+        y5 = raw(12).rearrange("p (j i) -> p j i", j=PACK)[:, 0:2, H - C : H]
+        times_gate(5, y5)
+        quantize_w1(12, 1)
+        first_matmuls(12)
+        scatter_one(5, 0, y5[:, 0, :])
+        scatter_one(5, 1, y5[:, 1, :])
+        round_w1(False, 14, 0, CUT0_7)
+        skew = UNIT + PACK * HOLD
+        start = UNIT + PACK * (P - 2 * HOLD)
+        source = w1_raw[1][:, start : start + 2 * skew].rearrange("p (o x) -> p o x", o=2)[:, :, 0:UNIT]
+        source = source.rearrange("p o (j i) -> p o j i", j=PACK)[:, :, :, 0 : PACK * HOLD]
+        target = w1_bf16[:, start : start + 2 * skew].rearrange("p (o x) -> p o x", o=2)[:, :, 0:UNIT]
+        target = target.rearrange("p o (t x) -> p o t x", t=PACK)[:, :, :, 0 : PACK * HOLD]
         nc.vector.tensor_copy(
-            late_bf16[1][:].rearrange("p (e g n j) -> p e g j n", e=LATE, n=RUN, j=PACK),
-            late_raw[1][:].rearrange("p (e j g n) -> p e g j n", e=LATE, j=PACK, n=RUN),
+            target.rearrange("p o t (m j) -> p o m j t", j=PACK), source.rearrange("p o j (m t) -> p o m j t", t=PACK)
         )
-        y_before = shared.tile([P, 1, C], F32, name="y_before", align_bytes=ALIGN, offset=0)
+        round_w1(True, 14, CUT0_7, P - HOLD)
+        quantize_w1(13, 2)
+        first_matmuls(13)
+        round_w1(False, 15, 0, CUT_A)
+        if CUT_A < P // 2:
+            round_w1(True, 15, CUT_A, P // 2)
+        quantize_w1(14, 1)
+        first_matmuls(14)
+        edge = 3 * UNIT + PACK * CUT_B
+        before_values = w1_raw[1][:, edge - PIECE : edge].bitcast(BF16)
+        last_values = stage70[:, 0:PIECE].bitcast(BF16)
+        if CUT_B > P // 2:
+            round_w1(False, 15, P // 2, CUT_B)
+        relu_h(6, before_values[:, PIECE:])
+        round_pair(15, CUT_B, P, 0)
+        round_pair(15, CUT_B, P, 2)
+        quantize_w1(15, PACK)
+        first_matmuls(15)
+        round_w2(V60, before_values[:, 0:PIECE], late_raw[6, 0], 1)
+        nc.vector.quantize_mx(
+            out=w2h_codes[6 % W2H_DEPTH][:, 0 : P + C].bitcast(FP8X4), scales=w2h_scales[6 % W2H_DEPTH][:, 0 : P + C], in_=before_values
+        )
+        second_matmul(6, 0)
+        round_w2(False, last_values[:, 0:PIECE], late_raw[7, 0], 1)
+        relu_h(7, last_values[:, PIECE:])
+        round_w2(True, late_values(6, 1), late_raw[6, 1], 1)
+        y6 = shared.tile([P, 1, C], F32, name="y6", align_bytes=ALIGN, offset=0)
         last_codes = shared.tile([P, P + C], U32, name="last_codes", align_bytes=ALIGN, offset=4 * C)
-        quantised[LAST] = (last_codes, last_scales)
-        times_gate(BEFORE_LAST, y_before[:])
-        quantize_late(1, 0, LATE * P)
+        quantised[7] = (last_codes, last_scales)
+        quantize_late(1, 6, 7)
+        times_gate(6, y6[:])
         nc.vector.quantize_mx(out=last_codes[:].bitcast(FP8X4), scales=last_scales[:], in_=last_values)
-        second_matmul(LAST, 0)
-        scatter_one(BEFORE_LAST, 0, y_before[:, 0, :])
-        times_gate(LAST, y_last[:])
-        scatter_one(LAST, 0, y_last[:, 0, :])
+        second_matmul(7, 0)
+        scatter_one(6, 0, y6[:, 0, :])
+        round_w2(False, late_values(7, 1), late_raw[7, 1], 1)
+        y7 = late_raw[7, 1][:, 0:C].rearrange("p (c s) -> p c s", c=1)
+        times_gate(7, y7)
+        quantize_late(1, 7, 8)
+        scatter_one(7, 0, y7[:, 0, :])
         store(0)
-
-        for e in range(LATE_FIRST[2], E):
-            place = e - LATE_FIRST[2]
-            round_w2(late_bf16[2][:, place * PIECE : (place + 1) * PIECE], late_piece(e, 2), 1)
-        quantize_late(2, 0, 2 * P)
-        quantize_late(2, 2 * P, 3 * P)
-
-        y_closing = {1: late_piece(LAST, 2)[:, 0 : closing_width[1]], 2: y_closing2[:]}
-        for c, first in CLOSING_FIRST.items():
-            for e in range(first, E):
+        for e in range(first[2], E):
+            round_w2(False, late_values(e, 2), late_raw[e, 2], 1)
+        quantize_late(2, 5, 7)
+        quantize_late(2, 7, 8)
+        y_closing = {1: late_raw[7, 2][:, 0 : 2 * C], 2: y_closing2[:]}
+        for c, f in first.items():
+            for e in range(f, E):
                 second_matmul(e, c)
             nc.scalar.copy(y_closing[c], acc_closing[c][:])
-            nc.vector.tensor_tensor(places(c, first, E), y_closing[c], gate_sb[:, first * C : E * C], MULT)
+            nc.vector.tensor_tensor(places(c, f, E), y_closing[c], gate_sb[:, f * C : E * C], MULT)
             store(c)

@@ -40,10 +40,11 @@ HOLD = 8
 CUT1 = (24, 52, 52, 52, 52, 68)
 CUT0 = (80, 80, 80, 80, 88, 88)
 CUT0_6 = 88
-CUT0_7 = 60
+CUT0_7 = 76
 CUT_A = 64
-CUT1_6 = 112
+CUT1_6 = 96
 V60 = True
+QP = (2, 2, 2, 2, 1, 2, 1, 2)
 CUT_B = 84
 EARLY0 = (120, 120, 120, 120, 120, 96)
 Y_COLUMN = 320
@@ -316,7 +317,7 @@ def tile_moe_two_mlp_relu_kernel(
             if not early:
                 quantize_w1(g, 1)
                 first_matmuls(g)
-            quantize_w1(g + 1, 2)
+            quantize_w1(g + 1, QP[e])
             first_matmuls(g + 1)
             if e > 0:
                 for c in range(ROW_TILES):
@@ -363,7 +364,7 @@ def tile_moe_two_mlp_relu_kernel(
             target.rearrange("p o t (m j) -> p o m j t", j=PACK), source.rearrange("p o j (m t) -> p o m j t", t=PACK)
         )
         round_w1(True, 14, CUT0_7, P - HOLD)
-        quantize_w1(13, 2)
+        quantize_w1(13, QP[6])
         first_matmuls(13)
         round_w1(False, 15, 0, CUT_A)
         if CUT_A < P // 2:
@@ -378,7 +379,7 @@ def tile_moe_two_mlp_relu_kernel(
         relu_h(6, before_values[:, PIECE:])
         round_pair(15, CUT_B, P, 0)
         round_pair(15, CUT_B, P, 2)
-        quantize_w1(15, PACK)
+        quantize_w1(15, QP[7])
         first_matmuls(15)
         round_w2(V60, before_values[:, 0:PIECE], late_raw[6, 0], 1)
         nc.vector.quantize_mx(

@@ -39,12 +39,12 @@ W2H_DEPTH = 4
 HOLD = 8
 CUT1 = (24, 52, 52, 52, 52, 68)
 CUT0 = (80, 80, 80, 80, 88, 88)
-CUT0_6 = 88
-CUT0_7 = 76
-CUT_A = 64
-CUT1_6 = 96
+CUT0_6 = 60
+CUT0_7 = 68
+CUT_A = 56
+CUT_G = 104
 V60 = True
-QP = (2, 2, 2, 2, 1, 2, 1, 2)
+QP = (2, 2, 2, 2, 1, 2, 2, 2)
 CUT_B = 84
 EARLY0 = (120, 120, 120, 120, 120, 96)
 Y_COLUMN = 320
@@ -99,6 +99,7 @@ def tile_moe_two_mlp_relu_kernel(
         y_closing2 = one("y_closing2", [P, (E - first[2]) * C], F32)
         acc1 = [psum.tile([P, PACK, C], F32, name=f"acc1_{i}") for i in range(2)]
         acc2 = [psum.tile([P, ROW_TILES, C], F32, name=f"acc2_{i}") for i in range(2)]
+        acc_pair = psum.tile([P, 2 * C], F32, name="acc_pair")
         acc_closing = {c: psum.tile([P, (E - f) * C], F32, name=f"acc_closing{c}") for c, f in first.items()}
 
         def load_words(o):
@@ -125,7 +126,8 @@ def tile_moe_two_mlp_relu_kernel(
             return w1_raw[g // SLOTS % 2][:, g % SLOTS * UNIT : (g % SLOTS + count) * UNIT]
 
         def rounded(g, count=1):
-            return w1_bf16[:, g % SLOTS * UNIT : (g % SLOTS + count) * UNIT]
+            slot = 2 if g == 12 else g % SLOTS
+            return w1_bf16[:, slot * UNIT : (slot + count) * UNIT]
 
         def load_w1(g, first_column=0, end_column=H):
             rows = w1[g // PASSES, g % PASSES * K_PASS : (g % PASSES + 1) * K_PASS, :]
@@ -241,6 +243,10 @@ def tile_moe_two_mlp_relu_kernel(
             else:
                 sums = acc2[e % 2][:, c, :]
                 codes, scales, a = h_codes, h_scales, (C + c * P if e < 6 else 0)
+                if c == 1 and e in (4, 5):
+                    sums = acc_pair[:, (e - 4) * C : (e - 3) * C]
+                if (e, c) == (4, 2):
+                    sums = acc2[e % 2][:, 1, :]
             nc.tensor.matmul_mx(
                 out=sums,
                 lhsT=codes[:, a : a + P].bitcast(FP8X4),
@@ -311,8 +317,9 @@ def tile_moe_two_mlp_relu_kernel(
                 round_w1(False, g + 1, 0, CUT1[e])
                 round_w1(True, g + 1, CUT1[e], P)
                 early = True
+            due = (0, 2) if e == 5 else (0, 1, 2)
             if e > 0:
-                y = raw(g + 1).rearrange("p (j i) -> p j i", j=PACK)[:, 0:ROW_TILES, Y_COLUMN : Y_COLUMN + C]
+                y = raw(g + 1).rearrange("p (j i) -> p j i", j=PACK)[:, 0 : len(due), Y_COLUMN : Y_COLUMN + C]
                 times_gate(e - 1, y)
             if not early:
                 quantize_w1(g, 1)
@@ -320,8 +327,8 @@ def tile_moe_two_mlp_relu_kernel(
             quantize_w1(g + 1, QP[e])
             first_matmuls(g + 1)
             if e > 0:
-                for c in range(ROW_TILES):
-                    scatter_one(e - 1, c, y[:, c, :])
+                for place, c in enumerate(due):
+                    scatter_one(e - 1, c, y[:, place, :])
             round_w2(False, w2h_values(e, C, C + tiles * P), w2_raw[e % W2_RAW_DEPTH][:], tiles)
             relu_h(e, w2h_values(e, 0, C))
             if tiles == ROW_TILES:
@@ -341,29 +348,22 @@ def tile_moe_two_mlp_relu_kernel(
             nc.sync.dma_start(late_raw[e, c].rearrange("p (j n) -> p j n", j=PACK), w2_rows(e, c, c + 1))
 
         round_w1(False, 12, 0, CUT0_6)
-        if CUT0_6 < P - HOLD:
-            round_w1(True, 12, CUT0_6, P - HOLD)
-        round_w1(False, 13, 0, CUT1_6)
-        round_w1(True, 12, P - HOLD, P, 2)
-        if CUT1_6 < P - 2 * HOLD:
-            round_w1(True, 13, CUT1_6, P - 2 * HOLD)
-        y5 = raw(12).rearrange("p (j i) -> p j i", j=PACK)[:, 0:2, H - C : H]
-        times_gate(5, y5)
+        round_w1(True, 12, CUT0_6, P)
+        y50 = raw(12).rearrange("p (j i) -> p j i", j=PACK)[:, 0:1, 0:C]
+        y451 = raw(12)[:, H : H + 2 * C]
+        times_gate(5, y50)
+        nc.vector.tensor_tensor(y451, acc_pair[:], gate_sb[:, 4 * C : 6 * C], MULT)
         quantize_w1(12, 1)
         first_matmuls(12)
-        scatter_one(5, 0, y5[:, 0, :])
-        scatter_one(5, 1, y5[:, 1, :])
+        scatter_one(5, 0, y50[:, 0, :])
+        nc.vector.tensor_copy(places(1, 4, 6), y451)
+        round_w1(False, 13, 0, P)
         round_w1(False, 14, 0, CUT0_7)
-        skew = UNIT + PACK * HOLD
-        start = UNIT + PACK * (P - 2 * HOLD)
-        source = w1_raw[1][:, start : start + 2 * skew].rearrange("p (o x) -> p o x", o=2)[:, :, 0:UNIT]
-        source = source.rearrange("p o (j i) -> p o j i", j=PACK)[:, :, :, 0 : PACK * HOLD]
-        target = w1_bf16[:, start : start + 2 * skew].rearrange("p (o x) -> p o x", o=2)[:, :, 0:UNIT]
-        target = target.rearrange("p o (t x) -> p o t x", t=PACK)[:, :, :, 0 : PACK * HOLD]
-        nc.vector.tensor_copy(
-            target.rearrange("p o t (m j) -> p o m j t", j=PACK), source.rearrange("p o j (m t) -> p o m j t", t=PACK)
-        )
-        round_w1(True, 14, CUT0_7, P - HOLD)
+        source = raw(14).rearrange("p (j m t) -> p t m j", j=PACK, t=PACK)
+        target = rounded(14).rearrange("p (t m j) -> p t m j", j=PACK, t=PACK)
+        nc.gpsimd.tensor_scalar(target[:, :, CUT0_7:CUT_G, :], source[:, :, CUT0_7:CUT_G, :], 1.0, 0.0, MULT, ADD)
+        if CUT_G < P:
+            round_w1(True, 14, CUT_G, P)
         quantize_w1(13, QP[6])
         first_matmuls(13)
         round_w1(False, 15, 0, CUT_A)

@@ -39,13 +39,12 @@ W2H_DEPTH = 4
 HOLD = 8
 CUT1 = (24, 52, 52, 52, 52, 68)
 CUT0 = (80, 80, 80, 80, 88, 88)
-CUT0_6 = 60
+CUT0_6 = 64
 CUT0_7 = 68
-CUT_A = 56
-CUT_G = 104
+CUT_A = 64
 V60 = True
 QP = (2, 2, 2, 2, 1, 2, 2, 2)
-CUT_B = 84
+CUT_B = 76
 EARLY0 = (120, 120, 120, 120, 120, 96)
 Y_COLUMN = 320
 STREAM = 6
@@ -126,8 +125,7 @@ def tile_moe_two_mlp_relu_kernel(
             return w1_raw[g // SLOTS % 2][:, g % SLOTS * UNIT : (g % SLOTS + count) * UNIT]
 
         def rounded(g, count=1):
-            slot = 2 if g == 12 else g % SLOTS
-            return w1_bf16[:, slot * UNIT : (slot + count) * UNIT]
+            return w1_bf16[:, g % SLOTS * UNIT : (g % SLOTS + count) * UNIT]
 
         def load_w1(g, first_column=0, end_column=H):
             rows = w1[g // PASSES, g % PASSES * K_PASS : (g % PASSES + 1) * K_PASS, :]
@@ -352,18 +350,15 @@ def tile_moe_two_mlp_relu_kernel(
         y50 = raw(12).rearrange("p (j i) -> p j i", j=PACK)[:, 0:1, 0:C]
         y451 = raw(12)[:, H : H + 2 * C]
         times_gate(5, y50)
-        nc.vector.tensor_tensor(y451, acc_pair[:], gate_sb[:, 4 * C : 6 * C], MULT)
+        nc.scalar.copy(y451, acc_pair[:])
         quantize_w1(12, 1)
         first_matmuls(12)
         scatter_one(5, 0, y50[:, 0, :])
-        nc.vector.tensor_copy(places(1, 4, 6), y451)
-        round_w1(False, 13, 0, P)
+        nc.vector.tensor_tensor(places(1, 4, 6), y451, gate_sb[:, 4 * C : 6 * C], MULT)
+        round_w1(False, 13, 0, P - HOLD)
         round_w1(False, 14, 0, CUT0_7)
-        source = raw(14).rearrange("p (j m t) -> p t m j", j=PACK, t=PACK)
-        target = rounded(14).rearrange("p (t m j) -> p t m j", j=PACK, t=PACK)
-        nc.gpsimd.tensor_scalar(target[:, :, CUT0_7:CUT_G, :], source[:, :, CUT0_7:CUT_G, :], 1.0, 0.0, MULT, ADD)
-        if CUT_G < P:
-            round_w1(True, 14, CUT_G, P)
+        round_w1(True, 13, P - HOLD, P, 2)
+        round_w1(True, 14, CUT0_7, P - HOLD)
         quantize_w1(13, QP[6])
         first_matmuls(13)
         round_w1(False, 15, 0, CUT_A)

@@ -30,25 +30,31 @@ QUADRANT = 32
 SCALE_ROWS = 4
 RUN = 4
 ALIGN = 256
+
 UNIT = PACK * H
 PIECE = PACK * P
-SLOTS = 4
+
+EARLY = E - 2
+LAST_EARLY, BEFORE_LAST, LAST = EARLY - 1, E - 2, E - 1
+CLOSING_FIRST = {1: BEFORE_LAST, 2: LAST_EARLY}
+LATE_PIECES = [(e, c) for c in range(ROW_TILES) for e in range(CLOSING_FIRST.get(c, EARLY), E)]
+PAIR, PAIR_TILE = (LAST_EARLY - 1, LAST_EARLY), 1
+
+TILE_UNITS = 4
 CODE_DEPTH = 6
 W2_RAW_DEPTH = 3
 W2H_DEPTH = 4
-HOLD = 8
-CUT1 = (24, 52, 52, 52, 52, 68)
-CUT0 = (80, 80, 80, 80, 88, 88)
-CUT0_6 = 64
-CUT0_7 = 68
-CUT_A = 64
-V60 = True
-QP = (2, 2, 2, 2, 1, 2, 2, 2)
-CUT_B = 76
-EARLY0 = (120, 120, 120, 120, 120, 96)
+
+BOTH = 8
+SHARED = P - BOTH
+FIRST_CUT = 24
+STREAM_CUT = 52
+LAST_EARLY_CUT = 68
+LAST_EARLY_PASS0_CUT = 96
+BEFORE_LAST_PASS0_CUT = P // 2
+LAST_PASS0_CUT = 68
+LAST_CUT = 76
 Y_COLUMN = 320
-STREAM = 6
-WHOLE = 0
 
 
 def tile_moe_two_mlp_relu_kernel(
@@ -77,29 +83,34 @@ def tile_moe_two_mlp_relu_kernel(
         gate_sb = one("gate_sb", [P, S], F32)
         zeros = one("zeros", [P, C], F32)
         out_sb = ring("out_sb", ROW_TILES, [P, T], F32)
-        w1_raw = ring("w1_raw", 2, [P, SLOTS * UNIT], F32)
-        w1_bf16 = one("w1_bf16", [P, SLOTS * UNIT], BF16)
+        w1_raw = ring("w1_raw", 2, [P, TILE_UNITS * UNIT], F32)
+        w1_bf16 = one("w1_bf16", [P, TILE_UNITS * UNIT], BF16)
         w1_codes = ring("w1_codes", CODE_DEPTH, [P, H], U32)
         w1_scales = ring("w1_scales", CODE_DEPTH, [P, H], U8)
         w2_raw = ring("w2_raw", W2_RAW_DEPTH, [P, PACK * N], F32)
         w2h_bf16 = ring("w2h_bf16", W2H_DEPTH, [P, (C + N) * PACK], BF16)
         w2h_codes = ring("w2h_codes", W2H_DEPTH, [P, C + N], U32)
         w2h_scales = ring("w2h_scales", W2H_DEPTH, [P, C + N], U8)
-        late = [(6, 0), (7, 0), (6, 1), (7, 1), (5, 2), (6, 2), (7, 2)]
-        late_raw = {ec: one("late_raw%d%d" % ec, [P, PIECE], F32)[:] for ec in late if ec not in ((7, 0), (6, 1))}
-        stage70 = one("stage70", [P, PIECE // 2 + PIECE], F32)
-        late_raw[7, 0] = stage70[:, PIECE // 2 :]
-        late_raw[6, 1] = shared.tile([P, PIECE], F32, name="late_raw61", align_bytes=ALIGN, offset=0)[:]
+        late_raw = {
+            (e, c): one(f"late_raw{e}{c}", [P, PIECE], F32)[:]
+            for e, c in LATE_PIECES
+            if (e, c) not in ((LAST, 0), (BEFORE_LAST, 1))
+        }
+        last_stage = one("stage70", [P, PIECE // 2 + PIECE], F32)
+        lent = shared.tile([P, PIECE], F32, name="late_raw61", align_bytes=ALIGN, offset=0)
+        late_raw[LAST, 0] = last_stage[:, PIECE // 2 :]
+        late_raw[BEFORE_LAST, 1] = lent[:]
         last_scales = one("last_scales", [P, P + C], U8)
-        first = {1: 6, 2: 5}
-        late_bf16 = {c: one(f"late_bf16{c}", [P, (E - f) * PIECE], BF16) for c, f in first.items()}
-        late_codes = {c: one(f"late_codes{c}", [P, (E - f) * P], U32) for c, f in first.items()}
-        late_scales = {c: one(f"late_scales{c}", [P, (E - f) * P], U8) for c, f in first.items()}
-        y_closing2 = one("y_closing2", [P, (E - first[2]) * C], F32)
+        late_bf16 = {c: one(f"late_bf16{c}", [P, (E - first) * PIECE], BF16) for c, first in CLOSING_FIRST.items()}
+        late_codes = {c: one(f"late_codes{c}", [P, (E - first) * P], U32) for c, first in CLOSING_FIRST.items()}
+        late_scales = {c: one(f"late_scales{c}", [P, (E - first) * P], U8) for c, first in CLOSING_FIRST.items()}
+        y_closing2 = one("y_closing2", [P, (E - CLOSING_FIRST[2]) * C], F32)
         acc1 = [psum.tile([P, PACK, C], F32, name=f"acc1_{i}") for i in range(2)]
         acc2 = [psum.tile([P, ROW_TILES, C], F32, name=f"acc2_{i}") for i in range(2)]
-        acc_pair = psum.tile([P, 2 * C], F32, name="acc_pair")
-        acc_closing = {c: psum.tile([P, (E - f) * C], F32, name=f"acc_closing{c}") for c, f in first.items()}
+        acc_pair = psum.tile([P, len(PAIR) * C], F32, name="acc_pair")
+        acc_closing = {
+            c: psum.tile([P, (E - first) * C], F32, name=f"acc_closing{c}") for c, first in CLOSING_FIRST.items()
+        }
 
         def load_words(o):
             nc.sync.dma_start(tok_words[o][:], x_words[o].rearrange("p t r -> p (t r)").bitcast(I32))
@@ -121,65 +132,56 @@ def tile_moe_two_mlp_relu_kernel(
                     nc.tensor.transpose(bank[:, q, :], gate_row[:, column : column + 1].to_broadcast([P, P]), identity[:])
                 nc.scalar.copy(by_slot[:, :, half * PACK : (half + 1) * PACK], bank[:].rearrange("p q n -> p n q"))
 
-        def raw(g, count=1):
-            return w1_raw[g // SLOTS % 2][:, g % SLOTS * UNIT : (g % SLOTS + count) * UNIT]
+        def raw(u, count=1):
+            return w1_raw[u // TILE_UNITS % 2][:, u % TILE_UNITS * UNIT : (u % TILE_UNITS + count) * UNIT]
 
-        def rounded(g, count=1):
-            return w1_bf16[:, g % SLOTS * UNIT : (g % SLOTS + count) * UNIT]
+        def raw_rows(u):
+            return raw(u).rearrange("p (j i) -> p j i", j=PACK)
 
-        def load_w1(g, first_column=0, end_column=H):
-            rows = w1[g // PASSES, g % PASSES * K_PASS : (g % PASSES + 1) * K_PASS, :]
-            if end_column - first_column == H:
-                nc.sync.dma_start(raw(g), rows.rearrange("(p j) i -> p (j i)", j=PACK))
-            else:
-                nc.sync.dma_start(
-                    raw(g).rearrange("p (j i) -> p j i", j=PACK)[:, :, first_column:end_column],
-                    rows.rearrange("(p j) i -> p j i", j=PACK)[:, :, first_column:end_column],
-                )
+        def rounded(u, count=1):
+            return w1_bf16[:, u % TILE_UNITS * UNIT : (u % TILE_UNITS + count) * UNIT]
 
-        def load_w1_whole(e):
-            nc.sync.dma_start(
-                raw(PASSES * e, PASSES).rearrange("p (o x) -> p o x", o=PASSES),
-                w1[e].rearrange("(o p j) i -> p o (j i)", o=PASSES, j=PACK),
-            )
+        def w1_rows(u):
+            return w1[u // PASSES, u % PASSES * K_PASS : (u % PASSES + 1) * K_PASS, :]
 
-        def round_w1(on_vector, g, m0, m1, count=1):
-            source = raw(g, count).rearrange("p (o j m t) -> p o m j t", o=count, j=PACK, t=PACK)
-            target = rounded(g, count).rearrange("p (o t m j) -> p o m j t", o=count, j=PACK, t=PACK)
-            if not on_vector:
-                nc.scalar.activation(target[:, 0, m0:m1], source[:, 0, m0:m1], COPY)
-            elif count == 1:
-                nc.vector.tensor_copy(target[:, 0, m0:m1], source[:, 0, m0:m1])
-            else:
-                nc.vector.tensor_copy(target[:, :, m0:m1], source[:, :, m0:m1])
+        def load_unit(u):
+            nc.sync.dma_start(raw(u), w1_rows(u).rearrange("(p j) i -> p (j i)", j=PACK))
 
-        def codes_of(g):
-            return w1_codes[g % CODE_DEPTH]
+        def rounding_views(u, count):
+            target = rounded(u, count).rearrange("p (o t m j) -> p o m j t", o=count, j=PACK, t=PACK)
+            source = raw(u, count).rearrange("p (o j m t) -> p o m j t", o=count, j=PACK, t=PACK)
+            return target, source
 
-        def round_pair(g, m0, m1, t0):
-            source = raw(g).rearrange("p (j m t) -> p m j t", j=PACK, t=PACK)
-            target = rounded(g).rearrange("p (t m j) -> p m j t", j=PACK, t=PACK)
-            nc.vector.tensor_copy(target[:, m0:m1, :, t0 : t0 + 2], source[:, m0:m1, :, t0 : t0 + 2])
+        def round_on_scalar(u, first, end):
+            target, source = rounding_views(u, 1)
+            nc.scalar.activation(target[:, 0, first:end], source[:, 0, first:end], COPY)
 
-        def quantize_w1(g, parts):
+        def round_on_vector(u, first, end, t_first=0, t_end=PACK):
+            target, source = rounding_views(u, 1)
+            nc.vector.tensor_copy(target[:, 0, first:end, :, t_first:t_end], source[:, 0, first:end, :, t_first:t_end])
+
+        def round_both(u):
+            target, source = rounding_views(u, 2)
+            nc.vector.tensor_copy(target[:, :, SHARED:P], source[:, :, SHARED:P])
+
+        def quantize_and_multiply(u, parts):
+            codes, scales = w1_codes[u % CODE_DEPTH], w1_scales[u % CODE_DEPTH]
             width = H // parts
             for a in range(parts):
                 cols = slice(a * width, (a + 1) * width)
                 nc.vector.quantize_mx(
-                    out=codes_of(g)[:, cols].bitcast(FP8X4),
-                    scales=w1_scales[g % CODE_DEPTH][:, cols],
-                    in_=rounded(g)[:, a * width * PACK : (a + 1) * width * PACK],
+                    out=codes[:, cols].bitcast(FP8X4),
+                    scales=scales[:, cols],
+                    in_=rounded(u)[:, a * width * PACK : (a + 1) * width * PACK],
                 )
-
-        def first_matmuls(g):
-            e, o = divmod(g, PASSES)
+            e, o = divmod(u, PASSES)
             slots = slice(e * C, (e + 1) * C)
             for t in range(PACK):
                 cols = slice(t * P, (t + 1) * P)
                 nc.tensor.matmul_mx(
                     out=acc1[e % 2][:, t, :],
-                    lhsT=codes_of(g)[:, cols].bitcast(FP8X4),
-                    lhsT_scale=w1_scales[g % CODE_DEPTH][:, cols],
+                    lhsT=codes[:, cols].bitcast(FP8X4),
+                    lhsT_scale=scales[:, cols],
                     rhs=slot_words[o][:, slots].bitcast(FP8X4),
                     rhs_scale=slot_scales[SCALE_ROWS * o : P, slots],
                     start=(o == 0 and t == 0),
@@ -193,78 +195,83 @@ def tile_moe_two_mlp_relu_kernel(
                 RELU,
             )
 
-        def w2_rows(e, c0, c1):
-            return w2[e].rearrange("(p j) n -> p j n", j=PACK)[:, :, c0 * P : c1 * P]
+        def w2_rows(e, first, end):
+            return w2[e].rearrange("(p j) n -> p j n", j=PACK)[:, :, first * P : end * P]
 
         def load_w2(e, tiles):
             target = w2_raw[e % W2_RAW_DEPTH][:].rearrange("p (j n) -> p j n", j=PACK)
             nc.sync.dma_start(target[:, :, 0 : tiles * P], w2_rows(e, 0, tiles))
 
-        def w2h_values(e, a, b):
-            return w2h_bf16[e % W2H_DEPTH][:, a * PACK : b * PACK]
+        def w2h_values(e, first, end):
+            return w2h_bf16[e % W2H_DEPTH][:, first * PACK : end * PACK]
 
-        def round_w2(on_vector, values, source, tiles):
+        def w2_views(values, landed, tiles):
             target = values.rearrange("p (g n j) -> p g j n", n=RUN, j=PACK)
-            source = source.rearrange("p (j g n) -> p g j n", j=PACK, n=RUN)[:, 0 : tiles * P // RUN]
-            if on_vector:
-                nc.vector.tensor_copy(target, source)
-            else:
-                nc.scalar.activation(target, source, COPY)
+            source = landed.rearrange("p (j g n) -> p g j n", j=PACK, n=RUN)
+            return target, source[:, 0 : tiles * P // RUN]
 
-        def quantize_w2h(e, a, b):
+        def quantize_w2h(e, first, end, values):
             nc.vector.quantize_mx(
-                out=w2h_codes[e % W2H_DEPTH][:, a:b].bitcast(FP8X4),
-                scales=w2h_scales[e % W2H_DEPTH][:, a:b],
-                in_=w2h_values(e, a, b),
+                out=w2h_codes[e % W2H_DEPTH][:, first:end].bitcast(FP8X4),
+                scales=w2h_scales[e % W2H_DEPTH][:, first:end],
+                in_=values,
             )
 
-        def late_values(e, c):
-            return late_bf16[c][:, (e - first[c]) * PIECE : (e - first[c] + 1) * PIECE]
+        def closing_views(e, c):
+            place = e - CLOSING_FIRST[c]
+            return w2_views(late_bf16[c][:, place * PIECE : (place + 1) * PIECE], late_raw[e, c], 1)
 
-        def quantize_late(c, e0, e1):
-            a, b = (e0 - first[c]) * P, (e1 - first[c]) * P
+        def quantize_closing(c, first_expert, end_expert):
+            first, end = (first_expert - CLOSING_FIRST[c]) * P, (end_expert - CLOSING_FIRST[c]) * P
             nc.vector.quantize_mx(
-                out=late_codes[c][:, a:b].bitcast(FP8X4),
-                scales=late_scales[c][:, a:b],
-                in_=late_bf16[c][:, a * PACK : b * PACK],
+                out=late_codes[c][:, first:end].bitcast(FP8X4),
+                scales=late_scales[c][:, first:end],
+                in_=late_bf16[c][:, first * PACK : end * PACK],
             )
 
-        quantised = {e: (w2h_codes[e % W2H_DEPTH], w2h_scales[e % W2H_DEPTH]) for e in range(E - 1)}
+        def closing(e, c):
+            return e >= CLOSING_FIRST.get(c, E)
+
+        def alone(e):
+            return [c for c in range(ROW_TILES) if not closing(e, c) and not (e in PAIR and c == PAIR_TILE)]
+
+        quantised = {e: (w2h_codes[e % W2H_DEPTH], w2h_scales[e % W2H_DEPTH]) for e in range(LAST)}
 
         def second_matmul(e, c):
             h_codes, h_scales = quantised[e]
-            h0 = 0 if e < 6 else P
-            if c in first and e >= first[c]:
-                place = e - first[c]
+            h_first = 0 if e < EARLY else P
+            codes, scales, first = h_codes, h_scales, (C + c * P if e < EARLY else 0)
+            if closing(e, c):
+                place = e - CLOSING_FIRST[c]
                 sums = acc_closing[c][:, place * C : (place + 1) * C]
-                codes, scales, a = late_codes[c], late_scales[c], place * P
+                codes, scales, first = late_codes[c], late_scales[c], place * P
+            elif c in alone(e):
+                sums = acc2[e % 2][:, alone(e).index(c), :]
             else:
-                sums = acc2[e % 2][:, c, :]
-                codes, scales, a = h_codes, h_scales, (C + c * P if e < 6 else 0)
-                if c == 1 and e in (4, 5):
-                    sums = acc_pair[:, (e - 4) * C : (e - 3) * C]
-                if (e, c) == (4, 2):
-                    sums = acc2[e % 2][:, 1, :]
+                sums = acc_pair[:, PAIR.index(e) * C : (PAIR.index(e) + 1) * C]
             nc.tensor.matmul_mx(
                 out=sums,
-                lhsT=codes[:, a : a + P].bitcast(FP8X4),
-                lhsT_scale=scales[:, a : a + P],
-                rhs=h_codes[:, h0 : h0 + C].bitcast(FP8X4),
-                rhs_scale=h_scales[:, h0 : h0 + C],
+                lhsT=codes[:, first : first + P].bitcast(FP8X4),
+                lhsT_scale=scales[:, first : first + P],
+                rhs=h_codes[:, h_first : h_first + C].bitcast(FP8X4),
+                rhs_scale=h_scales[:, h_first : h_first + C],
                 start=True,
                 stop=True,
             )
 
-        def places(c, e0, e1):
-            return out_sb[c][:].indirect(dst_list[:, e0 * C // LIST_ROWS : e1 * C // LIST_ROWS])
+        def places(c, first, end):
+            return out_sb[c][:].indirect(dst_list[:, first * C // LIST_ROWS : end * C // LIST_ROWS])
 
-        def times_gate(e, y, c0=0):
+        def times_gate(e, y):
             count = y.shape[1]
             gates = gate_sb[:, e * C : (e + 1) * C].rearrange("p (c s) -> p c s", c=1).to_broadcast([P, count, C])
-            nc.vector.tensor_tensor(y, acc2[e % 2][:, c0 : c0 + count, :], gates, MULT)
+            nc.vector.tensor_tensor(y, acc2[e % 2][:, 0:count, :], gates, MULT)
 
         def scatter_one(e, c, y):
             nc.vector.tensor_tensor(places(c, e, e + 1), y, zeros[:], ADD)
+
+        def scatter_group(c, first, end, y):
+            nc.vector.tensor_tensor(places(c, first, end), y, gate_sb[:, first * C : end * C], MULT)
 
         def store(c):
             nc.sync.dma_start(out[c * P : (c + 1) * P, :], out_sb[c][:])
@@ -288,124 +295,107 @@ def tile_moe_two_mlp_relu_kernel(
         make_identity(nc, identity[:])
         spread_gate()
 
-        for e in range(6):
-            g = PASSES * e
-            tiles = ROW_TILES if e < 5 else 2
-            if e < WHOLE:
-                load_w1_whole(e)
-            else:
-                load_w1(g)
-                load_w1(g + 1)
+        for e in range(EARLY):
+            pass0, pass1 = PASSES * e, PASSES * e + 1
+            tiles = len([c for c in range(ROW_TILES) if (e, c) not in LATE_PIECES])
+            load_unit(pass0)
+            load_unit(pass1)
             if e == 0:
                 nc.sync.dma_start(dst_list[:], dst)
             load_w2(e, tiles)
-            if e < STREAM:
-                round_w1(False, g, 0, EARLY0[e])
-                if EARLY0[e] < P - HOLD:
-                    round_w1(True, g, EARLY0[e], P - HOLD)
-                round_w1(False, g + 1, 0, CUT1[e])
-                round_w1(True, g, P - HOLD, P, 2)
-                round_w1(True, g + 1, CUT1[e], P - HOLD)
-                early = False
+            if e == LAST_EARLY:
+                round_on_scalar(pass0, 0, LAST_EARLY_PASS0_CUT)
+                round_on_vector(pass0, LAST_EARLY_PASS0_CUT, SHARED)
             else:
-                round_w1(False, g, 0, CUT0[e])
-                round_w1(True, g, CUT0[e], P)
-                quantize_w1(g, 1)
-                first_matmuls(g)
-                round_w1(False, g + 1, 0, CUT1[e])
-                round_w1(True, g + 1, CUT1[e], P)
-                early = True
-            due = (0, 2) if e == 5 else (0, 1, 2)
-            if e > 0:
-                y = raw(g + 1).rearrange("p (j i) -> p j i", j=PACK)[:, 0 : len(due), Y_COLUMN : Y_COLUMN + C]
+                round_on_scalar(pass0, 0, SHARED)
+            cut = {0: FIRST_CUT, LAST_EARLY: LAST_EARLY_CUT}.get(e, STREAM_CUT)
+            round_on_scalar(pass1, 0, cut)
+            round_both(pass0)
+            round_on_vector(pass1, cut, SHARED)
+            due = alone(e - 1) if e > 0 else []
+            if due:
+                y = raw_rows(pass1)[:, 0 : len(due), Y_COLUMN : Y_COLUMN + C]
                 times_gate(e - 1, y)
-            if not early:
-                quantize_w1(g, 1)
-                first_matmuls(g)
-            quantize_w1(g + 1, QP[e])
-            first_matmuls(g + 1)
-            if e > 0:
-                for place, c in enumerate(due):
-                    scatter_one(e - 1, c, y[:, place, :])
-            round_w2(False, w2h_values(e, C, C + tiles * P), w2_raw[e % W2_RAW_DEPTH][:], tiles)
+            quantize_and_multiply(pass0, 1)
+            quantize_and_multiply(pass1, 2 if e == LAST_EARLY else 1)
+            for place, c in enumerate(due):
+                scatter_one(e - 1, c, y[:, place, :])
+            nc.scalar.activation(*w2_views(w2h_values(e, C, C + tiles * P), w2_raw[e % W2_RAW_DEPTH][:], tiles), COPY)
             relu_h(e, w2h_values(e, 0, C))
             if tiles == ROW_TILES:
-                quantize_w2h(e, 0, C + N)
+                quantize_w2h(e, 0, C + N, w2h_values(e, 0, C + N))
             else:
-                quantize_w2h(e, C + P, C + 2 * P)
-                quantize_w2h(e, 0, C + P)
+                quantize_w2h(e, C + P, C + 2 * P, w2h_values(e, C + P, C + 2 * P))
+                quantize_w2h(e, 0, C + P, w2h_values(e, 0, C + P))
             for c in range(tiles):
                 second_matmul(e, c)
 
-        load_w1(12)
-        load_w1(13)
-        load_w1(14)
-        load_w1(15, 0, H // 2)
-        load_w1(15, H // 2, H)
-        for e, c in late:
+        before0, before1, last0, last1 = range(PASSES * BEFORE_LAST, PASSES * E)
+        for u in (before0, before1, last0):
+            load_unit(u)
+        for half in range(2):
+            cols = slice(half * H // 2, (half + 1) * H // 2)
+            nc.sync.dma_start(raw_rows(last1)[:, :, cols], w1_rows(last1).rearrange("(p j) i -> p j i", j=PACK)[:, :, cols])
+        for e, c in LATE_PIECES:
             nc.sync.dma_start(late_raw[e, c].rearrange("p (j n) -> p j n", j=PACK), w2_rows(e, c, c + 1))
 
-        round_w1(False, 12, 0, CUT0_6)
-        round_w1(True, 12, CUT0_6, P)
-        y50 = raw(12).rearrange("p (j i) -> p j i", j=PACK)[:, 0:1, 0:C]
-        y451 = raw(12)[:, H : H + 2 * C]
-        times_gate(5, y50)
-        nc.scalar.copy(y451, acc_pair[:])
-        quantize_w1(12, 1)
-        first_matmuls(12)
-        scatter_one(5, 0, y50[:, 0, :])
-        nc.vector.tensor_tensor(places(1, 4, 6), y451, gate_sb[:, 4 * C : 6 * C], MULT)
-        round_w1(False, 13, 0, P - HOLD)
-        round_w1(False, 14, 0, CUT0_7)
-        round_w1(True, 13, P - HOLD, P, 2)
-        round_w1(True, 14, CUT0_7, P - HOLD)
-        quantize_w1(13, QP[6])
-        first_matmuls(13)
-        round_w1(False, 15, 0, CUT_A)
-        if CUT_A < P // 2:
-            round_w1(True, 15, CUT_A, P // 2)
-        quantize_w1(14, 1)
-        first_matmuls(14)
-        edge = 3 * UNIT + PACK * CUT_B
-        before_values = w1_raw[1][:, edge - PIECE : edge].bitcast(BF16)
-        last_values = stage70[:, 0:PIECE].bitcast(BF16)
-        if CUT_B > P // 2:
-            round_w1(False, 15, P // 2, CUT_B)
-        relu_h(6, before_values[:, PIECE:])
-        round_pair(15, CUT_B, P, 0)
-        round_pair(15, CUT_B, P, 2)
-        quantize_w1(15, QP[7])
-        first_matmuls(15)
-        round_w2(V60, before_values[:, 0:PIECE], late_raw[6, 0], 1)
-        nc.vector.quantize_mx(
-            out=w2h_codes[6 % W2H_DEPTH][:, 0 : P + C].bitcast(FP8X4), scales=w2h_scales[6 % W2H_DEPTH][:, 0 : P + C], in_=before_values
-        )
-        second_matmul(6, 0)
-        round_w2(False, last_values[:, 0:PIECE], late_raw[7, 0], 1)
-        relu_h(7, last_values[:, PIECE:])
-        round_w2(True, late_values(6, 1), late_raw[6, 1], 1)
-        y6 = shared.tile([P, 1, C], F32, name="y6", align_bytes=ALIGN, offset=0)
+        round_on_scalar(before0, 0, BEFORE_LAST_PASS0_CUT)
+        round_on_vector(before0, BEFORE_LAST_PASS0_CUT, P)
+        y_alone = raw_rows(before0)[:, 0:1, 0:C]
+        y_pair = raw_rows(before0)[:, 1, 0 : len(PAIR) * C]
+        times_gate(LAST_EARLY, y_alone)
+        nc.scalar.copy(y_pair, acc_pair[:])
+        quantize_and_multiply(before0, 1)
+        scatter_one(LAST_EARLY, 0, y_alone[:, 0, :])
+        scatter_group(PAIR_TILE, PAIR[0], EARLY, y_pair)
+
+        round_on_scalar(before1, 0, SHARED)
+        round_on_scalar(last0, 0, LAST_PASS0_CUT)
+        round_both(before1)
+        round_on_vector(last0, LAST_PASS0_CUT, SHARED)
+        quantize_and_multiply(before1, 2)
+        round_on_scalar(last1, 0, P // 2)
+        quantize_and_multiply(last0, 1)
+
+        share_end = UNIT + PACK * LAST_CUT
+        before_values = raw(last0, 2)[:, share_end - PIECE : share_end].bitcast(BF16)
+        last_values = last_stage[:, 0:PIECE].bitcast(BF16)
+        round_on_scalar(last1, P // 2, LAST_CUT)
+        relu_h(BEFORE_LAST, before_values[:, PIECE:])
+        for t in range(0, PACK, 2):
+            round_on_vector(last1, LAST_CUT, P, t, t + 2)
+        quantize_and_multiply(last1, 2)
+
+        nc.vector.tensor_copy(*w2_views(before_values[:, 0:PIECE], late_raw[BEFORE_LAST, 0], 1))
+        quantize_w2h(BEFORE_LAST, 0, P + C, before_values)
+        second_matmul(BEFORE_LAST, 0)
+        nc.scalar.activation(*w2_views(last_values[:, 0:PIECE], late_raw[LAST, 0], 1), COPY)
+        relu_h(LAST, last_values[:, PIECE:])
+        nc.vector.tensor_copy(*closing_views(BEFORE_LAST, 1))
+        y_before = shared.tile([P, 1, C], F32, name="y6", align_bytes=ALIGN, offset=0)
         last_codes = shared.tile([P, P + C], U32, name="last_codes", align_bytes=ALIGN, offset=4 * C)
-        quantised[7] = (last_codes, last_scales)
-        quantize_late(1, 6, 7)
-        times_gate(6, y6[:])
+        quantised[LAST] = (last_codes, last_scales)
+        quantize_closing(1, BEFORE_LAST, LAST)
+        times_gate(BEFORE_LAST, y_before[:])
         nc.vector.quantize_mx(out=last_codes[:].bitcast(FP8X4), scales=last_scales[:], in_=last_values)
-        second_matmul(7, 0)
-        scatter_one(6, 0, y6[:, 0, :])
-        round_w2(False, late_values(7, 1), late_raw[7, 1], 1)
-        y7 = late_raw[7, 1][:, 0:C].rearrange("p (c s) -> p c s", c=1)
-        times_gate(7, y7)
-        quantize_late(1, 7, 8)
-        scatter_one(7, 0, y7[:, 0, :])
+        second_matmul(LAST, 0)
+        scatter_one(BEFORE_LAST, 0, y_before[:, 0, :])
+        nc.scalar.activation(*closing_views(LAST, 1), COPY)
+        y_last = late_raw[LAST, 1][:, 0:C].rearrange("p (c s) -> p c s", c=1)
+        times_gate(LAST, y_last)
+        quantize_closing(1, LAST, E)
+        scatter_one(LAST, 0, y_last[:, 0, :])
         store(0)
-        for e in range(first[2], E):
-            round_w2(False, late_values(e, 2), late_raw[e, 2], 1)
-        quantize_late(2, 5, 7)
-        quantize_late(2, 7, 8)
-        y_closing = {1: late_raw[7, 2][:, 0 : 2 * C], 2: y_closing2[:]}
-        for c, f in first.items():
-            for e in range(f, E):
+
+        for e in range(CLOSING_FIRST[2], E):
+            nc.scalar.activation(*closing_views(e, 2), COPY)
+        quantize_closing(2, CLOSING_FIRST[2], LAST)
+        quantize_closing(2, LAST, E)
+
+        y_closing = {1: late_raw[LAST, 2][:, 0 : (E - CLOSING_FIRST[1]) * C], 2: y_closing2[:]}
+        for c, first in CLOSING_FIRST.items():
+            for e in range(first, E):
                 second_matmul(e, c)
             nc.scalar.copy(y_closing[c], acc_closing[c][:])
-            nc.vector.tensor_tensor(places(c, f, E), y_closing[c], gate_sb[:, f * C : E * C], MULT)
+            scatter_group(c, first, E, y_closing[c])
             store(c)

@@ -37,7 +37,7 @@ PIECE = PACK * P
 EARLY = E - 2
 LAST_EARLY, BEFORE_LAST, LAST = EARLY - 1, E - 2, E - 1
 CLOSING_FIRST = {1: BEFORE_LAST, 2: LAST_EARLY}
-LATE_PIECES = [(e, c) for c in range(ROW_TILES) for e in range(CLOSING_FIRST.get(c, EARLY), E)]
+LATE_PIECES = [(LAST, 0), (BEFORE_LAST, 0)] + [(e, c) for c, first in CLOSING_FIRST.items() for e in range(first, E)]
 PAIR, PAIR_TILE = (LAST_EARLY - 1, LAST_EARLY), 1
 
 TILE_UNITS = 4
@@ -53,7 +53,6 @@ LAST_EARLY_CUT = 68
 LAST_EARLY_PASS0_CUT = 96
 BEFORE_LAST_PASS0_CUT = P // 2
 LAST_PASS0_CUT = 68
-LAST_CUT = 76
 Y_COLUMN = 320
 
 
@@ -94,11 +93,11 @@ def tile_moe_two_mlp_relu_kernel(
         late_raw = {
             (e, c): one(f"late_raw{e}{c}", [P, PIECE], F32)[:]
             for e, c in LATE_PIECES
-            if (e, c) not in ((LAST, 0), (BEFORE_LAST, 1))
+            if (e, c) not in ((BEFORE_LAST, 0), (BEFORE_LAST, 1))
         }
-        last_stage = one("stage70", [P, PIECE // 2 + PIECE], F32)
-        lent = shared.tile([P, PIECE], F32, name="late_raw61", align_bytes=ALIGN, offset=0)
-        late_raw[LAST, 0] = last_stage[:, PIECE // 2 :]
+        last_stage = one("last_stage", [P, PIECE // 2 + PIECE], F32)
+        lent = shared.tile([P, PIECE], F32, name="lent", align_bytes=ALIGN, offset=0)
+        late_raw[BEFORE_LAST, 0] = last_stage[:, PIECE // 2 :]
         late_raw[BEFORE_LAST, 1] = lent[:]
         last_scales = one("last_scales", [P, P + C], U8)
         late_bf16 = {c: one(f"late_bf16{c}", [P, (E - first) * PIECE], BF16) for c, first in CLOSING_FIRST.items()}
@@ -357,22 +356,21 @@ def tile_moe_two_mlp_relu_kernel(
         round_on_scalar(last1, 0, P // 2)
         quantize_and_multiply(last0, 1)
 
-        share_end = UNIT + PACK * LAST_CUT
+        share_end = UNIT + H // 2
         before_values = raw(last0, 2)[:, share_end - PIECE : share_end].bitcast(BF16)
         last_values = last_stage[:, 0:PIECE].bitcast(BF16)
-        round_on_scalar(last1, P // 2, LAST_CUT)
         relu_h(BEFORE_LAST, before_values[:, PIECE:])
         for t in range(0, PACK, 2):
-            round_on_vector(last1, LAST_CUT, P, t, t + 2)
+            round_on_vector(last1, P // 2, P, t, t + 2)
         quantize_and_multiply(last1, 2)
 
-        nc.vector.tensor_copy(*w2_views(before_values[:, 0:PIECE], late_raw[BEFORE_LAST, 0], 1))
+        nc.vector.tensor_copy(*w2_views(last_values[:, 0:PIECE], late_raw[LAST, 0], 1))
+        nc.scalar.activation(*w2_views(before_values[:, 0:PIECE], late_raw[BEFORE_LAST, 0], 1), COPY)
         quantize_w2h(BEFORE_LAST, 0, P + C, before_values)
         second_matmul(BEFORE_LAST, 0)
-        nc.scalar.activation(*w2_views(last_values[:, 0:PIECE], late_raw[LAST, 0], 1), COPY)
         relu_h(LAST, last_values[:, PIECE:])
         nc.vector.tensor_copy(*closing_views(BEFORE_LAST, 1))
-        y_before = shared.tile([P, 1, C], F32, name="y6", align_bytes=ALIGN, offset=0)
+        y_before = shared.tile([P, 1, C], F32, name="y_before", align_bytes=ALIGN, offset=0)
         last_codes = shared.tile([P, P + C], U32, name="last_codes", align_bytes=ALIGN, offset=4 * C)
         quantised[LAST] = (last_codes, last_scales)
         quantize_closing(1, BEFORE_LAST, LAST)

@@ -19,6 +19,7 @@ COPY = mybir.ActivationFunctionType.Copy
 RELU = mybir.ActivationFunctionType.Relu
 MULT = mybir.AluOpType.mult
 ADD = mybir.AluOpType.add
+MAX = mybir.AluOpType.max
 
 P = 128
 PACK = 4
@@ -33,27 +34,18 @@ ALIGN = 256
 
 UNIT = PACK * H
 PIECE = PACK * P
+LAST = E - 1
 
-EARLY = E - 2
-LAST_EARLY, BEFORE_LAST, LAST = EARLY - 1, E - 2, E - 1
-CLOSING_FIRST = {1: BEFORE_LAST, 2: LAST_EARLY}
-LATE_PIECES = [(LAST, 0), (BEFORE_LAST, 0)] + [(e, c) for c, first in CLOSING_FIRST.items() for e in range(first, E)]
-PAIR, PAIR_TILE = (LAST_EARLY - 1, LAST_EARLY), 1
+FIRST_LATE = (7, 5, 4)
+STREAM_GROUPS = {0: ((0, 2), (2, 4), (4, 6)), 1: ((0, 1), (1, 3), (3, 5)), 2: ((0, 2), (2, 4))}
+LATE_PIECES = ((5, 1), (6, 1), (7, 0), (4, 2), (5, 2), (7, 1), (6, 2), (7, 2))
 
-TILE_UNITS = 4
-CODE_DEPTH = 6
+RAW_DEPTH = 4
+ROUNDED_UNITS = 4
+CODE_DEPTH = 4
 W2_RAW_DEPTH = 3
-W2H_DEPTH = 4
 
-BOTH = 8
-SHARED = P - BOTH
-FIRST_CUT = 24
-STREAM_CUT = 52
-LAST_EARLY_CUT = 68
-LAST_EARLY_PASS0_CUT = 96
-BEFORE_LAST_PASS0_CUT = P // 2
-LAST_PASS0_CUT = 68
-Y_COLUMN = 320
+SCALAR_CUT = {0: 128, 1: 64, 9: 48, 13: 56}
 
 
 def tile_moe_two_mlp_relu_kernel(
@@ -62,7 +54,7 @@ def tile_moe_two_mlp_relu_kernel(
     nc = tc.nc
     with ExitStack() as ctx:
         keep = ctx.enter_context(tc.tile_pool(name="keep", bufs=1))
-        shared = ctx.enter_context(tc.tile_pool(name="shared", bufs=1))
+        placed = ctx.enter_context(tc.tile_pool(name="placed", bufs=1))
         psum = ctx.enter_context(tc.psum_pool(name="psum", bufs=1))
 
         def one(name, shape, dtype):
@@ -82,34 +74,40 @@ def tile_moe_two_mlp_relu_kernel(
         gate_sb = one("gate_sb", [P, S], F32)
         zeros = one("zeros", [P, C], F32)
         out_sb = ring("out_sb", ROW_TILES, [P, T], F32)
-        w1_raw = ring("w1_raw", 2, [P, TILE_UNITS * UNIT], F32)
-        w1_bf16 = one("w1_bf16", [P, TILE_UNITS * UNIT], BF16)
+        y_sb = one("y_sb", [P, ROW_TILES * S], F32)
+        even_bytes = 4 * (UNIT + PACK * N // 2)
+        even_first = W2_RAW_DEPTH * 4 * PACK * N
+        even_raw = [
+            placed.tile([P, UNIT + PACK * N // 2], F32, name=f"even_raw{e}", align_bytes=ALIGN, offset=even_first + e % RAW_DEPTH * even_bytes)
+            for e in range(E)
+        ]
+        odd_raw = ring("odd_raw", RAW_DEPTH, [P, UNIT], F32)
+        tail_bf16 = {e: one(f"tail_bf16{e}", [P, (C + P) * PACK], BF16) for e in (5, 6, 7)}
+        w1_bf16 = ring("w1_bf16", ROUNDED_UNITS, [P, UNIT], BF16)
         w1_codes = ring("w1_codes", CODE_DEPTH, [P, H], U32)
         w1_scales = ring("w1_scales", CODE_DEPTH, [P, H], U8)
-        w2_raw = ring("w2_raw", W2_RAW_DEPTH, [P, PACK * N], F32)
-        w2h_bf16 = ring("w2h_bf16", W2H_DEPTH, [P, (C + N) * PACK], BF16)
-        w2h_codes = ring("w2h_codes", W2H_DEPTH, [P, C + N], U32)
-        w2h_scales = ring("w2h_scales", W2H_DEPTH, [P, C + N], U8)
+        w2_first = 0
+        w2_raw = [
+            placed.tile([P, PACK * N], F32, name=f"w2_raw{e}", align_bytes=ALIGN, offset=w2_first + e % W2_RAW_DEPTH * 4 * PACK * N)
+            for e in range(LAST)
+        ]
+        w2h_codes = ring("w2h_codes", E, [P, C + N], U32)
+        w2h_scales = [
+            placed.tile([P, C + N], U8, name=f"w2h_scales{e}", align_bytes=ALIGN, offset=even_first + (e + 1) % RAW_DEPTH * even_bytes)
+            if e in (5, 6)
+            else one(f"w2h_scales{e}", [P, C + N], U8)
+            for e in range(E)
+        ]
         late_raw = {
-            (e, c): one(f"late_raw{e}{c}", [P, PIECE], F32)[:]
-            for e, c in LATE_PIECES
-            if (e, c) not in ((BEFORE_LAST, 0), (BEFORE_LAST, 1))
+            (e, c): placed.tile([P, PIECE], F32, name=f"late_raw{e}{c}", align_bytes=ALIGN, offset=w2_first + (place + 3) % 9 * 4 * PIECE)
+            for place, (e, c) in enumerate(LATE_PIECES)
         }
-        last_stage = one("last_stage", [P, PIECE // 2 + PIECE], F32)
-        lent = shared.tile([P, PIECE], F32, name="lent", align_bytes=ALIGN, offset=0)
-        late_raw[BEFORE_LAST, 0] = last_stage[:, PIECE // 2 :]
-        late_raw[BEFORE_LAST, 1] = lent[:]
-        last_scales = one("last_scales", [P, P + C], U8)
-        late_bf16 = {c: one(f"late_bf16{c}", [P, (E - first) * PIECE], BF16) for c, first in CLOSING_FIRST.items()}
-        late_codes = {c: one(f"late_codes{c}", [P, (E - first) * P], U32) for c, first in CLOSING_FIRST.items()}
-        late_scales = {c: one(f"late_scales{c}", [P, (E - first) * P], U8) for c, first in CLOSING_FIRST.items()}
-        y_closing2 = one("y_closing2", [P, (E - CLOSING_FIRST[2]) * C], F32)
+        late_bf16 = {c: one(f"late_bf16{c}", [P, (E - FIRST_LATE[c]) * PIECE], BF16) for c in (1, 2)}
+        late_codes = {c: one(f"late_codes{c}", [P, (E - FIRST_LATE[c]) * P], U32) for c in (1, 2)}
+        late_scales = {c: one(f"late_scales{c}", [P, (E - FIRST_LATE[c]) * P], U8) for c in (1, 2)}
         acc1 = [psum.tile([P, PACK, C], F32, name=f"acc1_{i}") for i in range(2)]
         acc2 = [psum.tile([P, ROW_TILES, C], F32, name=f"acc2_{i}") for i in range(2)]
-        acc_pair = psum.tile([P, len(PAIR) * C], F32, name="acc_pair")
-        acc_closing = {
-            c: psum.tile([P, (E - first) * C], F32, name=f"acc_closing{c}") for c, first in CLOSING_FIRST.items()
-        }
+        acc_late = [psum.tile([P, PACK * C], F32, name=f"acc_late{i}") for i in range(4)]
 
         def load_words(o):
             nc.sync.dma_start(tok_words[o][:], x_words[o].rearrange("p t r -> p (t r)").bitcast(I32))
@@ -131,48 +129,38 @@ def tile_moe_two_mlp_relu_kernel(
                     nc.tensor.transpose(bank[:, q, :], gate_row[:, column : column + 1].to_broadcast([P, P]), identity[:])
                 nc.scalar.copy(by_slot[:, :, half * PACK : (half + 1) * PACK], bank[:].rearrange("p q n -> p n q"))
 
-        def raw(u, count=1):
-            return w1_raw[u // TILE_UNITS % 2][:, u % TILE_UNITS * UNIT : (u % TILE_UNITS + count) * UNIT]
-
-        def raw_rows(u):
-            return raw(u).rearrange("p (j i) -> p j i", j=PACK)
-
-        def rounded(u, count=1):
-            return w1_bf16[:, u % TILE_UNITS * UNIT : (u % TILE_UNITS + count) * UNIT]
-
         def w1_rows(u):
-            return w1[u // PASSES, u % PASSES * K_PASS : (u % PASSES + 1) * K_PASS, :]
+            rows = w1[u // PASSES, u % PASSES * K_PASS : (u % PASSES + 1) * K_PASS, :]
+            return rows.rearrange("(p j) i -> p j i", j=PACK)
 
-        def load_unit(u):
-            nc.sync.dma_start(raw(u), w1_rows(u).rearrange("(p j) i -> p (j i)", j=PACK))
+        def raw(u):
+            return (odd_raw[u // PASSES % RAW_DEPTH] if u % PASSES else even_raw[u // PASSES])[:, 0:UNIT]
 
-        def rounding_views(u, count):
-            target = rounded(u, count).rearrange("p (o t m j) -> p o m j t", o=count, j=PACK, t=PACK)
-            source = raw(u, count).rearrange("p (o j m t) -> p o m j t", o=count, j=PACK, t=PACK)
-            return target, source
+        def load_unit(u, first=0, end=H):
+            target = raw(u).rearrange("p (j i) -> p j i", j=PACK)
+            nc.sync.dma_start(target[:, :, first:end], w1_rows(u)[:, :, first:end])
 
-        def round_on_scalar(u, first, end):
-            target, source = rounding_views(u, 1)
-            nc.scalar.activation(target[:, 0, first:end], source[:, 0, first:end], COPY)
+        def round_copy(on_scalar, target, source):
+            if on_scalar:
+                nc.scalar.activation(target, source, COPY)
+            else:
+                nc.vector.tensor_copy(target, source)
 
-        def round_on_vector(u, first, end, t_first=0, t_end=PACK):
-            target, source = rounding_views(u, 1)
-            nc.vector.tensor_copy(target[:, 0, first:end, :, t_first:t_end], source[:, 0, first:end, :, t_first:t_end])
+        def round_unit(u, on_scalar, first, end):
+            target = w1_bf16[u % ROUNDED_UNITS][:].rearrange("p (t m j) -> p m j t", j=PACK, t=PACK)
+            source = raw(u).rearrange("p (j m t) -> p m j t", j=PACK, t=PACK)
+            if end > first:
+                round_copy(on_scalar, target[:, first:end], source[:, first:end])
 
-        def round_both(u):
-            target, source = rounding_views(u, 2)
-            nc.vector.tensor_copy(target[:, :, SHARED:P], source[:, :, SHARED:P])
+        def quantize(codes, scales, values):
+            nc.vector.quantize_mx(out=codes.bitcast(FP8X4), scales=scales, in_=values)
 
         def quantize_and_multiply(u, parts):
             codes, scales = w1_codes[u % CODE_DEPTH], w1_scales[u % CODE_DEPTH]
             width = H // parts
             for a in range(parts):
                 cols = slice(a * width, (a + 1) * width)
-                nc.vector.quantize_mx(
-                    out=codes[:, cols].bitcast(FP8X4),
-                    scales=scales[:, cols],
-                    in_=rounded(u)[:, a * width * PACK : (a + 1) * width * PACK],
-                )
+                quantize(codes[:, cols], scales[:, cols], w1_bf16[u % ROUNDED_UNITS][:, a * width * PACK : (a + 1) * width * PACK])
             e, o = divmod(u, PASSES)
             slots = slice(e * C, (e + 1) * C)
             for t in range(PACK):
@@ -187,90 +175,83 @@ def tile_moe_two_mlp_relu_kernel(
                     stop=(o == PASSES - 1 and t == PACK - 1),
                 )
 
-        def relu_h(e, h):
-            nc.scalar.activation(
-                h.rearrange("p (s t) -> p s t", t=PACK),
-                acc1[e % 2][:].rearrange("p t s -> p s t"),
-                RELU,
-            )
+        def w2h_values(e, first, end):
+            if e in tail_bf16:
+                return tail_bf16[e][:, first * PACK : end * PACK]
+            start = UNIT - C * PACK // 2
+            return even_raw[e + 1][:, start + first * PACK // 2 : start + end * PACK // 2].bitcast(BF16)
+
+        def relu_h(e, on_scalar):
+            h = w2h_values(e, 0, C).rearrange("p (s t) -> p s t", t=PACK)
+            sums = acc1[e % 2][:].rearrange("p t s -> p s t")
+            if on_scalar:
+                nc.scalar.activation(h, sums, RELU)
+            else:
+                nc.vector.tensor_scalar(h, sums, 0.0, None, MAX)
 
         def w2_rows(e, first, end):
             return w2[e].rearrange("(p j) n -> p j n", j=PACK)[:, :, first * P : end * P]
 
-        def load_w2(e, tiles):
-            target = w2_raw[e % W2_RAW_DEPTH][:].rearrange("p (j n) -> p j n", j=PACK)
-            nc.sync.dma_start(target[:, :, 0 : tiles * P], w2_rows(e, 0, tiles))
-
-        def w2h_values(e, first, end):
-            return w2h_bf16[e % W2H_DEPTH][:, first * PACK : end * PACK]
-
-        def w2_views(values, landed, tiles):
+        def round_w2(on_scalar, values, landed, tiles):
             target = values.rearrange("p (g n j) -> p g j n", n=RUN, j=PACK)
             source = landed.rearrange("p (j g n) -> p g j n", j=PACK, n=RUN)
-            return target, source[:, 0 : tiles * P // RUN]
+            round_copy(on_scalar, target, source[:, 0 : tiles * P // RUN])
 
-        def quantize_w2h(e, first, end, values):
-            nc.vector.quantize_mx(
-                out=w2h_codes[e % W2H_DEPTH][:, first:end].bitcast(FP8X4),
-                scales=w2h_scales[e % W2H_DEPTH][:, first:end],
-                in_=values,
-            )
+        def quantize_w2h(e, tiles):
+            end = C + tiles * P
+            quantize(w2h_codes[e][:, 0:end], w2h_scales[e][:, 0:end], w2h_values(e, 0, end))
 
-        def closing_views(e, c):
-            place = e - CLOSING_FIRST[c]
-            return w2_views(late_bf16[c][:, place * PIECE : (place + 1) * PIECE], late_raw[e, c], 1)
-
-        def quantize_closing(c, first_expert, end_expert):
-            first, end = (first_expert - CLOSING_FIRST[c]) * P, (end_expert - CLOSING_FIRST[c]) * P
-            nc.vector.quantize_mx(
-                out=late_codes[c][:, first:end].bitcast(FP8X4),
-                scales=late_scales[c][:, first:end],
-                in_=late_bf16[c][:, first * PACK : end * PACK],
-            )
-
-        def closing(e, c):
-            return e >= CLOSING_FIRST.get(c, E)
-
-        def alone(e):
-            return [c for c in range(ROW_TILES) if not closing(e, c) and not (e in PAIR and c == PAIR_TILE)]
-
-        quantised = {e: (w2h_codes[e % W2H_DEPTH], w2h_scales[e % W2H_DEPTH]) for e in range(LAST)}
-
-        def second_matmul(e, c):
-            h_codes, h_scales = quantised[e]
-            h_first = 0 if e < EARLY else P
-            codes, scales, first = h_codes, h_scales, (C + c * P if e < EARLY else 0)
-            if closing(e, c):
-                place = e - CLOSING_FIRST[c]
-                sums = acc_closing[c][:, place * C : (place + 1) * C]
-                codes, scales, first = late_codes[c], late_scales[c], place * P
-            elif c in alone(e):
-                sums = acc2[e % 2][:, alone(e).index(c), :]
-            else:
-                sums = acc_pair[:, PAIR.index(e) * C : (PAIR.index(e) + 1) * C]
+        def second_matmul(sums, e, codes, scales):
             nc.tensor.matmul_mx(
                 out=sums,
-                lhsT=codes[:, first : first + P].bitcast(FP8X4),
-                lhsT_scale=scales[:, first : first + P],
-                rhs=h_codes[:, h_first : h_first + C].bitcast(FP8X4),
-                rhs_scale=h_scales[:, h_first : h_first + C],
+                lhsT=codes.bitcast(FP8X4),
+                lhsT_scale=scales,
+                rhs=w2h_codes[e][:, 0:C].bitcast(FP8X4),
+                rhs_scale=w2h_scales[e][:, 0:C],
                 start=True,
                 stop=True,
             )
 
+        def y_rows(c, first, end):
+            return y_sb[:, c * S + first * C : c * S + end * C]
+
+        def second_layer(e, tiles):
+            for c in range(tiles):
+                cols = slice(C + c * P, C + (c + 1) * P)
+                second_matmul(acc2[e % 2][:, c, :], e, w2h_codes[e][:, cols], w2h_scales[e][:, cols])
+
+        def times_gate(e, tiles):
+            y = y_sb[:].rearrange("p (c s) -> p c s", c=ROW_TILES)[:, 0:tiles, e * C : (e + 1) * C]
+            gates = gate_sb[:, e * C : (e + 1) * C].rearrange("p (c s) -> p c s", c=1).to_broadcast([P, tiles, C])
+            nc.vector.tensor_tensor(y, acc2[e % 2][:, 0:tiles, :], gates, MULT)
+
         def places(c, first, end):
             return out_sb[c][:].indirect(dst_list[:, first * C // LIST_ROWS : end * C // LIST_ROWS])
 
-        def times_gate(e, y):
-            count = y.shape[1]
-            gates = gate_sb[:, e * C : (e + 1) * C].rearrange("p (c s) -> p c s", c=1).to_broadcast([P, count, C])
-            nc.vector.tensor_tensor(y, acc2[e % 2][:, 0:count, :], gates, MULT)
+        def scatter_group(c, first, end):
+            nc.scalar.activation(places(c, first, end), y_rows(c, first, end), COPY)
 
-        def scatter_one(e, c, y):
-            nc.vector.tensor_tensor(places(c, e, e + 1), y, zeros[:], ADD)
+        def scatter_one(c, e, y=None):
+            nc.vector.tensor_tensor(places(c, e, e + 1), y_rows(c, e, e + 1) if y is None else y, zeros[:], ADD)
 
-        def scatter_group(c, first, end, y):
-            nc.vector.tensor_tensor(places(c, first, end), y, gate_sb[:, first * C : end * C], MULT)
+        def staged_gate(e, y):
+            nc.vector.tensor_tensor(y, acc2[e % 2][:, 0, :], gate_sb[:, e * C : (e + 1) * C], MULT)
+
+        def round_late(on_scalar, e, c):
+            place = e - FIRST_LATE[c]
+            round_w2(on_scalar, late_bf16[c][:, place * PIECE : (place + 1) * PIECE], late_raw[e, c][:], 1)
+
+        def late_sums(c, first, end, bank):
+            a, b = first - FIRST_LATE[c], end - FIRST_LATE[c]
+            quantize(late_codes[c][:, a * P : b * P], late_scales[c][:, a * P : b * P], late_bf16[c][:, a * PIECE : b * PIECE])
+            for e in range(first, end):
+                cols = slice((e - FIRST_LATE[c]) * P, (e - FIRST_LATE[c] + 1) * P)
+                second_matmul(acc_late[bank][:, (e - first) * C : (e - first + 1) * C], e, late_codes[c][:, cols], late_scales[c][:, cols])
+
+        def late_gate(c, first, end, bank):
+            nc.vector.tensor_tensor(
+                y_rows(c, first, end), acc_late[bank][:, 0 : (end - first) * C], gate_sb[:, first * C : end * C], MULT
+            )
 
         def store(c):
             nc.sync.dma_start(out[c * P : (c + 1) * P, :], out_sb[c][:])
@@ -294,106 +275,100 @@ def tile_moe_two_mlp_relu_kernel(
         make_identity(nc, identity[:])
         spread_gate()
 
-        for e in range(EARLY):
+        def stream_tiles(e):
+            return len([c for c in range(ROW_TILES) if e < FIRST_LATE[c]])
+
+        def scatter_closed(e):
+            for c, groups in STREAM_GROUPS.items():
+                for first, end in groups:
+                    if end == e + 1 and end - first > 1:
+                        scatter_group(c, first, end)
+                    elif end == e + 1:
+                        scatter_one(c, first)
+
+        def round_shared(u):
+            cut = SCALAR_CUT.get(u, 0)
+            round_unit(u, True, 0, cut)
+            if u % PASSES == 0 and cut < P // 2 and u < 12:
+                round_unit(u, False, P // 2, P)
+                round_unit(u, False, cut, P // 2)
+            else:
+                round_unit(u, False, cut, P)
+
+        def load_and_round_w2(e):
+            tiles = stream_tiles(e)
+            landed = w2_raw[e][:]
+            nc.sync.dma_start(landed.rearrange("p (j n) -> p j n", j=PACK)[:, :, 0 : tiles * P], w2_rows(e, 0, tiles))
+            round_w2(True, w2h_values(e, C, C + tiles * P), landed, tiles)
+
+        def second(e):
+            quantize_w2h(e, stream_tiles(e))
+            second_layer(e, stream_tiles(e))
+
+        for e in range(E):
             pass0, pass1 = PASSES * e, PASSES * e + 1
-            tiles = len([c for c in range(ROW_TILES) if (e, c) not in LATE_PIECES])
+            if e < LAST:
+                load_and_round_w2(e)
             load_unit(pass0)
-            load_unit(pass1)
+            if e < LAST:
+                load_unit(pass1)
             if e == 0:
                 nc.sync.dma_start(dst_list[:], dst)
-            load_w2(e, tiles)
-            if e == LAST_EARLY:
-                round_on_scalar(pass0, 0, LAST_EARLY_PASS0_CUT)
-                round_on_vector(pass0, LAST_EARLY_PASS0_CUT, SHARED)
-            else:
-                round_on_scalar(pass0, 0, SHARED)
-            cut = {0: FIRST_CUT, LAST_EARLY: LAST_EARLY_CUT}.get(e, STREAM_CUT)
-            round_on_scalar(pass1, 0, cut)
-            round_both(pass0)
-            round_on_vector(pass1, cut, SHARED)
-            due = alone(e - 1) if e > 0 else []
-            if due:
-                y = raw_rows(pass1)[:, 0 : len(due), Y_COLUMN : Y_COLUMN + C]
-                times_gate(e - 1, y)
+            round_shared(pass0)
+            if e > 0:
+                relu_h(e - 1, e > 5)
+            if e == LAST:
+                break
             quantize_and_multiply(pass0, 1)
-            quantize_and_multiply(pass1, 2 if e == LAST_EARLY else 1)
-            for place, c in enumerate(due):
-                scatter_one(e - 1, c, y[:, place, :])
-            nc.scalar.activation(*w2_views(w2h_values(e, C, C + tiles * P), w2_raw[e % W2_RAW_DEPTH][:], tiles), COPY)
-            relu_h(e, w2h_values(e, 0, C))
-            if tiles == ROW_TILES:
-                quantize_w2h(e, 0, C + N, w2h_values(e, 0, C + N))
-            else:
-                quantize_w2h(e, C + P, C + 2 * P, w2h_values(e, C + P, C + 2 * P))
-                quantize_w2h(e, 0, C + P, w2h_values(e, 0, C + P))
-            for c in range(tiles):
-                second_matmul(e, c)
+            if e > 0:
+                second(e - 1)
+            round_shared(pass1)
+            if e > 0:
+                times_gate(e - 1, stream_tiles(e - 1))
+            quantize_and_multiply(pass1, 2 if e == 6 else 1)
+            scatter_closed(e - 1)
 
-        before0, before1, last0, last1 = range(PASSES * BEFORE_LAST, PASSES * E)
-        for u in (before0, before1, last0):
-            load_unit(u)
+        last0, last1 = PASSES * LAST, PASSES * LAST + 1
         for half in range(2):
-            cols = slice(half * H // 2, (half + 1) * H // 2)
-            nc.sync.dma_start(raw_rows(last1)[:, :, cols], w1_rows(last1).rearrange("(p j) i -> p j i", j=PACK)[:, :, cols])
+            load_unit(last1, half * H // 2, (half + 1) * H // 2)
         for e, c in LATE_PIECES:
-            nc.sync.dma_start(late_raw[e, c].rearrange("p (j n) -> p j n", j=PACK), w2_rows(e, c, c + 1))
-
-        round_on_scalar(before0, 0, BEFORE_LAST_PASS0_CUT)
-        round_on_vector(before0, BEFORE_LAST_PASS0_CUT, P)
-        y_alone = raw_rows(before0)[:, 0:1, 0:C]
-        y_pair = raw_rows(before0)[:, 1, 0 : len(PAIR) * C]
-        times_gate(LAST_EARLY, y_alone)
-        nc.scalar.copy(y_pair, acc_pair[:])
-        quantize_and_multiply(before0, 1)
-        scatter_one(LAST_EARLY, 0, y_alone[:, 0, :])
-        scatter_group(PAIR_TILE, PAIR[0], EARLY, y_pair)
-
-        round_on_scalar(before1, 0, SHARED)
-        round_on_scalar(last0, 0, LAST_PASS0_CUT)
-        round_both(before1)
-        round_on_vector(last0, LAST_PASS0_CUT, SHARED)
-        quantize_and_multiply(before1, 2)
-        round_on_scalar(last1, 0, P // 2)
+            nc.sync.dma_start(late_raw[e, c][:].rearrange("p (j n) -> p j n", j=PACK), w2_rows(e, c, c + 1))
+        round_unit(last1, True, 0, 40)
+        round_unit(last1, False, 40, P // 2)
         quantize_and_multiply(last0, 1)
-
-        share_end = UNIT + H // 2
-        before_values = raw(last0, 2)[:, share_end - PIECE : share_end].bitcast(BF16)
-        last_values = last_stage[:, 0:PIECE].bitcast(BF16)
-        relu_h(BEFORE_LAST, before_values[:, PIECE:])
-        for t in range(0, PACK, 2):
-            round_on_vector(last1, P // 2, P, t, t + 2)
+        second(6)
+        round_unit(last1, False, P // 2, 108)
+        round_unit(last1, True, 108, P)
         quantize_and_multiply(last1, 2)
-
-        nc.vector.tensor_copy(*w2_views(last_values[:, 0:PIECE], late_raw[LAST, 0], 1))
-        nc.scalar.activation(*w2_views(before_values[:, 0:PIECE], late_raw[BEFORE_LAST, 0], 1), COPY)
-        quantize_w2h(BEFORE_LAST, 0, P + C, before_values)
-        second_matmul(BEFORE_LAST, 0)
-        relu_h(LAST, last_values[:, PIECE:])
-        nc.vector.tensor_copy(*closing_views(BEFORE_LAST, 1))
-        y_before = shared.tile([P, 1, C], F32, name="y_before", align_bytes=ALIGN, offset=0)
-        last_codes = shared.tile([P, P + C], U32, name="last_codes", align_bytes=ALIGN, offset=4 * C)
-        quantised[LAST] = (last_codes, last_scales)
-        quantize_closing(1, BEFORE_LAST, LAST)
-        times_gate(BEFORE_LAST, y_before[:])
-        nc.vector.quantize_mx(out=last_codes[:].bitcast(FP8X4), scales=last_scales[:], in_=last_values)
-        second_matmul(LAST, 0)
-        scatter_one(BEFORE_LAST, 0, y_before[:, 0, :])
-        nc.scalar.activation(*closing_views(LAST, 1), COPY)
-        y_last = late_raw[LAST, 1][:, 0:C].rearrange("p (c s) -> p c s", c=1)
-        times_gate(LAST, y_last)
-        quantize_closing(1, LAST, E)
-        scatter_one(LAST, 0, y_last[:, 0, :])
+        round_late(True, 5, 1)
+        round_late(True, 6, 1)
+        round_w2(False, w2h_values(LAST, C, C + P), late_raw[LAST, 0][:], 1)
+        relu_h(LAST, True)
+        y_six = late_raw[6, 1][:, 0:C]
+        staged_gate(6, y_six)
+        late_sums(1, 5, 7, 0)
+        scatter_one(0, 6, y_six)
+        quantize_w2h(LAST, 1)
+        second_layer(LAST, 1)
+        round_late(True, 4, 2)
+        round_late(True, 5, 2)
+        late_gate(1, 5, 7, 0)
+        scatter_group(1, 5, 7)
+        round_late(False, 7, 1)
+        y_last = late_raw[5, 2][:, 0:C]
+        staged_gate(LAST, y_last)
+        late_sums(2, 4, 6, 1)
+        scatter_one(0, LAST, y_last)
         store(0)
-
-        for e in range(CLOSING_FIRST[2], E):
-            nc.scalar.activation(*closing_views(e, 2), COPY)
-        quantize_closing(2, CLOSING_FIRST[2], LAST)
-        quantize_closing(2, LAST, E)
-
-        y_closing = {1: late_raw[LAST, 2][:, 0 : (E - CLOSING_FIRST[1]) * C], 2: y_closing2[:]}
-        for c, first in CLOSING_FIRST.items():
-            for e in range(first, E):
-                second_matmul(e, c)
-            nc.scalar.copy(y_closing[c], acc_closing[c][:])
-            scatter_group(c, first, E, y_closing[c])
-            store(c)
+        late_sums(1, 7, 8, 2)
+        late_gate(2, 4, 6, 1)
+        round_late(True, 6, 2)
+        scatter_group(2, 4, 6)
+        round_late(False, 7, 2)
+        late_gate(1, 7, 8, 2)
+        late_sums(2, 6, 8, 3)
+        scatter_one(1, LAST)
+        store(1)
+        late_gate(2, 6, 8, 3)
+        scatter_group(2, 6, 8)
+        store(2)

@@ -41,11 +41,13 @@ STREAM_GROUPS = {0: ((0, 2), (2, 4), (4, 6)), 1: ((0, 1), (1, 3), (3, 5)), 2: ((
 LATE_PIECES = ((5, 1), (6, 1), (7, 0), (4, 2), (5, 2), (7, 1), (6, 2), (7, 2))
 
 RAW_DEPTH = 4
+WHOLE = 3
+PAIRED = 2
 ROUNDED_UNITS = 4
 CODE_DEPTH = 4
 W2_RAW_DEPTH = 3
 
-SCALAR_CUT = {0: 128, 1: 64, 9: 48, 13: 56}
+SCALAR_CUT = {0: 64, 1: 64, 3: 64, 5: 128, 9: 48, 11: 40, 13: 56}
 
 
 def tile_moe_two_mlp_relu_kernel(
@@ -65,7 +67,7 @@ def tile_moe_two_mlp_relu_kernel(
 
         src_list = one("src_list", [P, S // LIST_ROWS], U16)
         dst_list = one("dst_list", [P, S // LIST_ROWS], U16)
-        tok_words = ring("tok_words", PASSES, [P, T], I32)
+        tok_words = one("tok_words", [P, PASSES * T], I32)
         tok_scales = one("tok_scales", [P, T], U8)
         slot_words = ring("slot_words", PASSES, [P, S], U32)
         slot_scales = one("slot_scales", [P, S], U8)
@@ -75,25 +77,35 @@ def tile_moe_two_mlp_relu_kernel(
         zeros = one("zeros", [P, C], F32)
         out_sb = ring("out_sb", ROW_TILES, [P, T], F32)
         y_sb = one("y_sb", [P, ROW_TILES * S], F32)
-        even_bytes = 4 * (UNIT + PACK * N // 2)
+        even_values = UNIT + PACK * N // 2
+        slot_bytes = 4 * (even_values + UNIT)
         even_first = W2_RAW_DEPTH * 4 * PACK * N
-        even_raw = [
-            placed.tile([P, UNIT + PACK * N // 2], F32, name=f"even_raw{e}", align_bytes=ALIGN, offset=even_first + e % RAW_DEPTH * even_bytes)
-            for e in range(E)
-        ]
-        odd_raw = ring("odd_raw", RAW_DEPTH, [P, UNIT], F32)
+
+        def slot(name, e, first, values):
+            offset = even_first + e % RAW_DEPTH * slot_bytes + 4 * first
+            return placed.tile([P, values], F32, name=f"{name}{e}", align_bytes=ALIGN, offset=offset)
+
+        whole = {e: slot("whole_raw", e, 0, UNIT + even_values) for e in range(WHOLE)}
+        even_raw = [whole[e][:, UNIT:] if e < WHOLE else slot("even_raw", e, UNIT, even_values)[:] for e in range(E)]
+        odd_raw = [whole[e][:, 0:UNIT] if e < WHOLE else slot("odd_raw", e, 0, UNIT)[:] for e in range(E)]
         tail_bf16 = {e: one(f"tail_bf16{e}", [P, (C + P) * PACK], BF16) for e in (5, 6, 7)}
         w1_bf16 = ring("w1_bf16", ROUNDED_UNITS, [P, UNIT], BF16)
         w1_codes = ring("w1_codes", CODE_DEPTH, [P, H], U32)
         w1_scales = ring("w1_scales", CODE_DEPTH, [P, H], U8)
         w2_first = 0
+        w2_pair = {
+            e: placed.tile([P, 2 * PACK * N], F32, name=f"w2_pair{e}", align_bytes=ALIGN, offset=e // 2 * 4 * PACK * N)
+            for e in range(0, PAIRED, 2)
+        }
         w2_raw = [
-            placed.tile([P, PACK * N], F32, name=f"w2_raw{e}", align_bytes=ALIGN, offset=w2_first + e % W2_RAW_DEPTH * 4 * PACK * N)
+            w2_pair[e - e % 2][:, e % 2 * PACK * N : (e % 2 + 1) * PACK * N]
+            if e < PAIRED
+            else placed.tile([P, PACK * N], F32, name=f"w2_raw{e}", align_bytes=ALIGN, offset=w2_first + e % W2_RAW_DEPTH * 4 * PACK * N)[:]
             for e in range(LAST)
         ]
         w2h_codes = ring("w2h_codes", E, [P, C + N], U32)
         w2h_scales = [
-            placed.tile([P, C + N], U8, name=f"w2h_scales{e}", align_bytes=ALIGN, offset=even_first + (e + 1) % RAW_DEPTH * even_bytes)
+            placed.tile([P, C + N], U8, name=f"w2h_scales{e}", align_bytes=ALIGN, offset=even_first + (e + 1) % RAW_DEPTH * slot_bytes + 4 * UNIT)
             if e in (5, 6)
             else one(f"w2h_scales{e}", [P, C + N], U8)
             for e in range(E)
@@ -109,8 +121,11 @@ def tile_moe_two_mlp_relu_kernel(
         acc2 = [psum.tile([P, ROW_TILES, C], F32, name=f"acc2_{i}") for i in range(2)]
         acc_late = [psum.tile([P, PACK * C], F32, name=f"acc_late{i}") for i in range(4)]
 
-        def load_words(o):
-            nc.sync.dma_start(tok_words[o][:], x_words[o].rearrange("p t r -> p (t r)").bitcast(I32))
+        def load_words():
+            nc.sync.dma_start(
+                tok_words[:].rearrange("p (o t) -> p o t", o=PASSES),
+                x_words.rearrange("o p t r -> p o (t r)").bitcast(I32),
+            )
 
         def load_scales(rows):
             for r in rows:
@@ -130,15 +145,28 @@ def tile_moe_two_mlp_relu_kernel(
                 nc.scalar.copy(by_slot[:, :, half * PACK : (half + 1) * PACK], bank[:].rearrange("p q n -> p n q"))
 
         def w1_rows(u):
-            rows = w1[u // PASSES, u % PASSES * K_PASS : (u % PASSES + 1) * K_PASS, :]
+            o = PASSES - 1 - u % PASSES
+            rows = w1[u // PASSES, o * K_PASS : (o + 1) * K_PASS, :]
             return rows.rearrange("(p j) i -> p j i", j=PACK)
 
         def raw(u):
-            return (odd_raw[u // PASSES % RAW_DEPTH] if u % PASSES else even_raw[u // PASSES])[:, 0:UNIT]
+            return (odd_raw[u // PASSES] if u % PASSES else even_raw[u // PASSES])[:, 0:UNIT]
 
         def load_unit(u, first=0, end=H):
             target = raw(u).rearrange("p (j i) -> p j i", j=PACK)
             nc.sync.dma_start(target[:, :, first:end], w1_rows(u)[:, :, first:end])
+
+        def load_expert(e):
+            nc.sync.dma_start(
+                whole[e][:, 0 : PASSES * UNIT].rearrange("p (o x) -> p o x", o=PASSES),
+                w1[e].rearrange("(o p j) i -> p o (j i)", o=PASSES, j=PACK),
+            )
+
+        def load_w2_pair(e):
+            nc.sync.dma_start(
+                w2_pair[e][:].rearrange("p (a x) -> p a x", a=2),
+                w2[e : e + 2].rearrange("a (p j) n -> p a (j n)", j=PACK),
+            )
 
         def round_copy(on_scalar, target, source):
             if on_scalar:
@@ -161,7 +189,8 @@ def tile_moe_two_mlp_relu_kernel(
             for a in range(parts):
                 cols = slice(a * width, (a + 1) * width)
                 quantize(codes[:, cols], scales[:, cols], w1_bf16[u % ROUNDED_UNITS][:, a * width * PACK : (a + 1) * width * PACK])
-            e, o = divmod(u, PASSES)
+            e, turn = divmod(u, PASSES)
+            o = PASSES - 1 - turn
             slots = slice(e * C, (e + 1) * C)
             for t in range(PACK):
                 cols = slice(t * P, (t + 1) * P)
@@ -171,8 +200,8 @@ def tile_moe_two_mlp_relu_kernel(
                     lhsT_scale=scales[:, cols],
                     rhs=slot_words[o][:, slots].bitcast(FP8X4),
                     rhs_scale=slot_scales[SCALE_ROWS * o : P, slots],
-                    start=(o == 0 and t == 0),
-                    stop=(o == PASSES - 1 and t == PACK - 1),
+                    start=(turn == 0 and t == 0),
+                    stop=(turn == PASSES - 1 and t == PACK - 1),
                 )
 
         def w2h_values(e, first, end):
@@ -263,14 +292,14 @@ def tile_moe_two_mlp_relu_kernel(
         for c in range(1, ROW_TILES):
             nc.scalar.copy(out_sb[c][:].rearrange("p (a s) -> p a s", s=C), repeated)
 
-        load_words(0)
+        load_words()
         nc.sync.dma_start(src_list[:], offs)
         load_scales((0, 1))
-        load_words(1)
+        load_w2_pair(0)
         nc.sync.dma_start(gate_row[:], gate[0].rearrange("(n q) -> n q", n=P))
         load_scales((2, 3))
         for o in range(PASSES):
-            nc.vector.tensor_copy(slot_words[o][:], tok_words[o][:].bitcast(U32).indirect(src_list[:]))
+            nc.vector.tensor_copy(slot_words[o][:], tok_words[:, o * T : (o + 1) * T].bitcast(U32).indirect(src_list[:]))
         nc.vector.tensor_copy(slot_scales[:], tok_scales[:].indirect(src_list[:]))
         make_identity(nc, identity[:])
         spread_gate()
@@ -297,8 +326,11 @@ def tile_moe_two_mlp_relu_kernel(
 
         def load_and_round_w2(e):
             tiles = stream_tiles(e)
-            landed = w2_raw[e][:]
-            nc.sync.dma_start(landed.rearrange("p (j n) -> p j n", j=PACK)[:, :, 0 : tiles * P], w2_rows(e, 0, tiles))
+            landed = w2_raw[e]
+            if e >= PAIRED:
+                nc.sync.dma_start(landed.rearrange("p (j n) -> p j n", j=PACK)[:, :, 0 : tiles * P], w2_rows(e, 0, tiles))
+            elif e % 2 == 0 and e > 0:
+                load_w2_pair(e)
             round_w2(True, w2h_values(e, C, C + tiles * P), landed, tiles)
 
         def second(e):
@@ -307,10 +339,13 @@ def tile_moe_two_mlp_relu_kernel(
 
         for e in range(E):
             pass0, pass1 = PASSES * e, PASSES * e + 1
-            if e < LAST:
+            if e < LAST - 1:
                 load_and_round_w2(e)
-            load_unit(pass0)
-            if e < LAST:
+            if e < WHOLE:
+                load_expert(e)
+            else:
+                load_unit(pass0)
+            if WHOLE <= e < LAST:
                 load_unit(pass1)
             if e == 0:
                 nc.sync.dma_start(dst_list[:], dst)
@@ -326,6 +361,8 @@ def tile_moe_two_mlp_relu_kernel(
             if e > 0:
                 times_gate(e - 1, stream_tiles(e - 1))
             quantize_and_multiply(pass1, 2 if e == 6 else 1)
+            if e == LAST - 1:
+                load_and_round_w2(e)
             scatter_closed(e - 1)
 
         last0, last1 = PASSES * LAST, PASSES * LAST + 1

@@ -41,13 +41,14 @@ STREAM_GROUPS = {0: ((0, 2), (2, 4), (4, 6)), 1: ((0, 1), (1, 3), (3, 5)), 2: ((
 LATE_PIECES = ((5, 1), (6, 1), (7, 0), (4, 2), (5, 2), (7, 1), (6, 2), (7, 2))
 
 RAW_DEPTH = 4
-WHOLE = 3
+WHOLE = (0, 1, 2)
 PAIRED = 2
+FIRST_RELU_ON_SCALAR = 5
 ROUNDED_UNITS = 4
 CODE_DEPTH = 4
 W2_RAW_DEPTH = 3
 
-SCALAR_CUT = {0: 64, 1: 64, 3: 64, 5: 128, 9: 48, 11: 40, 13: 56}
+THIRD = 20
 
 
 def tile_moe_two_mlp_relu_kernel(
@@ -85,16 +86,16 @@ def tile_moe_two_mlp_relu_kernel(
             offset = even_first + e % RAW_DEPTH * slot_bytes + 4 * first
             return placed.tile([P, values], F32, name=f"{name}{e}", align_bytes=ALIGN, offset=offset)
 
-        whole = {e: slot("whole_raw", e, 0, UNIT + even_values) for e in range(WHOLE)}
-        even_raw = [whole[e][:, UNIT:] if e < WHOLE else slot("even_raw", e, UNIT, even_values)[:] for e in range(E)]
-        odd_raw = [whole[e][:, 0:UNIT] if e < WHOLE else slot("odd_raw", e, 0, UNIT)[:] for e in range(E)]
+        whole = {e: slot("whole_raw", e, 0, UNIT + even_values) for e in WHOLE}
+        even_raw = [whole[e][:, UNIT:] if e in WHOLE else slot("even_raw", e, UNIT, even_values)[:] for e in range(E)]
+        odd_raw = [whole[e][:, 0:UNIT] if e in WHOLE else slot("odd_raw", e, 0, UNIT)[:] for e in range(E)]
         tail_bf16 = {e: one(f"tail_bf16{e}", [P, (C + P) * PACK], BF16) for e in (5, 6, 7)}
         w1_bf16 = ring("w1_bf16", ROUNDED_UNITS, [P, UNIT], BF16)
         w1_codes = ring("w1_codes", CODE_DEPTH, [P, H], U32)
         w1_scales = ring("w1_scales", CODE_DEPTH, [P, H], U8)
         w2_first = 0
         w2_pair = {
-            e: placed.tile([P, 2 * PACK * N], F32, name=f"w2_pair{e}", align_bytes=ALIGN, offset=e // 2 * 4 * PACK * N)
+            e: placed.tile([P, 2 * PACK * N], F32, name=f"w2_pair{e}", align_bytes=ALIGN, offset=e * 4 * PACK * N)
             for e in range(0, PAIRED, 2)
         }
         w2_raw = [
@@ -292,10 +293,16 @@ def tile_moe_two_mlp_relu_kernel(
         for c in range(1, ROW_TILES):
             nc.scalar.copy(out_sb[c][:].rearrange("p (a s) -> p a s", s=C), repeated)
 
+        def load_first(e):
+            if e in WHOLE:
+                load_expert(e)
+            else:
+                load_unit(PASSES * e)
+
         load_words()
         nc.sync.dma_start(src_list[:], offs)
         load_scales((0, 1))
-        load_w2_pair(0)
+        load_first(0)
         nc.sync.dma_start(gate_row[:], gate[0].rearrange("(n q) -> n q", n=P))
         load_scales((2, 3))
         for o in range(PASSES):
@@ -315,8 +322,17 @@ def tile_moe_two_mlp_relu_kernel(
                     elif end == e + 1:
                         scatter_one(c, first)
 
+        def scalar_share(u):
+            e, turn = divmod(u, PASSES)
+            if e == 0:
+                return P // 2
+            if turn == 0:
+                return 0
+            pairs = [first for groups in STREAM_GROUPS.values() for first, end in groups if end == e - 1 and end - first > 1]
+            return P // 2 ** len(pairs)
+
         def round_shared(u):
-            cut = SCALAR_CUT.get(u, 0)
+            cut = scalar_share(u)
             round_unit(u, True, 0, cut)
             if u % PASSES == 0 and cut < P // 2 and u < 12:
                 round_unit(u, False, P // 2, P)
@@ -329,8 +345,11 @@ def tile_moe_two_mlp_relu_kernel(
             landed = w2_raw[e]
             if e >= PAIRED:
                 nc.sync.dma_start(landed.rearrange("p (j n) -> p j n", j=PACK)[:, :, 0 : tiles * P], w2_rows(e, 0, tiles))
-            elif e % 2 == 0 and e > 0:
-                load_w2_pair(e)
+            elif e % 2 == 0:
+                return
+            else:
+                load_w2_pair(e - 1)
+                round_w2(True, w2h_values(e - 1, C, C + tiles * P), w2_raw[e - 1], tiles)
             round_w2(True, w2h_values(e, C, C + tiles * P), landed, tiles)
 
         def second(e):
@@ -339,19 +358,17 @@ def tile_moe_two_mlp_relu_kernel(
 
         for e in range(E):
             pass0, pass1 = PASSES * e, PASSES * e + 1
-            if e < LAST - 1:
-                load_and_round_w2(e)
-            if e < WHOLE:
-                load_expert(e)
-            else:
-                load_unit(pass0)
-            if WHOLE <= e < LAST:
+            if e > 0:
+                load_first(e)
+            if e not in WHOLE and e < LAST:
                 load_unit(pass1)
-            if e == 0:
+            if e == 1:
                 nc.sync.dma_start(dst_list[:], dst)
+            if e < PAIRED:
+                load_and_round_w2(e)
             round_shared(pass0)
             if e > 0:
-                relu_h(e - 1, e > 5)
+                relu_h(e - 1, e - 1 >= FIRST_RELU_ON_SCALAR)
             if e == LAST:
                 break
             quantize_and_multiply(pass0, 1)
@@ -361,7 +378,7 @@ def tile_moe_two_mlp_relu_kernel(
             if e > 0:
                 times_gate(e - 1, stream_tiles(e - 1))
             quantize_and_multiply(pass1, 2 if e == 6 else 1)
-            if e == LAST - 1:
+            if e >= PAIRED:
                 load_and_round_w2(e)
             scatter_closed(e - 1)
 
@@ -370,12 +387,12 @@ def tile_moe_two_mlp_relu_kernel(
             load_unit(last1, half * H // 2, (half + 1) * H // 2)
         for e, c in LATE_PIECES:
             nc.sync.dma_start(late_raw[e, c][:].rearrange("p (j n) -> p j n", j=PACK), w2_rows(e, c, c + 1))
-        round_unit(last1, True, 0, 40)
-        round_unit(last1, False, 40, P // 2)
+        round_unit(last1, True, 0, P // 2 - THIRD)
+        round_unit(last1, False, P // 2 - THIRD, P // 2)
         quantize_and_multiply(last0, 1)
         second(6)
-        round_unit(last1, False, P // 2, 108)
-        round_unit(last1, True, 108, P)
+        round_unit(last1, False, P // 2, P - THIRD)
+        round_unit(last1, True, P - THIRD, P)
         quantize_and_multiply(last1, 2)
         round_late(True, 5, 1)
         round_late(True, 6, 1)

from contextlib import ExitStack

import concourse.mybir as mybir
from concourse.masks import make_identity

K, T, E, C, H, N = 1024, 2048, 8, 128, 512, 384
S = E * C
FLOPS = 2 * S * (K * H + H * N)
BYTES = K * T + K // 32 * T + 4 * (E * H * (K + N) + S + N * T) + 2 * 2 * 8 * S

F32 = mybir.dt.float32
BF16 = mybir.dt.bfloat16
I32 = mybir.dt.int32
U32 = mybir.dt.uint32
U16 = mybir.dt.uint16
U8 = mybir.dt.uint8
FP8X4 = mybir.dt.float8_e4m3fn_x4
COPY = mybir.ActivationFunctionType.Copy
RELU = mybir.ActivationFunctionType.Relu
MULT = mybir.AluOpType.mult
ADD = mybir.AluOpType.add
MAX = mybir.AluOpType.max

P = 128
PACK = 4
K_PASS = P * PACK
PASSES = K // K_PASS
ROW_TILES = N // P
LIST_ROWS = 16
QUADRANT = 32
SCALE_ROWS = 4
RUN = 4
ALIGN = 256

UNIT = PACK * H
PIECE = PACK * P
LAST = E - 1

FIRST_LATE = (7, 5, 4)
STREAM_GROUPS = {0: ((0, 2), (2, 4), (4, 6)), 1: ((0, 1), (1, 3), (3, 5)), 2: ((0, 2), (2, 4))}
LATE_PIECES = ((5, 1), (6, 1), (7, 0), (4, 2), (5, 2), (7, 1), (6, 2), (7, 2))

RAW_DEPTH = 4
WHOLE = (0, 1, 2)
PAIRED = 2
FIRST_RELU_ON_SCALAR = 5
ROUNDED_UNITS = 4
CODE_DEPTH = 4
W2_RAW_DEPTH = 3

THIRD = 20


def tile_moe_two_mlp_relu_kernel(
    tc, x_words, x_scales, w1, w2, gate, offs, dst, out
):
    nc = tc.nc
    with ExitStack() as ctx:
        keep = ctx.enter_context(tc.tile_pool(name="keep", bufs=1))
        placed = ctx.enter_context(tc.tile_pool(name="placed", bufs=1))
        psum = ctx.enter_context(tc.psum_pool(name="psum", bufs=1))

        def one(name, shape, dtype):
            return keep.tile(shape, dtype, name=name, align_bytes=ALIGN)

        def ring(name, count, shape, dtype):
            return [one(f"{name}{i}", shape, dtype) for i in range(count)]

        src_list = one("src_list", [P, S // LIST_ROWS], U16)
        dst_list = one("dst_list", [P, S // LIST_ROWS], U16)
        tok_words = one("tok_words", [P, PASSES * T], I32)
        tok_scales = one("tok_scales", [P, T], U8)
        slot_words = ring("slot_words", PASSES, [P, S], U32)
        slot_scales = one("slot_scales", [P, S], U8)
        gate_row = one("gate_row", [P, S // P], F32)
        identity = one("identity", [P, P], F32)
        gate_sb = one("gate_sb", [P, S], F32)
        zeros = one("zeros", [P, C], F32)
        out_sb = ring("out_sb", ROW_TILES, [P, T], F32)
        y_sb = one("y_sb", [P, ROW_TILES * S], F32)
        even_values = UNIT + PACK * N // 2
        slot_bytes = 4 * (even_values + UNIT)
        even_first = W2_RAW_DEPTH * 4 * PACK * N

        def slot(name, e, first, values):
            offset = even_first + e % RAW_DEPTH * slot_bytes + 4 * first
            return placed.tile([P, values], F32, name=f"{name}{e}", align_bytes=ALIGN, offset=offset)

        whole = {e: slot("whole_raw", e, 0, UNIT + even_values) for e in WHOLE}
        even_raw = [whole[e][:, UNIT:] if e in WHOLE else slot("even_raw", e, UNIT, even_values)[:] for e in range(E)]
        odd_raw = [whole[e][:, 0:UNIT] if e in WHOLE else slot("odd_raw", e, 0, UNIT)[:] for e in range(E)]
        tail_bf16 = {e: one(f"tail_bf16{e}", [P, (C + P) * PACK], BF16) for e in (5, 6, 7)}
        w1_bf16 = ring("w1_bf16", ROUNDED_UNITS, [P, UNIT], BF16)
        w1_codes = ring("w1_codes", CODE_DEPTH, [P, H], U32)
        w1_scales = ring("w1_scales", CODE_DEPTH, [P, H], U8)
        w2_first = 0
        w2_pair = {
            e: placed.tile([P, 2 * PACK * N], F32, name=f"w2_pair{e}", align_bytes=ALIGN, offset=e * 4 * PACK * N)
            for e in range(0, PAIRED, 2)
        }
        w2_raw = [
            w2_pair[e - e % 2][:, e % 2 * PACK * N : (e % 2 + 1) * PACK * N]
            if e < PAIRED
            else placed.tile([P, PACK * N], F32, name=f"w2_raw{e}", align_bytes=ALIGN, offset=w2_first + e % W2_RAW_DEPTH * 4 * PACK * N)[:]
            for e in range(LAST)
        ]
        w2h_codes = ring("w2h_codes", E, [P, C + N], U32)
        w2h_scales = [
            placed.tile([P, C + N], U8, name=f"w2h_scales{e}", align_bytes=ALIGN, offset=even_first + (e + 1) % RAW_DEPTH * slot_bytes + 4 * UNIT)
            if e in (5, 6)
            else one(f"w2h_scales{e}", [P, C + N], U8)
            for e in range(E)
        ]
        late_raw = {
            (e, c): placed.tile([P, PIECE], F32, name=f"late_raw{e}{c}", align_bytes=ALIGN, offset=w2_first + (place + 3) % 9 * 4 * PIECE)
            for place, (e, c) in enumerate(LATE_PIECES)
        }
        late_bf16 = {c: one(f"late_bf16{c}", [P, (E - FIRST_LATE[c]) * PIECE], BF16) for c in (1, 2)}
        late_codes = {c: one(f"late_codes{c}", [P, (E - FIRST_LATE[c]) * P], U32) for c in (1, 2)}
        late_scales = {c: one(f"late_scales{c}", [P, (E - FIRST_LATE[c]) * P], U8) for c in (1, 2)}
        acc1 = [psum.tile([P, PACK, C], F32, name=f"acc1_{i}") for i in range(2)]
        acc2 = [psum.tile([P, ROW_TILES, C], F32, name=f"acc2_{i}") for i in range(2)]
        acc_late = [psum.tile([P, PACK * C], F32, name=f"acc_late{i}") for i in range(4)]

        def load_words():
            nc.sync.dma_start(
                tok_words[:].rearrange("p (o t) -> p o t", o=PASSES),
                x_words.rearrange("o p t r -> p o (t r)").bitcast(I32),
            )

        def load_scales(rows):
            for r in rows:
                for o in range(PASSES):
                    nc.sync.dma_start(
                        tok_scales[SCALE_ROWS * o + r : P : QUADRANT, :].bitcast(I32),
                        x_scales[o, r::SCALE_ROWS, :].bitcast(I32),
                    )

        def spread_gate():
            by_slot = gate_sb[:].rearrange("p (n q) -> p n q", n=P)
            for half in range(2):
                bank = acc1[half]
                for q in range(PACK):
                    column = half * PACK + q
                    nc.tensor.transpose(bank[:, q, :], gate_row[:, column : column + 1].to_broadcast([P, P]), identity[:])
                nc.scalar.copy(by_slot[:, :, half * PACK : (half + 1) * PACK], bank[:].rearrange("p q n -> p n q"))

        def w1_rows(u):
            o = PASSES - 1 - u % PASSES
            rows = w1[u // PASSES, o * K_PASS : (o + 1) * K_PASS, :]
            return rows.rearrange("(p j) i -> p j i", j=PACK)

        def raw(u):
            return (odd_raw[u // PASSES] if u % PASSES else even_raw[u // PASSES])[:, 0:UNIT]

        def load_unit(u, first=0, end=H):
            target = raw(u).rearrange("p (j i) -> p j i", j=PACK)
            nc.sync.dma_start(target[:, :, first:end], w1_rows(u)[:, :, first:end])

        def load_expert(e):
            nc.sync.dma_start(
                whole[e][:, 0 : PASSES * UNIT].rearrange("p (o x) -> p o x", o=PASSES),
                w1[e].rearrange("(o p j) i -> p o (j i)", o=PASSES, j=PACK),
            )

        def load_w2_pair(e):
            nc.sync.dma_start(
                w2_pair[e][:].rearrange("p (a x) -> p a x", a=2),
                w2[e : e + 2].rearrange("a (p j) n -> p a (j n)", j=PACK),
            )

        def round_copy(on_scalar, target, source):
            if on_scalar:
                nc.scalar.activation(target, source, COPY)
            else:
                nc.vector.tensor_copy(target, source)

        def round_unit(u, on_scalar, first, end):
            target = w1_bf16[u % ROUNDED_UNITS][:].rearrange("p (t m j) -> p m j t", j=PACK, t=PACK)
            source = raw(u).rearrange("p (j m t) -> p m j t", j=PACK, t=PACK)
            if end > first:
                round_copy(on_scalar, target[:, first:end], source[:, first:end])

        def quantize(codes, scales, values):
            nc.vector.quantize_mx(out=codes.bitcast(FP8X4), scales=scales, in_=values)

        def quantize_and_multiply(u, parts):
            codes, scales = w1_codes[u % CODE_DEPTH], w1_scales[u % CODE_DEPTH]
            width = H // parts
            for a in range(parts):
                cols = slice(a * width, (a + 1) * width)
                quantize(codes[:, cols], scales[:, cols], w1_bf16[u % ROUNDED_UNITS][:, a * width * PACK : (a + 1) * width * PACK])
            e, turn = divmod(u, PASSES)
            o = PASSES - 1 - turn
            slots = slice(e * C, (e + 1) * C)
            for t in range(PACK):
                cols = slice(t * P, (t + 1) * P)
                nc.tensor.matmul_mx(
                    out=acc1[e % 2][:, t, :],
                    lhsT=codes[:, cols].bitcast(FP8X4),
                    lhsT_scale=scales[:, cols],
                    rhs=slot_words[o][:, slots].bitcast(FP8X4),
                    rhs_scale=slot_scales[SCALE_ROWS * o : P, slots],
                    start=(turn == 0 and t == 0),
                    stop=(turn == PASSES - 1 and t == PACK - 1),
                )

        def w2h_values(e, first, end):
            if e in tail_bf16:
                return tail_bf16[e][:, first * PACK : end * PACK]
            start = UNIT - C * PACK // 2
            return even_raw[e + 1][:, start + first * PACK // 2 : start + end * PACK // 2].bitcast(BF16)

        def relu_h(e, on_scalar):
            h = w2h_values(e, 0, C).rearrange("p (s t) -> p s t", t=PACK)
            sums = acc1[e % 2][:].rearrange("p t s -> p s t")
            if on_scalar:
                nc.scalar.activation(h, sums, RELU)
            else:
                nc.vector.tensor_scalar(h, sums, 0.0, None, MAX)

        def w2_rows(e, first, end):
            return w2[e].rearrange("(p j) n -> p j n", j=PACK)[:, :, first * P : end * P]

        def round_w2(on_scalar, values, landed, tiles):
            target = values.rearrange("p (g n j) -> p g j n", n=RUN, j=PACK)
            source = landed.rearrange("p (j g n) -> p g j n", j=PACK, n=RUN)
            round_copy(on_scalar, target, source[:, 0 : tiles * P // RUN])

        def quantize_w2h(e, tiles):
            end = C + tiles * P
            quantize(w2h_codes[e][:, 0:end], w2h_scales[e][:, 0:end], w2h_values(e, 0, end))

        def second_matmul(sums, e, codes, scales):
            nc.tensor.matmul_mx(
                out=sums,
                lhsT=codes.bitcast(FP8X4),
                lhsT_scale=scales,
                rhs=w2h_codes[e][:, 0:C].bitcast(FP8X4),
                rhs_scale=w2h_scales[e][:, 0:C],
                start=True,
                stop=True,
            )

        def y_rows(c, first, end):
            return y_sb[:, c * S + first * C : c * S + end * C]

        def second_layer(e, tiles):
            for c in range(tiles):
                cols = slice(C + c * P, C + (c + 1) * P)
                second_matmul(acc2[e % 2][:, c, :], e, w2h_codes[e][:, cols], w2h_scales[e][:, cols])

        def times_gate(e, tiles):
            y = y_sb[:].rearrange("p (c s) -> p c s", c=ROW_TILES)[:, 0:tiles, e * C : (e + 1) * C]
            gates = gate_sb[:, e * C : (e + 1) * C].rearrange("p (c s) -> p c s", c=1).to_broadcast([P, tiles, C])
            nc.vector.tensor_tensor(y, acc2[e % 2][:, 0:tiles, :], gates, MULT)

        def places(c, first, end):
            return out_sb[c][:].indirect(dst_list[:, first * C // LIST_ROWS : end * C // LIST_ROWS])

        def scatter_group(c, first, end):
            nc.scalar.activation(places(c, first, end), y_rows(c, first, end), COPY)

        def scatter_one(c, e, y=None):
            nc.vector.tensor_tensor(places(c, e, e + 1), y_rows(c, e, e + 1) if y is None else y, zeros[:], ADD)

        def staged_gate(e, y):
            nc.vector.tensor_tensor(y, acc2[e % 2][:, 0, :], gate_sb[:, e * C : (e + 1) * C], MULT)

        def round_late(on_scalar, e, c):
            place = e - FIRST_LATE[c]
            round_w2(on_scalar, late_bf16[c][:, place * PIECE : (place + 1) * PIECE], late_raw[e, c][:], 1)

        def late_sums(c, first, end, bank):
            a, b = first - FIRST_LATE[c], end - FIRST_LATE[c]
            quantize(late_codes[c][:, a * P : b * P], late_scales[c][:, a * P : b * P], late_bf16[c][:, a * PIECE : b * PIECE])
            for e in range(first, end):
                cols = slice((e - FIRST_LATE[c]) * P, (e - FIRST_LATE[c] + 1) * P)
                second_matmul(acc_late[bank][:, (e - first) * C : (e - first + 1) * C], e, late_codes[c][:, cols], late_scales[c][:, cols])

        def late_gate(c, first, end, bank):
            nc.vector.tensor_tensor(
                y_rows(c, first, end), acc_late[bank][:, 0 : (end - first) * C], gate_sb[:, first * C : end * C], MULT
            )

        def store(c):
            nc.sync.dma_start(out[c * P : (c + 1) * P, :], out_sb[c][:])

        nc.vector.memset(tok_scales[:].bitcast(I32), 0)
        nc.vector.memset(zeros[:], 0.0)
        nc.vector.memset(out_sb[0][:], 0.0)
        repeated = zeros[:].rearrange("p (a s) -> p a s", a=1).to_broadcast([P, T // C, C])
        for c in range(1, ROW_TILES):
            nc.scalar.copy(out_sb[c][:].rearrange("p (a s) -> p a s", s=C), repeated)

        def load_first(e):
            if e in WHOLE:
                load_expert(e)
            else:
                load_unit(PASSES * e)

        load_words()
        nc.sync.dma_start(src_list[:], offs)
        load_scales((0, 1))
        load_first(0)
        nc.sync.dma_start(gate_row[:], gate[0].rearrange("(n q) -> n q", n=P))
        load_scales((2, 3))
        for o in range(PASSES):
            nc.vector.tensor_copy(slot_words[o][:], tok_words[:, o * T : (o + 1) * T].bitcast(U32).indirect(src_list[:]))
        nc.vector.tensor_copy(slot_scales[:], tok_scales[:].indirect(src_list[:]))
        make_identity(nc, identity[:])
        spread_gate()

        def stream_tiles(e):
            return len([c for c in range(ROW_TILES) if e < FIRST_LATE[c]])

        def scatter_closed(e):
            for c, groups in STREAM_GROUPS.items():
                for first, end in groups:
                    if end == e + 1 and end - first > 1:
                        scatter_group(c, first, end)
                    elif end == e + 1:
                        scatter_one(c, first)

        def scalar_share(u):
            e, turn = divmod(u, PASSES)
            if e == 0:
                return P // 2
            if turn == 0:
                return 0
            pairs = [first for groups in STREAM_GROUPS.values() for first, end in groups if end == e - 1 and end - first > 1]
            return P // 2 ** len(pairs)

        def round_shared(u):
            cut = scalar_share(u)
            round_unit(u, True, 0, cut)
            if u % PASSES == 0 and cut < P // 2 and u < 12:
                round_unit(u, False, P // 2, P)
                round_unit(u, False, cut, P // 2)
            else:
                round_unit(u, False, cut, P)

        def load_and_round_w2(e):
            tiles = stream_tiles(e)
            landed = w2_raw[e]
            if e >= PAIRED:
                nc.sync.dma_start(landed.rearrange("p (j n) -> p j n", j=PACK)[:, :, 0 : tiles * P], w2_rows(e, 0, tiles))
            elif e % 2 == 0:
                return
            else:
                load_w2_pair(e - 1)
                round_w2(True, w2h_values(e - 1, C, C + tiles * P), w2_raw[e - 1], tiles)
            round_w2(True, w2h_values(e, C, C + tiles * P), landed, tiles)

        def second(e):
            quantize_w2h(e, stream_tiles(e))
            second_layer(e, stream_tiles(e))

        for e in range(E):
            pass0, pass1 = PASSES * e, PASSES * e + 1
            if e > 0:
                load_first(e)
            if e not in WHOLE and e < LAST:
                load_unit(pass1)
            if e == 1:
                nc.sync.dma_start(dst_list[:], dst)
            if e < PAIRED:
                load_and_round_w2(e)
            round_shared(pass0)
            if e > 0:
                relu_h(e - 1, e - 1 >= FIRST_RELU_ON_SCALAR)
            if e == LAST:
                break
            quantize_and_multiply(pass0, 1)
            if e > 0:
                second(e - 1)
            round_shared(pass1)
            if e > 0:
                times_gate(e - 1, stream_tiles(e - 1))
            quantize_and_multiply(pass1, 2 if e == 6 else 1)
            if e >= PAIRED:
                load_and_round_w2(e)
            scatter_closed(e - 1)

        last0, last1 = PASSES * LAST, PASSES * LAST + 1
        for half in range(2):
            load_unit(last1, half * H // 2, (half + 1) * H // 2)
        for e, c in LATE_PIECES:
            nc.sync.dma_start(late_raw[e, c][:].rearrange("p (j n) -> p j n", j=PACK), w2_rows(e, c, c + 1))
        round_unit(last1, True, 0, P // 2 - THIRD)
        round_unit(last1, False, P // 2 - THIRD, P // 2)
        quantize_and_multiply(last0, 1)
        second(6)
        round_unit(last1, False, P // 2, P - THIRD)
        round_unit(last1, True, P - THIRD, P)
        quantize_and_multiply(last1, 2)
        round_late(True, 5, 1)
        round_late(True, 6, 1)
        round_w2(False, w2h_values(LAST, C, C + P), late_raw[LAST, 0][:], 1)
        relu_h(LAST, True)
        y_six = late_raw[6, 1][:, 0:C]
        staged_gate(6, y_six)
        late_sums(1, 5, 7, 0)
        scatter_one(0, 6, y_six)
        quantize_w2h(LAST, 1)
        second_layer(LAST, 1)
        round_late(True, 4, 2)
        round_late(True, 5, 2)
        late_gate(1, 5, 7, 0)
        scatter_group(1, 5, 7)
        round_late(False, 7, 1)
        y_last = late_raw[5, 2][:, 0:C]
        staged_gate(LAST, y_last)
        late_sums(2, 4, 6, 1)
        scatter_one(0, LAST, y_last)
        store(0)
        late_sums(1, 7, 8, 2)
        late_gate(2, 4, 6, 1)
        round_late(True, 6, 2)
        scatter_group(2, 4, 6)
        round_late(False, 7, 2)
        late_gate(1, 7, 8, 2)
        late_sums(2, 6, 8, 3)
        scatter_one(1, LAST)
        store(1)
        late_gate(2, 6, 8, 3)
        scatter_group(2, 6, 8)
        store(2)
